import numpy as np
import ml_dtypes


def mxq(x, axis, fmt="e4m3"):
    dtype, down = {"e4m3": (ml_dtypes.float8_e4m3fn, 7), "e5m2": (ml_dtypes.float8_e5m2, 14)}[fmt]
    v = np.moveaxis(np.asarray(x, np.float32).astype(ml_dtypes.bfloat16).astype(np.float64), axis, -1)
    blocks = v.reshape(v.shape[:-1] + (-1, 32))
    amax = np.abs(blocks).max(-1, keepdims=True)
    byte = np.maximum(np.where(amax > 0, np.frexp(amax)[1] - 1 + 127, 0) - down, 1)
    scale = np.exp2(byte - 127.0)
    codes = (blocks / scale).astype(np.float32).astype(dtype).astype(np.float64)
    return np.moveaxis((codes * scale).reshape(v.shape), -1, axis)


WIDE = False


def mx_kscale(k):
    if not WIDE:
        return np.ones(k)
    levels = np.array([10, -10, 5, -5, 0])
    if k % 512:
        return np.exp2(np.random.permutation(np.resize(levels, k // 32))).repeat(32)
    a = np.empty((k // 512, 16))
    for p in range(k // 512):
        a[p, :8] = np.random.permutation(np.resize(levels, 8))
        for g in range(8):
            far = levels[np.abs(levels - a[p, g]) >= 10]
            a[p, g + 8] = far[np.random.randint(len(far))]
    return np.exp2(a.ravel()).repeat(32)


def f64(x):
    return np.asarray(x).astype(np.float64)


def striped(idx):
    return np.tile(idx.reshape(-1, 16).T, (8, 1)).astype(np.uint16)


def unstriped(offs):
    return offs[:16].T.reshape(-1).astype(np.int64)


E2M1 = np.array([0.0, 0.5, 1.0, 1.5, 2.0, 3.0, 4.0, 6.0, -0.0, -0.5, -1.0, -1.5, -2.0, -3.0, -4.0, -6.0])


def pack_weight(w, fmt):
    k, n = w.shape
    w = f64(np.asarray(w, np.float32).astype(ml_dtypes.bfloat16)).reshape(k // 32, 32, n)
    amax = np.abs(w).max(1)
    if fmt == "e4m3":
        byte = np.frexp(amax)[1] - 1 + 127 - 7
    else:
        mant, ex = np.frexp(amax / 6.0)
        byte = np.where(mant > 0.5, ex, ex - 1) + 127
    byte = np.clip(np.where(amax > 0, byte, 1), 1, 254)
    scaled = (w * np.exp2(127.0 - byte)[:, None, :]).reshape(k, n).astype(np.float32)
    by_word = np.ascontiguousarray(scaled.reshape(k // 512, 128, 4, n).transpose(0, 1, 3, 2))
    if fmt == "e4m3":
        words = by_word.astype(ml_dtypes.float8_e4m3fn).view(np.uint8)
    else:
        c = by_word.astype(ml_dtypes.float4_e2m1fn).view(np.uint8) & 0xF
        words = (c[..., 0::2] | (c[..., 1::2] << 4)).reshape(k // 512, 128, 2 * n)
    return np.ascontiguousarray(words), np.ascontiguousarray(byte.astype(np.uint8).reshape(k // 512, 16, n))


def unpack_weight(words, scales, fmt):
    g, _, n = scales.shape
    words = np.ascontiguousarray(words).reshape(g, 128, n, -1)
    if fmt == "e4m3":
        vals = words.view(ml_dtypes.float8_e4m3fn).astype(np.float64)
    else:
        nib = np.empty((g, 128, n, 4), np.uint8)
        nib[..., 0::2] = words & 0xF
        nib[..., 1::2] = words >> 4
        vals = E2M1[nib]
    vals = vals * np.repeat(np.exp2(scales.astype(np.float64) - 127.0), 8, axis=1)[..., None]
    return vals.transpose(0, 1, 3, 2).reshape(g * 512, n)


def gelu(v):
    return 0.5 * v * (1.0 + np.tanh(np.sqrt(2.0 / np.pi) * (v + 0.044715 * v**3)))


T, T2, S, K, K2, H, N = 2048, 2048, 1024, 1024, 512, 1024, 512

def setup_inputs():
    n = np.random.standard_normal
    s, s2, u = mx_kscale(K)[:, None], mx_kscale(K2)[:, None], mx_kscale(H)[:, None]
    tab_words, tab_scales = pack_weight(n((K, T)) * s, "e4m3")
    tab2_words, tab2_scales = pack_weight(n((K2, T2)) * s2, "e4m3")
    wb_words, wb_scales = pack_weight(n((K2, H)) / np.sqrt(K2) / s2 * u.T, "e2m1")
    return {
        "tab_words": tab_words, "tab_scales": tab_scales,
        "tab2_words": tab2_words, "tab2_scales": tab2_scales,
        "offs": striped(np.random.permutation(T)[:S]),
        "offs2": striped(np.random.permutation(T2)[:S]),
        "wa": (n((K, H)) / np.sqrt(K) / s * u.T).astype(np.float32),
        "wb_words": wb_words, "wb_scales": wb_scales,
        "b": (0.5 * n(H) * u[:, 0]).astype(np.float32),
        "w2": (1.5 * n((H, N)) / np.sqrt(H) / u).astype(np.float32),
        "c": (0.5 * n(N)).astype(np.float32),
        "gT": n((N, T)).astype(np.float32),
    }

def reference(tab_words, tab_scales, tab2_words, tab2_scales, offs, offs2, wa, wb_words, wb_scales, b, w2, c, gT):
    v = unpack_weight(tab_words, tab_scales, "e4m3")[:, unstriped(offs)]
    v2 = unpack_weight(tab2_words, tab2_scales, "e4m3")[:, unstriped(offs2)]
    wb = unpack_weight(wb_words, wb_scales, "e2m1")
    wa_q = mxq(f64(wa), 0, "e4m3")
    a = wa_q.T @ v + wb.T @ v2
    h = np.maximum(a + f64(b)[:, None], 0.0)
    w2_q = mxq(f64(w2), 0, "e4m3")
    h_q = mxq(h, 0, "e4m3")
    z = (w2_q.T @ h_q) + f64(c)[:, None]
    g = f64(gT)[:, unstriped(offs)]
    return g / (1.0 + np.exp(-z))

@@ -1,0 +1,265 @@
+from contextlib import ExitStack
+
+import concourse.mybir as mybir
+
+F32 = mybir.dt.float32
+BF16 = mybir.dt.bfloat16
+I32 = mybir.dt.int32
+U32 = mybir.dt.uint32
+U16 = mybir.dt.uint16
+U8 = mybir.dt.uint8
+FP8X4 = mybir.dt.float8_e4m3fn_x4
+FP4X4 = mybir.dt.float4_e2m1fn_x4
+ACT = mybir.ActivationFunctionType
+MULT = mybir.AluOpType.mult
+
+T, S, K, K2, H, N = 2048, 1024, 1024, 512, 1024, 512
+P = 128
+HALF = 512
+FLOPS = 2 * S * (K * H + K2 * H + H * N)
+
+
+def tile_list_edge_gated_messages_kernel(
+    tc, tab_words, tab_scales, tab2_words, tab2_scales, offs, offs2, wa, wb_words, wb_scales, b, w2, c, gT, out
+):
+    nc = tc.nc
+    with ExitStack() as ctx:
+        keep = ctx.enter_context(tc.tile_pool(name="keep", bufs=1))
+        big = ctx.enter_context(tc.tile_pool(name="big", bufs=6))
+        stage = ctx.enter_context(tc.tile_pool(name="stage", bufs=3))
+        psum = ctx.enter_context(tc.psum_pool(name="psum", bufs=8))
+
+        list1 = keep.tile([P, S // 16], U16, name="list1")
+        list2 = keep.tile([P, S // 16], U16, name="list2")
+        tab_sc = keep.tile([P, T // 4], I32, name="tab_sc")
+        tab2_sc = keep.tile([P, T // 4], I32, name="tab2_sc")
+        wb_sc_raw = keep.tile([P, H // 4], I32, name="wb_sc_raw")
+        wb_raw = keep.tile([P, H // 2], I32, name="wb_raw")
+        b_sb = keep.tile([P, 2, 4], F32, name="b_sb")
+        c_sb = keep.tile([P, 4], F32, name="c_sb")
+        warm_in = keep.tile([P, 1], F32, name="warm_in")
+        warm_out = keep.tile([P, 1], F32, name="warm_out")
+
+        nc.vector.memset(tab_sc[:], 0)
+        nc.vector.memset(warm_in[:], 0.0)
+        nc.gpsimd.memset(tab2_sc[:], 0)
+        nc.gpsimd.memset(wb_sc_raw[:], 0)
+
+        def load_table(words, name):
+            tile = big.tile([P, T], I32, tag="big", name=name)
+            nc.sync.dma_start(out=tile[:], in_=words.rearrange("p t i -> p (t i)").bitcast(I32))
+            return tile
+
+        def load_rows(rows, name):
+            tile = big.tile([P, 4, HALF], F32, tag="big", name=name)
+            nc.sync.dma_start(out=tile[:], in_=rows.rearrange("(p j) x -> p j x", j=4))
+            return tile
+
+        def load_plane(engine, tile, scales):
+            rows = scales.bitcast(I32).rearrange("(q r) x -> r q x", r=4)
+            for r in range(4):
+                engine.dma_start(out=tile[r:P:32, :], in_=rows[r])
+
+        for q in range(4):
+            nc.scalar.dma_start(
+                out=tab_sc[32 * q : 32 * q + 8, :], in_=tab_scales.bitcast(I32)[:, 4 * q : 4 * q + 4, :]
+            )
+        load_plane(nc.scalar, tab2_sc, tab2_scales[0])
+        nc.scalar.activation(out=warm_out[:], in_=warm_in[:], func=ACT.Sigmoid)
+        nc.scalar.dma_start(out=b_sb[:], in_=b.rearrange("(g p t) -> p g t", g=2, t=4))
+        with nc.allow_non_contiguous_dma(reason="one bias value a partition"):
+            nc.scalar.dma_start(out=c_sb[:], in_=c.rearrange("(u p) -> p u", p=P))
+
+        tabs = [None, None, None]
+        wa_raw = {}
+        nc.sync.dma_start(list1[:], offs)
+        tabs[0] = load_table(tab_words[0], "tab0")
+        wa_raw[0, 0] = load_rows(wa[0:512, 0:512], "wa00")
+        nc.sync.dma_start(list2[:], offs2)
+        tabs[1] = load_table(tab_words[1], "tab1")
+        nc.sync.dma_start(out=wb_raw[:], in_=wb_words[0].bitcast(I32))
+        load_plane(nc.sync, wb_sc_raw, wb_scales[0])
+        wa_raw[1, 0] = load_rows(wa[512:1024, 0:512], "wa10")
+        tabs[2] = load_table(tab2_words[0], "tab2")
+
+        picked = [keep.tile([P, S], U32, name=f"picked{a}", align_bytes=64) for a in range(3)]
+        picked_sc = keep.tile([P, S], U8, name="picked_sc", align_bytes=64)
+        picked2_sc = keep.tile([P, S], U8, name="picked2_sc", align_bytes=64)
+        lists = [list1, list1, list2]
+
+        def cols(jh):
+            return slice(jh * HALF, (jh + 1) * HALF)
+
+        def lcols(jh):
+            return slice(jh * HALF // 16, (jh + 1) * HALF // 16)
+
+        def gather_words(a, jh):
+            nc.vector.tensor_copy(
+                out=picked[a][:, cols(jh)], in_=tabs[a][:].bitcast(U32).indirect(lists[a][:, lcols(jh)])
+            )
+
+        def gather_scales(dst, src, lst, jh):
+            nc.vector.tensor_copy(out=dst[:, cols(jh)], in_=src[:].bitcast(U8).indirect(lst[:, lcols(jh)]))
+
+        wb_codes = keep.tile([P, H], U16, name="wb_codes", align_bytes=64)
+        wb_sc = keep.tile([P, H], U8, name="wb_sc", align_bytes=64)
+
+        def permute_wb():
+            nc.vector.tensor_copy(
+                out=wb_codes[:].rearrange("p (g t m) -> p g m t", g=2, t=4),
+                in_=wb_raw[:].bitcast(U16).rearrange("p (g m t) -> p g m t", g=2, t=4),
+            )
+            nc.vector.tensor_copy(
+                out=wb_sc[:].rearrange("p (g t m) -> p g m t", g=2, t=4),
+                in_=wb_sc_raw[:].bitcast(U8).rearrange("p (g m t) -> p g m t", g=2, t=4),
+            )
+
+        def copy_on(engine, out, in_):
+            if engine is nc.scalar:
+                nc.scalar.copy(out=out, in_=in_)
+            else:
+                nc.vector.tensor_copy(out=out, in_=in_)
+
+        def cast_wa(raw, engine, name):
+            grouped = stage.tile([P, 4 * HALF], BF16, tag="grouped", name=name, align_bytes=64)
+            copy_on(
+                engine,
+                grouped[:].rearrange("p (t m j) -> p m j t", t=4, j=4),
+                raw[:].rearrange("p j (m t) -> p m j t", t=4),
+            )
+            return grouped
+
+        def interleave(raw, engine, name):
+            grouped = stage.tile([P, 4 * HALF], BF16, tag="grouped", name=name, align_bytes=64)
+            copy_on(
+                engine,
+                grouped[:].rearrange("p (x i j) -> p x j i", i=4, j=4),
+                raw[:].rearrange("p j (x i) -> p x j i", i=4),
+            )
+            return grouped
+
+        def quantize(grouped, name):
+            codes = keep.tile([P, HALF], U32, name=name + "_codes", align_bytes=64)
+            scales = keep.tile([P, HALF], U8, name=name + "_sc", align_bytes=64)
+            nc.vector.quantize_mx(out=codes[:].bitcast(FP8X4), scales=scales[:], in_=grouped[:])
+            return codes, scales
+
+        wa_q = {}
+        w2_q = {}
+        h_q = {}
+        banks = {}
+
+        def pass_wa(a, g, jh, start, stop):
+            codes, scales = wa_q[a, g]
+            for t in range(4):
+                if start:
+                    banks[g, jh, t] = psum.tile([P, HALF], F32, tag="bank", name=f"a{g}{jh}{t}")
+                m = slice(t * P, (t + 1) * P)
+                nc.tensor.matmul_mx(
+                    out=banks[g, jh, t][:],
+                    lhsT=codes[:, m].bitcast(FP8X4),
+                    lhsT_scale=scales[:, m],
+                    rhs=picked[a][:, cols(jh)].bitcast(FP8X4),
+                    rhs_scale=picked_sc[4 * a : P, cols(jh)],
+                    start=start,
+                    stop=stop,
+                )
+
+        def pass_wb(g, jh, start, stop):
+            for t in range(4):
+                if start:
+                    banks[g, jh, t] = psum.tile([P, HALF], F32, tag="bank", name=f"a{g}{jh}{t}")
+                m = slice(g * HALF + t * P, g * HALF + (t + 1) * P)
+                m2 = slice(2 * m.start, 2 * m.stop)
+                nc.tensor.matmul_mx(
+                    out=banks[g, jh, t][:],
+                    lhsT=wb_codes[:].bitcast(U8)[:, m2].bitcast(FP4X4),
+                    lhsT_scale=wb_sc[:, m],
+                    rhs=picked[2][:, cols(jh)].bitcast(FP8X4),
+                    rhs_scale=picked2_sc[:, cols(jh)],
+                    start=start,
+                    stop=stop,
+                )
+
+        def relu(g, jh):
+            hs = stage.tile([P, 4, HALF], BF16, tag="hs", name=f"hs{g}{jh}")
+            for t in range(4):
+                nc.scalar.activation(
+                    out=hs[:, t, :], in_=banks[g, jh, t][:], func=ACT.Relu, bias=b_sb[:, g, t : t + 1]
+                )
+            return hs
+
+        def quantize_h(hs, g, jh):
+            h_q[g, jh] = quantize(interleave(hs, nc.vector, f"hg{g}{jh}"), f"h{g}{jh}")
+
+        states = []
+
+        def gate(jh):
+            for u in range(4):
+                z = psum.tile([P, HALF], F32, tag="bank", name=f"z{jh}{u}")
+                m = slice(u * P, (u + 1) * P)
+                for g in range(2):
+                    nc.tensor.matmul_mx(
+                        out=z[:],
+                        lhsT=w2_q[g][0][:, m].bitcast(FP8X4),
+                        lhsT_scale=w2_q[g][1][:, m],
+                        rhs=h_q[g, jh][0][:].bitcast(FP8X4),
+                        rhs_scale=h_q[g, jh][1][:],
+                        start=(g == 0),
+                        stop=(g == 1),
+                    )
+                sig = stage.tile([P, HALF], F32, tag="sig", name=f"sig{jh}{u}", bufs=8)
+                nc.scalar.activation(out=sig[:], in_=z[:], func=ACT.Sigmoid, bias=c_sb[:, u : u + 1])
+                res = stage.tile([P, HALF], F32, tag="res", name=f"res{jh}{u}", bufs=8)
+                nc.vector.tensor_tensor(res[:], states[u][:].indirect(list1[:, lcols(jh)]), sig[:], MULT)
+                nc.sync.dma_start(out=out[m, cols(jh)], in_=res[:])
+
+        gather_scales(picked_sc, tab_sc, list1, 0)
+        gather_words(0, 0)
+        wa_q[0, 0] = quantize(cast_wa(wa_raw[0, 0], nc.scalar, "g00"), "wa00")
+        pass_wa(0, 0, 0, True, False)
+        gather_words(1, 0)
+        permute_wb()
+        gather_scales(picked2_sc, tab2_sc, list2, 0)
+        wa_q[1, 0] = quantize(cast_wa(wa_raw[1, 0], nc.scalar, "g10"), "wa10")
+        pass_wa(1, 0, 0, False, False)
+        gather_words(2, 0)
+        pass_wb(0, 0, False, True)
+        gather_scales(picked_sc, tab_sc, list1, 1)
+        gather_words(0, 1)
+        pass_wa(0, 0, 1, True, False)
+        gather_words(1, 1)
+        pass_wa(1, 0, 1, False, False)
+        gather_scales(picked2_sc, tab2_sc, list2, 1)
+        gather_words(2, 1)
+        pass_wb(0, 1, False, True)
+
+        wa_raw[0, 1] = load_rows(wa[0:512, 512:1024], "wa01")
+        wa_raw[1, 1] = load_rows(wa[512:1024, 512:1024], "wa11")
+        w2_raw = [load_rows(w2[0:512, :], "w20"), load_rows(w2[512:1024, :], "w21")]
+        for u in range(4):
+            state = big.tile([P, T], F32, tag="big", name=f"state{u}")
+            nc.sync.dma_start(out=state[:], in_=gT[u * P : (u + 1) * P, :])
+            states.append(state)
+
+        hs00 = relu(0, 0)
+        wa_q[0, 1] = quantize(cast_wa(wa_raw[0, 1], nc.vector, "g01"), "wa01")
+        g11 = cast_wa(wa_raw[1, 1], nc.scalar, "g11")
+        wa_q[1, 1] = quantize(g11, "wa11")
+        pass_wb(1, 0, True, False)
+        pass_wa(0, 1, 0, False, False)
+        pass_wa(1, 1, 0, False, True)
+        quantize_h(hs00, 0, 0)
+        hs01 = relu(0, 1)
+        hs10 = relu(1, 0)
+        pass_wb(1, 1, True, False)
+        pass_wa(0, 1, 1, False, False)
+        pass_wa(1, 1, 1, False, True)
+        w2_q[0] = quantize(interleave(w2_raw[0], nc.vector, "gw0"), "w20")
+        w2_q[1] = quantize(interleave(w2_raw[1], nc.vector, "gw1"), "w21")
+        quantize_h(hs10, 1, 0)
+        quantize_h(hs01, 0, 1)
+        hs11 = relu(1, 1)
+        quantize_h(hs11, 1, 1)
+        gate(0)
+        gate(1)

@@ -1,6 +1,7 @@
 from contextlib import ExitStack
 
 import concourse.mybir as mybir
+from concourse.masks import make_identity
 
 F32 = mybir.dt.float32
 BF16 = mybir.dt.bfloat16
@@ -25,7 +26,7 @@ def tile_list_edge_gated_messages_kernel(
     nc = tc.nc
     with ExitStack() as ctx:
         keep = ctx.enter_context(tc.tile_pool(name="keep", bufs=1))
-        big = ctx.enter_context(tc.tile_pool(name="big", bufs=6))
+        big = ctx.enter_context(tc.tile_pool(name="big", bufs=13))
         stage = ctx.enter_context(tc.tile_pool(name="stage", bufs=3))
         psum = ctx.enter_context(tc.psum_pool(name="psum", bufs=8))
 
@@ -35,15 +36,13 @@ def tile_list_edge_gated_messages_kernel(
         tab2_sc = keep.tile([P, T // 4], I32, name="tab2_sc")
         wb_sc_raw = keep.tile([P, H // 4], I32, name="wb_sc_raw")
         wb_raw = keep.tile([P, H // 2], I32, name="wb_raw")
-        b_sb = keep.tile([P, 2, 4], F32, name="b_sb")
-        c_sb = keep.tile([P, 4], F32, name="c_sb")
+        b_sb = keep.tile([P, 4, 2], F32, name="b_sb")
+        c_sb = keep.tile([P, 4, 1], F32, name="c_sb")
+        bias_rows = keep.tile([P, HALF], F32, name="bias_rows")
+        bias_sorted = keep.tile([P, HALF], F32, name="bias_sorted")
+        identity = keep.tile([P, P], F32, name="identity")
         warm_in = keep.tile([P, 1], F32, name="warm_in")
         warm_out = keep.tile([P, 1], F32, name="warm_out")
-
-        nc.vector.memset(tab_sc[:], 0)
-        nc.vector.memset(warm_in[:], 0.0)
-        nc.gpsimd.memset(tab2_sc[:], 0)
-        nc.gpsimd.memset(wb_sc_raw[:], 0)
 
         def load_table(words, name):
             tile = big.tile([P, T], I32, tag="big", name=name)
@@ -60,38 +59,16 @@ def tile_list_edge_gated_messages_kernel(
             for r in range(4):
                 engine.dma_start(out=tile[r:P:32, :], in_=rows[r])
 
-        for q in range(4):
-            nc.scalar.dma_start(
-                out=tab_sc[32 * q : 32 * q + 8, :], in_=tab_scales.bitcast(I32)[:, 4 * q : 4 * q + 4, :]
-            )
-        load_plane(nc.scalar, tab2_sc, tab2_scales[0])
-        nc.scalar.activation(out=warm_out[:], in_=warm_in[:], func=ACT.Sigmoid)
-        nc.scalar.dma_start(out=b_sb[:], in_=b.rearrange("(g p t) -> p g t", g=2, t=4))
-        with nc.allow_non_contiguous_dma(reason="one bias value a partition"):
-            nc.scalar.dma_start(out=c_sb[:], in_=c.rearrange("(u p) -> p u", p=P))
-
-        tabs = [None, None, None]
-        wa_raw = {}
-        nc.sync.dma_start(list1[:], offs)
-        tabs[0] = load_table(tab_words[0], "tab0")
-        wa_raw[0, 0] = load_rows(wa[0:512, 0:512], "wa00")
-        nc.sync.dma_start(list2[:], offs2)
-        tabs[1] = load_table(tab_words[1], "tab1")
-        nc.sync.dma_start(out=wb_raw[:], in_=wb_words[0].bitcast(I32))
-        load_plane(nc.sync, wb_sc_raw, wb_scales[0])
-        wa_raw[1, 0] = load_rows(wa[512:1024, 0:512], "wa10")
-        tabs[2] = load_table(tab2_words[0], "tab2")
-
         picked = [keep.tile([P, S], U32, name=f"picked{a}", align_bytes=64) for a in range(3)]
         picked_sc = keep.tile([P, S], U8, name="picked_sc", align_bytes=64)
         picked2_sc = keep.tile([P, S], U8, name="picked2_sc", align_bytes=64)
         lists = [list1, list1, list2]
 
         def cols(jh):
-            return slice(jh * HALF, (jh + 1) * HALF)
+            return slice(0, S) if jh is None else slice(jh * HALF, (jh + 1) * HALF)
 
         def lcols(jh):
-            return slice(jh * HALF // 16, (jh + 1) * HALF // 16)
+            return slice(cols(jh).start // 16, cols(jh).stop // 16)
 
         def gather_words(a, jh):
             nc.vector.tensor_copy(
@@ -101,17 +78,17 @@ def tile_list_edge_gated_messages_kernel(
         def gather_scales(dst, src, lst, jh):
             nc.vector.tensor_copy(out=dst[:, cols(jh)], in_=src[:].bitcast(U8).indirect(lst[:, lcols(jh)]))
 
-        wb_codes = keep.tile([P, H], U16, name="wb_codes", align_bytes=64)
-        wb_sc = keep.tile([P, H], U8, name="wb_sc", align_bytes=64)
+        wb_codes = keep.tile([P, H // 2], I32, name="wb_codes", align_bytes=64)
+        wb_sc = keep.tile([P, H // 4], I32, name="wb_sc", align_bytes=64)
 
         def permute_wb():
             nc.vector.tensor_copy(
-                out=wb_codes[:].rearrange("p (g t m) -> p g m t", g=2, t=4),
-                in_=wb_raw[:].bitcast(U16).rearrange("p (g m t) -> p g m t", g=2, t=4),
+                out=wb_codes[:].rearrange("p (g t x w) -> p g t x w", g=2, t=4, w=2),
+                in_=wb_raw[:].rearrange("p (g x t w) -> p g t x w", g=2, t=4, w=2),
             )
             nc.vector.tensor_copy(
-                out=wb_sc[:].rearrange("p (g t m) -> p g m t", g=2, t=4),
-                in_=wb_sc_raw[:].bitcast(U8).rearrange("p (g m t) -> p g m t", g=2, t=4),
+                out=wb_sc[:].rearrange("p (g t x) -> p g t x", g=2, t=4),
+                in_=wb_sc_raw[:].rearrange("p (g x t) -> p g t x", g=2, t=4),
             )
 
         def copy_on(engine, out, in_):
@@ -120,22 +97,27 @@ def tile_list_edge_gated_messages_kernel(
             else:
                 nc.vector.tensor_copy(out=out, in_=in_)
 
-        def cast_wa(raw, engine, name):
-            grouped = stage.tile([P, 4 * HALF], BF16, tag="grouped", name=name, align_bytes=64)
-            copy_on(
-                engine,
-                grouped[:].rearrange("p (t m j) -> p m j t", t=4, j=4),
-                raw[:].rearrange("p j (m t) -> p m j t", t=4),
-            )
+        def cast_wa(raw, engines, name):
+            grouped = stage.tile([P, 4 * HALF], BF16, tag="grouped", name=name, bufs=5, align_bytes=64)
+            share = 4 // len(engines)
+            for s, engine in enumerate(engines):
+                ts = slice(share * s, share * (s + 1))
+                copy_on(
+                    engine,
+                    grouped[:].rearrange("p (t x i j) -> p t x j i", t=4, i=4, j=4)[:, ts],
+                    raw[:].rearrange("p j (x t i) -> p t x j i", t=4, i=4)[:, ts],
+                )
             return grouped
 
-        def interleave(raw, engine, name):
-            grouped = stage.tile([P, 4 * HALF], BF16, tag="grouped", name=name, align_bytes=64)
-            copy_on(
-                engine,
-                grouped[:].rearrange("p (x i j) -> p x j i", i=4, j=4),
-                raw[:].rearrange("p j (x i) -> p x j i", i=4),
-            )
+        def interleave(raw, engines, name):
+            grouped = stage.tile([P, 4 * HALF], BF16, tag="grouped", name=name, bufs=5, align_bytes=64)
+            share = HALF // len(engines)
+            for s, engine in enumerate(engines):
+                copy_on(
+                    engine,
+                    grouped[:, 4 * share * s : 4 * share * (s + 1)].rearrange("p (x i j) -> p x j i", i=4, j=4),
+                    raw[:, :, share * s : share * (s + 1)].rearrange("p j (x i) -> p x j i", i=4),
+                )
             return grouped
 
         def quantize(grouped, name):
@@ -174,7 +156,7 @@ def tile_list_edge_gated_messages_kernel(
                 nc.tensor.matmul_mx(
                     out=banks[g, jh, t][:],
                     lhsT=wb_codes[:].bitcast(U8)[:, m2].bitcast(FP4X4),
-                    lhsT_scale=wb_sc[:, m],
+                    lhsT_scale=wb_sc[:].bitcast(U8)[:, m],
                     rhs=picked[2][:, cols(jh)].bitcast(FP8X4),
                     rhs_scale=picked2_sc[:, cols(jh)],
                     start=start,
@@ -182,84 +164,160 @@ def tile_list_edge_gated_messages_kernel(
                 )
 
         def relu(g, jh):
-            hs = stage.tile([P, 4, HALF], BF16, tag="hs", name=f"hs{g}{jh}")
+            hs = stage.tile([P, 4, HALF], BF16, tag="hs", name=f"hs{g}{jh}", bufs=4)
             for t in range(4):
                 nc.scalar.activation(
-                    out=hs[:, t, :], in_=banks[g, jh, t][:], func=ACT.Relu, bias=b_sb[:, g, t : t + 1]
+                    out=hs[:, t, :], in_=banks[g, jh, t][:], func=ACT.Relu, bias=b_sb[:, t, g : g + 1]
                 )
             return hs
 
-        def quantize_h(hs, g, jh):
-            h_q[g, jh] = quantize(interleave(hs, nc.vector, f"hg{g}{jh}"), f"h{g}{jh}")
 
-        states = []
+        tabs = {}
+        raw = {}
+        states = {}
+        grouped = {}
+        hs = {}
+        sigs = {}
 
-        def gate(jh):
-            for u in range(4):
-                z = psum.tile([P, HALF], F32, tag="bank", name=f"z{jh}{u}")
-                m = slice(u * P, (u + 1) * P)
-                for g in range(2):
-                    nc.tensor.matmul_mx(
-                        out=z[:],
-                        lhsT=w2_q[g][0][:, m].bitcast(FP8X4),
-                        lhsT_scale=w2_q[g][1][:, m],
-                        rhs=h_q[g, jh][0][:].bitcast(FP8X4),
-                        rhs_scale=h_q[g, jh][1][:],
-                        start=(g == 0),
-                        stop=(g == 1),
-                    )
-                sig = stage.tile([P, HALF], F32, tag="sig", name=f"sig{jh}{u}", bufs=8)
-                nc.scalar.activation(out=sig[:], in_=z[:], func=ACT.Sigmoid, bias=c_sb[:, u : u + 1])
-                res = stage.tile([P, HALF], F32, tag="res", name=f"res{jh}{u}", bufs=8)
-                nc.vector.tensor_tensor(res[:], states[u][:].indirect(list1[:, lcols(jh)]), sig[:], MULT)
-                nc.sync.dma_start(out=out[m, cols(jh)], in_=res[:])
+        def load_tab_scales(engine):
+            for q in range(4):
+                engine.dma_start(
+                    out=tab_sc[32 * q : 32 * q + 8, :], in_=tab_scales.bitcast(I32)[:, 4 * q : 4 * q + 4, :]
+                )
 
-        gather_scales(picked_sc, tab_sc, list1, 0)
-        gather_words(0, 0)
-        wa_q[0, 0] = quantize(cast_wa(wa_raw[0, 0], nc.scalar, "g00"), "wa00")
-        pass_wa(0, 0, 0, True, False)
-        gather_words(1, 0)
-        permute_wb()
-        gather_scales(picked2_sc, tab2_sc, list2, 0)
-        wa_q[1, 0] = quantize(cast_wa(wa_raw[1, 0], nc.scalar, "g10"), "wa10")
-        pass_wa(1, 0, 0, False, False)
-        gather_words(2, 0)
-        pass_wb(0, 0, False, True)
-        gather_scales(picked_sc, tab_sc, list1, 1)
-        gather_words(0, 1)
-        pass_wa(0, 0, 1, True, False)
-        gather_words(1, 1)
-        pass_wa(1, 0, 1, False, False)
-        gather_scales(picked2_sc, tab2_sc, list2, 1)
-        gather_words(2, 1)
-        pass_wb(0, 1, False, True)
+        def load_w2(g):
+            tile = big.tile([P, 4, HALF], F32, tag="big", name=f"w2_raw{g}")
+            rows = w2[g * HALF : (g + 1) * HALF, :].rearrange("(x t i) n -> t x i n", t=4, i=4)
+            for t in range(4):
+                nc.sync.dma_start(out=tile[:, t, :], in_=rows[t])
+            return tile
 
-        wa_raw[0, 1] = load_rows(wa[0:512, 512:1024], "wa01")
-        wa_raw[1, 1] = load_rows(wa[512:1024, 512:1024], "wa11")
-        w2_raw = [load_rows(w2[0:512, :], "w20"), load_rows(w2[512:1024, :], "w21")]
-        for u in range(4):
+        def load_state(u):
             state = big.tile([P, T], F32, tag="big", name=f"state{u}")
             nc.sync.dma_start(out=state[:], in_=gT[u * P : (u + 1) * P, :])
-            states.append(state)
+            return state
 
-        hs00 = relu(0, 0)
-        wa_q[0, 1] = quantize(cast_wa(wa_raw[0, 1], nc.vector, "g01"), "wa01")
-        g11 = cast_wa(wa_raw[1, 1], nc.scalar, "g11")
-        wa_q[1, 1] = quantize(g11, "wa11")
+        def turn(rows, first, dst, name):
+            turned = psum.tile([P, 4, P], F32, tag="bank", name=name)
+            for t in range(4):
+                nc.tensor.transpose(turned[:, t, :], rows[:, t * P : (t + 1) * P], identity[:])
+            nc.scalar.copy(out=dst[:], in_=turned[:, :, first : first + dst.shape[2]])
+
+        def sort_bias(engine):
+            engine.tensor_copy(
+                out=bias_sorted[:].rearrange("p (t x i) -> p t x i", t=4, i=4),
+                in_=bias_rows[:].rearrange("p (x t i) -> p t x i", t=4, i=4),
+            )
+
+        def gate(jh, u):
+            z = psum.tile([P, HALF], F32, tag="bank", name=f"z{jh}{u}")
+            m = slice(u * P, (u + 1) * P)
+            for g in range(2):
+                nc.tensor.matmul_mx(
+                    out=z[:],
+                    lhsT=w2_q[g][0][:, m].bitcast(FP8X4),
+                    lhsT_scale=w2_q[g][1][:, m],
+                    rhs=h_q[g, jh][0][:].bitcast(FP8X4),
+                    rhs_scale=h_q[g, jh][1][:],
+                    start=(g == 0),
+                    stop=(g == 1),
+                )
+            sig = stage.tile([P, HALF], F32, tag="sig", name=f"sig{jh}{u}", bufs=8)
+            nc.scalar.activation(out=sig[:], in_=z[:], func=ACT.Sigmoid, bias=c_sb[:, u, :])
+            sigs[jh, u] = sig
+
+        def message(jh, u):
+            res = stage.tile([P, HALF], F32, tag="res", name=f"res{jh}{u}", bufs=8)
+            nc.vector.tensor_tensor(res[:], states[u][:].indirect(list1[:, lcols(jh)]), sigs[jh, u][:], MULT)
+            nc.sync.dma_start(out=out[u * P : (u + 1) * P, cols(jh)], in_=res[:])
+
+        nc.gpsimd.memset(wb_sc_raw[:], 0)
+        nc.gpsimd.memset(tab2_sc[:], 0)
+        make_identity(nc, identity[:])
+        nc.gpsimd.memset(bias_rows[:], 0.0)
+        nc.gpsimd.memset(tab_sc[:], 0)
+        nc.vector.memset(warm_in[:], 0.0)
+        nc.scalar.activation(out=warm_out[:], in_=warm_in[:], func=ACT.Sigmoid)
+        nc.scalar.dma_start(out=wb_raw[:], in_=wb_words[0].bitcast(I32))
+        load_plane(nc.scalar, wb_sc_raw, wb_scales[0])
+        nc.scalar.dma_start(out=bias_rows[2:3, :], in_=c.rearrange("(g x) -> g x", g=1))
+        load_plane(nc.scalar, tab2_sc, tab2_scales[0])
+        nc.scalar.dma_start(out=bias_rows[0:2, :], in_=b.rearrange("(g x) -> g x", g=2))
+        tabs[2] = load_table(tab2_words[0], "tab2")
+        nc.sync.dma_start(list2[:], offs2)
+        nc.sync.dma_start(list1[:], offs)
+        tabs[0] = load_table(tab_words[0], "tab0")
+        raw["A00"] = load_rows(wa[0:512, 0:512], "wA00")
+        tabs[1] = load_table(tab_words[1], "tab1")
+        load_tab_scales(nc.sync)
+        raw["A10"] = load_rows(wa[512:1024, 0:512], "wA10")
+        raw["A11"] = load_rows(wa[512:1024, 512:1024], "wA11")
+        raw["A01"] = load_rows(wa[0:512, 512:1024], "wA01")
+        raw["W0"] = load_w2(0)
+        raw["W1"] = load_w2(1)
+        states[0] = load_state(0)
+        states[1] = load_state(1)
+        states[2] = load_state(2)
+        states[3] = load_state(3)
+        turn(bias_rows, 2, c_sb, "c_turned")
+        sort_bias(nc.gpsimd)
+        turn(bias_sorted, 0, b_sb, "b_turned")
+        gather_words(2, None)
+        permute_wb()
+        gather_words(0, None)
+        gather_scales(picked2_sc, tab2_sc, list2, None)
+        grouped["A00"] = cast_wa(raw["A00"], [nc.scalar], "gA00")
+        wa_q[0, 0] = quantize(grouped["A00"], "qA00")
+        gather_words(1, None)
+        gather_scales(picked_sc, tab_sc, list1, 0)
+        gather_scales(picked_sc, tab_sc, list1, 1)
+        grouped["A10"] = cast_wa(raw["A10"], [nc.scalar], "gA10")
+        wa_q[1, 0] = quantize(grouped["A10"], "qA10")
+        pass_wb(0, 0, True, False)
+        pass_wb(0, 1, True, False)
+        pass_wa(0, 0, 0, False, False)
+        pass_wa(1, 0, 0, False, True)
+        pass_wa(1, 0, 1, False, False)
+        pass_wa(0, 0, 1, False, True)
+        grouped["A11"] = cast_wa(raw["A11"], [nc.scalar, nc.vector], "gA11")
+        wa_q[1, 1] = quantize(grouped["A11"], "qA11")
+        grouped["A01"] = cast_wa(raw["A01"], [nc.vector], "gA01")
+        hs["00"] = relu(0, 0)
+        wa_q[0, 1] = quantize(grouped["A01"], "qA01")
+        grouped["h00"] = interleave(hs["00"], [nc.vector], "hg00")
         pass_wb(1, 0, True, False)
-        pass_wa(0, 1, 0, False, False)
-        pass_wa(1, 1, 0, False, True)
-        quantize_h(hs00, 0, 0)
-        hs01 = relu(0, 1)
-        hs10 = relu(1, 0)
-        pass_wb(1, 1, True, False)
-        pass_wa(0, 1, 1, False, False)
+        pass_wa(1, 1, 0, False, False)
+        pass_wa(0, 1, 0, False, True)
+        h_q[0, 0] = quantize(grouped["h00"], "qh00")
+        grouped["W0"] = interleave(raw["W0"], [nc.scalar, nc.vector], "gW0")
+        hs["01"] = relu(0, 1)
+        hs["10"] = relu(1, 0)
+        pass_wa(0, 1, 1, True, False)
+        pass_wb(1, 1, False, False)
         pass_wa(1, 1, 1, False, True)
-        w2_q[0] = quantize(interleave(w2_raw[0], nc.vector, "gw0"), "w20")
-        w2_q[1] = quantize(interleave(w2_raw[1], nc.vector, "gw1"), "w21")
-        quantize_h(hs10, 1, 0)
-        quantize_h(hs01, 0, 1)
-        hs11 = relu(1, 1)
-        quantize_h(hs11, 1, 1)
-        gate(0)
-        gate(1)
+        w2_q[0] = quantize(grouped["W0"], "qW0")
+        grouped["W1"] = interleave(raw["W1"], [nc.vector], "gW1")
+        grouped["h10"] = interleave(hs["10"], [nc.vector], "hg10")
+        grouped["h01"] = interleave(hs["01"], [nc.vector], "hg01")
+        w2_q[1] = quantize(grouped["W1"], "qW1")
+        h_q[1, 0] = quantize(grouped["h10"], "qh10")
+        h_q[0, 1] = quantize(grouped["h01"], "qh01")
+        hs["11"] = relu(1, 1)
+        grouped["h11"] = interleave(hs["11"], [nc.vector], "hg11")
+        h_q[1, 1] = quantize(grouped["h11"], "qh11")
+        gate(0, 0)
+        message(0, 0)
+        gate(0, 1)
+        message(0, 1)
+        gate(0, 2)
+        message(0, 2)
+        gate(0, 3)
+        message(0, 3)
+        gate(1, 0)
+        message(1, 0)
+        gate(1, 1)
+        message(1, 1)
+        gate(1, 2)
+        message(1, 2)
+        gate(1, 3)
+        message(1, 3)

@@ -98,7 +98,7 @@ def tile_list_edge_gated_messages_kernel(
                 nc.vector.tensor_copy(out=out, in_=in_)
 
         def cast_wa(raw, engines, name):
-            grouped = stage.tile([P, 4 * HALF], BF16, tag="grouped", name=name, bufs=5, align_bytes=64)
+            grouped = stage.tile([P, 4 * HALF], BF16, tag="grouped", name=name, bufs=6, align_bytes=64)
             share = 4 // len(engines)
             for s, engine in enumerate(engines):
                 ts = slice(share * s, share * (s + 1))
@@ -110,7 +110,7 @@ def tile_list_edge_gated_messages_kernel(
             return grouped
 
         def interleave(raw, engines, name):
-            grouped = stage.tile([P, 4 * HALF], BF16, tag="grouped", name=name, bufs=5, align_bytes=64)
+            grouped = stage.tile([P, 4 * HALF], BF16, tag="grouped", name=name, bufs=6, align_bytes=64)
             share = HALF // len(engines)
             for s, engine in enumerate(engines):
                 copy_on(
@@ -204,9 +204,10 @@ def tile_list_edge_gated_messages_kernel(
             nc.scalar.copy(out=dst[:], in_=turned[:, :, first : first + dst.shape[2]])
 
         def sort_bias(engine):
-            engine.tensor_copy(
-                out=bias_sorted[:].rearrange("p (t x i) -> p t x i", t=4, i=4),
-                in_=bias_rows[:].rearrange("p (x t i) -> p t x i", t=4, i=4),
+            copy_on(
+                engine,
+                bias_sorted[:].rearrange("p (t x i) -> p t x i", t=4, i=4),
+                bias_rows[:].rearrange("p (x t i) -> p t x i", t=4, i=4),
             )
 
         def gate(jh, u):
@@ -231,25 +232,25 @@ def tile_list_edge_gated_messages_kernel(
             nc.vector.tensor_tensor(res[:], states[u][:].indirect(list1[:, lcols(jh)]), sigs[jh, u][:], MULT)
             nc.sync.dma_start(out=out[u * P : (u + 1) * P, cols(jh)], in_=res[:])
 
-        nc.gpsimd.memset(wb_sc_raw[:], 0)
-        nc.gpsimd.memset(tab2_sc[:], 0)
-        make_identity(nc, identity[:])
-        nc.gpsimd.memset(bias_rows[:], 0.0)
-        nc.gpsimd.memset(tab_sc[:], 0)
+        nc.gpsimd.dma_start(out=wb_raw[:], in_=wb_words[0].bitcast(I32))
+        nc.vector.memset(tab2_sc[:], 0)
+        nc.vector.memset(bias_rows[:], 0.0)
+        nc.vector.memset(wb_sc_raw[:], 0)
         nc.vector.memset(warm_in[:], 0.0)
         nc.scalar.activation(out=warm_out[:], in_=warm_in[:], func=ACT.Sigmoid)
-        nc.scalar.dma_start(out=wb_raw[:], in_=wb_words[0].bitcast(I32))
-        load_plane(nc.scalar, wb_sc_raw, wb_scales[0])
-        nc.scalar.dma_start(out=bias_rows[2:3, :], in_=c.rearrange("(g x) -> g x", g=1))
-        load_plane(nc.scalar, tab2_sc, tab2_scales[0])
-        nc.scalar.dma_start(out=bias_rows[0:2, :], in_=b.rearrange("(g x) -> g x", g=2))
+        nc.vector.memset(tab_sc[:], 0)
+        make_identity(nc, identity[:])
+        nc.gpsimd.dma_start(out=bias_rows[2:3, :], in_=c.rearrange("(g x) -> g x", g=1))
         tabs[2] = load_table(tab2_words[0], "tab2")
+        load_plane(nc.sync, tab2_sc, tab2_scales[0])
+        nc.sync.dma_start(out=bias_rows[0:2, :], in_=b.rearrange("(g x) -> g x", g=2))
         nc.sync.dma_start(list2[:], offs2)
-        nc.sync.dma_start(list1[:], offs)
         tabs[0] = load_table(tab_words[0], "tab0")
+        load_plane(nc.sync, wb_sc_raw, wb_scales[0])
         raw["A00"] = load_rows(wa[0:512, 0:512], "wA00")
-        tabs[1] = load_table(tab_words[1], "tab1")
+        nc.sync.dma_start(list1[:], offs)
         load_tab_scales(nc.sync)
+        tabs[1] = load_table(tab_words[1], "tab1")
         raw["A10"] = load_rows(wa[512:1024, 0:512], "wA10")
         raw["A11"] = load_rows(wa[512:1024, 512:1024], "wA11")
         raw["A01"] = load_rows(wa[0:512, 512:1024], "wA01")
@@ -259,47 +260,48 @@ def tile_list_edge_gated_messages_kernel(
         states[1] = load_state(1)
         states[2] = load_state(2)
         states[3] = load_state(3)
-        turn(bias_rows, 2, c_sb, "c_turned")
-        sort_bias(nc.gpsimd)
+        sort_bias(nc.scalar)
         turn(bias_sorted, 0, b_sb, "b_turned")
+        turn(bias_rows, 2, c_sb, "c_turned")
+        gather_scales(picked2_sc, tab2_sc, list2, None)
         gather_words(2, None)
         permute_wb()
         gather_words(0, None)
-        gather_scales(picked2_sc, tab2_sc, list2, None)
         grouped["A00"] = cast_wa(raw["A00"], [nc.scalar], "gA00")
         wa_q[0, 0] = quantize(grouped["A00"], "qA00")
-        gather_words(1, None)
         gather_scales(picked_sc, tab_sc, list1, 0)
         gather_scales(picked_sc, tab_sc, list1, 1)
+        gather_words(1, 0)
+        gather_words(1, 1)
         grouped["A10"] = cast_wa(raw["A10"], [nc.scalar], "gA10")
         wa_q[1, 0] = quantize(grouped["A10"], "qA10")
         pass_wb(0, 0, True, False)
         pass_wb(0, 1, True, False)
         pass_wa(0, 0, 0, False, False)
+        pass_wa(0, 0, 1, False, False)
         pass_wa(1, 0, 0, False, True)
-        pass_wa(1, 0, 1, False, False)
-        pass_wa(0, 0, 1, False, True)
-        grouped["A11"] = cast_wa(raw["A11"], [nc.scalar, nc.vector], "gA11")
+        pass_wa(1, 0, 1, False, True)
+        grouped["A11"] = cast_wa(raw["A11"], [nc.scalar], "gA11")
         wa_q[1, 1] = quantize(grouped["A11"], "qA11")
         grouped["A01"] = cast_wa(raw["A01"], [nc.vector], "gA01")
-        hs["00"] = relu(0, 0)
         wa_q[0, 1] = quantize(grouped["A01"], "qA01")
+        hs["00"] = relu(0, 0)
         grouped["h00"] = interleave(hs["00"], [nc.vector], "hg00")
-        pass_wb(1, 0, True, False)
-        pass_wa(1, 1, 0, False, False)
+        pass_wa(1, 1, 0, True, False)
+        pass_wb(1, 0, False, False)
         pass_wa(0, 1, 0, False, True)
+        grouped["W0"] = interleave(raw["W0"], [nc.vector], "gW0")
         h_q[0, 0] = quantize(grouped["h00"], "qh00")
-        grouped["W0"] = interleave(raw["W0"], [nc.scalar, nc.vector], "gW0")
-        hs["01"] = relu(0, 1)
+        w2_q[0] = quantize(grouped["W0"], "qW0")
         hs["10"] = relu(1, 0)
+        grouped["W1"] = interleave(raw["W1"], [nc.scalar, nc.vector], "gW1")
+        hs["01"] = relu(0, 1)
         pass_wa(0, 1, 1, True, False)
         pass_wb(1, 1, False, False)
         pass_wa(1, 1, 1, False, True)
-        w2_q[0] = quantize(grouped["W0"], "qW0")
-        grouped["W1"] = interleave(raw["W1"], [nc.vector], "gW1")
         grouped["h10"] = interleave(hs["10"], [nc.vector], "hg10")
-        grouped["h01"] = interleave(hs["01"], [nc.vector], "hg01")
         w2_q[1] = quantize(grouped["W1"], "qW1")
+        grouped["h01"] = interleave(hs["01"], [nc.vector], "hg01")
         h_q[1, 0] = quantize(grouped["h10"], "qh10")
         h_q[0, 1] = quantize(grouped["h01"], "qh01")
         hs["11"] = relu(1, 1)

@@ -142,7 +142,7 @@ def tile_list_edge_gated_messages_kernel(
                     lhsT=codes[:, m].bitcast(FP8X4),
                     lhsT_scale=scales[:, m],
                     rhs=picked[a][:, cols(jh)].bitcast(FP8X4),
-                    rhs_scale=picked_sc[4 * a : P, cols(jh)],
+                    rhs_scale=picked_sc[4 + 4 * a : P, cols(jh)],
                     start=start,
                     stop=stop,
                 )
@@ -182,7 +182,7 @@ def tile_list_edge_gated_messages_kernel(
         def load_tab_scales(engine):
             for q in range(4):
                 engine.dma_start(
-                    out=tab_sc[32 * q : 32 * q + 8, :], in_=tab_scales.bitcast(I32)[:, 4 * q : 4 * q + 4, :]
+                    out=tab_sc[32 * q + 4 : 32 * q + 12, :], in_=tab_scales.bitcast(I32)[:, 4 * q : 4 * q + 4, :]
                 )
 
         def load_w2(g):
@@ -232,24 +232,24 @@ def tile_list_edge_gated_messages_kernel(
             nc.vector.tensor_tensor(res[:], states[u][:].indirect(list1[:, lcols(jh)]), sigs[jh, u][:], MULT)
             nc.sync.dma_start(out=out[u * P : (u + 1) * P, cols(jh)], in_=res[:])
 
-        nc.gpsimd.dma_start(out=wb_raw[:], in_=wb_words[0].bitcast(I32))
-        nc.vector.memset(tab2_sc[:], 0)
-        nc.vector.memset(bias_rows[:], 0.0)
-        nc.vector.memset(wb_sc_raw[:], 0)
+        nc.gpsimd.memset(tab2_sc[:], 0)
+        nc.gpsimd.memset(tab_sc[:], 0)
+        nc.gpsimd.memset(wb_sc_raw[:], 0)
+        nc.gpsimd.memset(bias_rows[:], 0.0)
+        make_identity(nc, identity[:])
         nc.vector.memset(warm_in[:], 0.0)
         nc.scalar.activation(out=warm_out[:], in_=warm_in[:], func=ACT.Sigmoid)
-        nc.vector.memset(tab_sc[:], 0)
-        make_identity(nc, identity[:])
-        nc.gpsimd.dma_start(out=bias_rows[2:3, :], in_=c.rearrange("(g x) -> g x", g=1))
-        tabs[2] = load_table(tab2_words[0], "tab2")
-        load_plane(nc.sync, tab2_sc, tab2_scales[0])
-        nc.sync.dma_start(out=bias_rows[0:2, :], in_=b.rearrange("(g x) -> g x", g=2))
         nc.sync.dma_start(list2[:], offs2)
-        tabs[0] = load_table(tab_words[0], "tab0")
+        nc.sync.dma_start(list1[:], offs)
+        load_plane(nc.sync, tab2_sc, tab2_scales[0])
+        load_tab_scales(nc.sync)
+        nc.sync.dma_start(out=wb_raw[:], in_=wb_words[0].bitcast(I32))
         load_plane(nc.sync, wb_sc_raw, wb_scales[0])
         raw["A00"] = load_rows(wa[0:512, 0:512], "wA00")
-        nc.sync.dma_start(list1[:], offs)
-        load_tab_scales(nc.sync)
+        tabs[2] = load_table(tab2_words[0], "tab2")
+        nc.sync.dma_start(out=bias_rows[0:2, :], in_=b.rearrange("(g x) -> g x", g=2))
+        nc.sync.dma_start(out=bias_rows[2:3, :], in_=c.rearrange("(g x) -> g x", g=1))
+        tabs[0] = load_table(tab_words[0], "tab0")
         tabs[1] = load_table(tab_words[1], "tab1")
         raw["A10"] = load_rows(wa[512:1024, 0:512], "wA10")
         raw["A11"] = load_rows(wa[512:1024, 512:1024], "wA11")
@@ -264,16 +264,15 @@ def tile_list_edge_gated_messages_kernel(
         turn(bias_sorted, 0, b_sb, "b_turned")
         turn(bias_rows, 2, c_sb, "c_turned")
         gather_scales(picked2_sc, tab2_sc, list2, None)
-        gather_words(2, None)
+        gather_scales(picked_sc, tab_sc, list1, None)
         permute_wb()
-        gather_words(0, None)
-        grouped["A00"] = cast_wa(raw["A00"], [nc.scalar], "gA00")
+        grouped["A00"] = cast_wa(raw["A00"], [nc.scalar, nc.vector], "gA00")
         wa_q[0, 0] = quantize(grouped["A00"], "qA00")
-        gather_scales(picked_sc, tab_sc, list1, 0)
-        gather_scales(picked_sc, tab_sc, list1, 1)
-        gather_words(1, 0)
-        gather_words(1, 1)
-        grouped["A10"] = cast_wa(raw["A10"], [nc.scalar], "gA10")
+        gather_words(2, 0)
+        gather_words(2, 1)
+        gather_words(0, None)
+        gather_words(1, None)
+        grouped["A10"] = cast_wa(raw["A10"], [nc.scalar, nc.vector], "gA10")
         wa_q[1, 0] = quantize(grouped["A10"], "qA10")
         pass_wb(0, 0, True, False)
         pass_wb(0, 1, True, False)
@@ -281,7 +280,7 @@ def tile_list_edge_gated_messages_kernel(
         pass_wa(0, 0, 1, False, False)
         pass_wa(1, 0, 0, False, True)
         pass_wa(1, 0, 1, False, True)
-        grouped["A11"] = cast_wa(raw["A11"], [nc.scalar], "gA11")
+        grouped["A11"] = cast_wa(raw["A11"], [nc.scalar, nc.vector], "gA11")
         wa_q[1, 1] = quantize(grouped["A11"], "qA11")
         grouped["A01"] = cast_wa(raw["A01"], [nc.vector], "gA01")
         wa_q[0, 1] = quantize(grouped["A01"], "qA01")
@@ -293,16 +292,16 @@ def tile_list_edge_gated_messages_kernel(
         grouped["W0"] = interleave(raw["W0"], [nc.vector], "gW0")
         h_q[0, 0] = quantize(grouped["h00"], "qh00")
         w2_q[0] = quantize(grouped["W0"], "qW0")
-        hs["10"] = relu(1, 0)
-        grouped["W1"] = interleave(raw["W1"], [nc.scalar, nc.vector], "gW1")
         hs["01"] = relu(0, 1)
+        hs["10"] = relu(1, 0)
         pass_wa(0, 1, 1, True, False)
         pass_wb(1, 1, False, False)
         pass_wa(1, 1, 1, False, True)
-        grouped["h10"] = interleave(hs["10"], [nc.vector], "hg10")
-        w2_q[1] = quantize(grouped["W1"], "qW1")
         grouped["h01"] = interleave(hs["01"], [nc.vector], "hg01")
+        grouped["h10"] = interleave(hs["10"], [nc.vector], "hg10")
+        grouped["W1"] = interleave(raw["W1"], [nc.scalar, nc.vector], "gW1")
         h_q[1, 0] = quantize(grouped["h10"], "qh10")
+        w2_q[1] = quantize(grouped["W1"], "qW1")
         h_q[0, 1] = quantize(grouped["h01"], "qh01")
         hs["11"] = relu(1, 1)
         grouped["h11"] = interleave(hs["11"], [nc.vector], "hg11")

@@ -17,6 +17,7 @@ MULT = mybir.AluOpType.mult
 T, S, K, K2, H, N = 2048, 1024, 1024, 512, 1024, 512
 P = 128
 HALF = 512
+C_ROW = 32
 FLOPS = 2 * S * (K * H + K2 * H + H * N)
 
 
@@ -26,43 +27,32 @@ def tile_list_edge_gated_messages_kernel(
     nc = tc.nc
     with ExitStack() as ctx:
         keep = ctx.enter_context(tc.tile_pool(name="keep", bufs=1))
-        big = ctx.enter_context(tc.tile_pool(name="big", bufs=13))
-        stage = ctx.enter_context(tc.tile_pool(name="stage", bufs=3))
-        psum = ctx.enter_context(tc.psum_pool(name="psum", bufs=8))
+        slots = ctx.enter_context(tc.tile_pool(name="slots", bufs=1))
+        psum = ctx.enter_context(tc.psum_pool(name="psum", bufs=1))
+
+        def slot(shape, dtype, tag, name):
+            return slots.tile(shape, dtype, tag=tag, name=name, align_bytes=64)
+
+        def bank(i, shape, name):
+            return psum.tile(shape, F32, tag=f"bank{i}", name=name)
 
         list1 = keep.tile([P, S // 16], U16, name="list1")
         list2 = keep.tile([P, S // 16], U16, name="list2")
-        tab_sc = keep.tile([P, T // 4], I32, name="tab_sc")
+        tab_sc = slot([P, T // 4], I32, "tab_sc", "tab_sc")
         tab2_sc = keep.tile([P, T // 4], I32, name="tab2_sc")
-        wb_sc_raw = keep.tile([P, H // 4], I32, name="wb_sc_raw")
+        wb_sc_raw = slot([P, H // 4], I32, "wb_sc_raw", "wb_sc_raw")
         wb_raw = keep.tile([P, H // 2], I32, name="wb_raw")
-        b_sb = keep.tile([P, 4, 2], F32, name="b_sb")
-        c_sb = keep.tile([P, 4, 1], F32, name="c_sb")
+        b_rows = keep.tile([C_ROW, HALF], F32, name="b_rows")
         bias_rows = keep.tile([P, HALF], F32, name="bias_rows")
-        bias_sorted = keep.tile([P, HALF], F32, name="bias_sorted")
+        bias = keep.tile([P, 4, C_ROW + 1], F32, name="bias")
         identity = keep.tile([P, P], F32, name="identity")
         warm_in = keep.tile([P, 1], F32, name="warm_in")
         warm_out = keep.tile([P, 1], F32, name="warm_out")
-
-        def load_table(words, name):
-            tile = big.tile([P, T], I32, tag="big", name=name)
-            nc.sync.dma_start(out=tile[:], in_=words.rearrange("p t i -> p (t i)").bitcast(I32))
-            return tile
-
-        def load_rows(rows, name):
-            tile = big.tile([P, 4, HALF], F32, tag="big", name=name)
-            nc.sync.dma_start(out=tile[:], in_=rows.rearrange("(p j) x -> p j x", j=4))
-            return tile
-
-        def load_plane(engine, tile, scales):
-            rows = scales.bitcast(I32).rearrange("(q r) x -> r q x", r=4)
-            for r in range(4):
-                engine.dma_start(out=tile[r:P:32, :], in_=rows[r])
-
-        picked = [keep.tile([P, S], U32, name=f"picked{a}", align_bytes=64) for a in range(3)]
+        picked = {a: keep.tile([P, S], U32, name=f"picked{a}", align_bytes=64) for a in range(3)}
         picked_sc = keep.tile([P, S], U8, name="picked_sc", align_bytes=64)
         picked2_sc = keep.tile([P, S], U8, name="picked2_sc", align_bytes=64)
-        lists = [list1, list1, list2]
+        wb_codes = keep.tile([P, H // 2], I32, name="wb_codes", align_bytes=64)
+        wb_sc = keep.tile([P, H // 4], I32, name="wb_sc", align_bytes=64)
 
         def cols(jh):
             return slice(0, S) if jh is None else slice(jh * HALF, (jh + 1) * HALF)
@@ -70,26 +60,45 @@ def tile_list_edge_gated_messages_kernel(
         def lcols(jh):
             return slice(cols(jh).start // 16, cols(jh).stop // 16)
 
-        def gather_words(a, jh):
-            nc.vector.tensor_copy(
-                out=picked[a][:, cols(jh)], in_=tabs[a][:].bitcast(U32).indirect(lists[a][:, lcols(jh)])
-            )
+        def load_table(words, name):
+            tile = slot([P, T], I32, name, name)
+            nc.sync.dma_start(out=tile[:], in_=words.rearrange("p t i -> p (t i)").bitcast(I32))
+            return tile
 
-        def gather_scales(dst, src, lst, jh):
-            nc.vector.tensor_copy(out=dst[:, cols(jh)], in_=src[:].bitcast(U8).indirect(lst[:, lcols(jh)]))
+        def load_wa(a, g):
+            tile = slot([P, 4, HALF], F32, f"wa{a}{g}", f"wa{a}{g}")
+            rows = wa[a * HALF : (a + 1) * HALF, g * HALF : (g + 1) * HALF]
+            nc.sync.dma_start(out=tile[:], in_=rows.rearrange("(p j) x -> p j x", j=4))
+            return tile
 
-        wb_codes = keep.tile([P, H // 2], I32, name="wb_codes", align_bytes=64)
-        wb_sc = keep.tile([P, H // 4], I32, name="wb_sc", align_bytes=64)
+        def load_w2(g):
+            tile = slot([P, 4, HALF], F32, f"w2{g}", f"w2{g}")
+            rows = w2[g * HALF : (g + 1) * HALF, :].rearrange("(x t i) n -> t x i n", t=4, i=4)
+            for t in range(4):
+                nc.sync.dma_start(out=tile[:, t, :], in_=rows[t])
+            return tile
 
-        def permute_wb():
-            nc.vector.tensor_copy(
-                out=wb_codes[:].rearrange("p (g t x w) -> p g t x w", g=2, t=4, w=2),
-                in_=wb_raw[:].rearrange("p (g x t w) -> p g t x w", g=2, t=4, w=2),
-            )
-            nc.vector.tensor_copy(
-                out=wb_sc[:].rearrange("p (g t x) -> p g t x", g=2, t=4),
-                in_=wb_sc_raw[:].rearrange("p (g x t) -> p g t x", g=2, t=4),
-            )
+        def load_plane(tile, scales):
+            rows = scales.bitcast(I32).rearrange("(q r) x -> r q x", r=4)
+            for r in range(4):
+                nc.sync.dma_start(out=tile[r:P:32, :], in_=rows[r])
+
+        def load_tab_scales():
+            for q in range(4):
+                nc.sync.dma_start(
+                    out=tab_sc[32 * q + 4 : 32 * q + 12, :], in_=tab_scales.bitcast(I32)[:, 4 * q : 4 * q + 4, :]
+                )
+
+        def load_state(u):
+            state = keep.tile([P, T], F32, name=f"state{u}")
+            nc.sync.dma_start(out=state[:], in_=gT[u * P : (u + 1) * P, :])
+            return state
+
+        def gather_words(dst, table, lst, jh):
+            nc.vector.tensor_copy(out=dst[:, cols(jh)], in_=table[:].bitcast(U32).indirect(lst[:, lcols(jh)]))
+
+        def gather_scales(dst, src, lst):
+            nc.vector.tensor_copy(out=dst[:], in_=src[:].bitcast(U8).indirect(lst[:]))
 
         def copy_on(engine, out, in_):
             if engine is nc.scalar:
@@ -97,8 +106,8 @@ def tile_list_edge_gated_messages_kernel(
             else:
                 nc.vector.tensor_copy(out=out, in_=in_)
 
-        def cast_wa(raw, engines, name):
-            grouped = stage.tile([P, 4 * HALF], BF16, tag="grouped", name=name, bufs=6, align_bytes=64)
+        def cast_wa(raw, engines, tag, name):
+            grouped = slot([P, 4 * HALF], BF16, tag, name)
             share = 4 // len(engines)
             for s, engine in enumerate(engines):
                 ts = slice(share * s, share * (s + 1))
@@ -109,36 +118,33 @@ def tile_list_edge_gated_messages_kernel(
                 )
             return grouped
 
-        def interleave(raw, engines, name):
-            grouped = stage.tile([P, 4 * HALF], BF16, tag="grouped", name=name, bufs=6, align_bytes=64)
-            share = HALF // len(engines)
-            for s, engine in enumerate(engines):
-                copy_on(
-                    engine,
-                    grouped[:, 4 * share * s : 4 * share * (s + 1)].rearrange("p (x i j) -> p x j i", i=4, j=4),
-                    raw[:, :, share * s : share * (s + 1)].rearrange("p j (x i) -> p x j i", i=4),
-                )
+        def interleave(raw, engine, tag, name):
+            grouped = slot([P, 4 * HALF], BF16, tag, name)
+            copy_on(
+                engine,
+                grouped[:].rearrange("p (x i j) -> p x j i", i=4, j=4),
+                raw[:].rearrange("p j (x i) -> p x j i", i=4),
+            )
             return grouped
 
-        def quantize(grouped, name):
-            codes = keep.tile([P, HALF], U32, name=name + "_codes", align_bytes=64)
+        def quantize(grouped, name, tag=None):
+            codes = slot([P, HALF], U32, tag or name, name + "_codes")
             scales = keep.tile([P, HALF], U8, name=name + "_sc", align_bytes=64)
             nc.vector.quantize_mx(out=codes[:].bitcast(FP8X4), scales=scales[:], in_=grouped[:])
             return codes, scales
 
-        wa_q = {}
-        w2_q = {}
-        h_q = {}
-        banks = {}
+        acc = {}
 
-        def pass_wa(a, g, jh, start, stop):
-            codes, scales = wa_q[a, g]
+        def open_banks(g, jh):
             for t in range(4):
-                if start:
-                    banks[g, jh, t] = psum.tile([P, HALF], F32, tag="bank", name=f"a{g}{jh}{t}")
+                acc[g, jh, t] = bank(4 * jh + t, [P, HALF], f"a{g}{jh}{t}")
+
+        def pass_wa(quantized, a, g, jh, start, stop):
+            codes, scales = quantized
+            for t in range(4):
                 m = slice(t * P, (t + 1) * P)
                 nc.tensor.matmul_mx(
-                    out=banks[g, jh, t][:],
+                    out=acc[g, jh, t][:],
                     lhsT=codes[:, m].bitcast(FP8X4),
                     lhsT_scale=scales[:, m],
                     rhs=picked[a][:, cols(jh)].bitcast(FP8X4),
@@ -149,12 +155,10 @@ def tile_list_edge_gated_messages_kernel(
 
         def pass_wb(g, jh, start, stop):
             for t in range(4):
-                if start:
-                    banks[g, jh, t] = psum.tile([P, HALF], F32, tag="bank", name=f"a{g}{jh}{t}")
                 m = slice(g * HALF + t * P, g * HALF + (t + 1) * P)
                 m2 = slice(2 * m.start, 2 * m.stop)
                 nc.tensor.matmul_mx(
-                    out=banks[g, jh, t][:],
+                    out=acc[g, jh, t][:],
                     lhsT=wb_codes[:].bitcast(U8)[:, m2].bitcast(FP4X4),
                     lhsT_scale=wb_sc[:].bitcast(U8)[:, m],
                     rhs=picked[2][:, cols(jh)].bitcast(FP8X4),
@@ -163,162 +167,126 @@ def tile_list_edge_gated_messages_kernel(
                     stop=stop,
                 )
 
-        def relu(g, jh):
-            hs = stage.tile([P, 4, HALF], BF16, tag="hs", name=f"hs{g}{jh}", bufs=4)
+        def relu(g, jh, tag):
+            hs = slot([P, 4, HALF], BF16, tag, f"hs{g}{jh}")
             for t in range(4):
-                nc.scalar.activation(
-                    out=hs[:, t, :], in_=banks[g, jh, t][:], func=ACT.Relu, bias=b_sb[:, t, g : g + 1]
-                )
+                nc.scalar.activation(out=hs[:, t, :], in_=acc[g, jh, t][:], func=ACT.Relu, bias=bias[:, t, g : g + 1])
             return hs
 
-
-        tabs = {}
-        raw = {}
-        states = {}
-        grouped = {}
-        hs = {}
-        sigs = {}
-
-        def load_tab_scales(engine):
-            for q in range(4):
-                engine.dma_start(
-                    out=tab_sc[32 * q + 4 : 32 * q + 12, :], in_=tab_scales.bitcast(I32)[:, 4 * q : 4 * q + 4, :]
-                )
-
-        def load_w2(g):
-            tile = big.tile([P, 4, HALF], F32, tag="big", name=f"w2_raw{g}")
-            rows = w2[g * HALF : (g + 1) * HALF, :].rearrange("(x t i) n -> t x i n", t=4, i=4)
-            for t in range(4):
-                nc.sync.dma_start(out=tile[:, t, :], in_=rows[t])
-            return tile
-
-        def load_state(u):
-            state = big.tile([P, T], F32, tag="big", name=f"state{u}")
-            nc.sync.dma_start(out=state[:], in_=gT[u * P : (u + 1) * P, :])
-            return state
-
-        def turn(rows, first, dst, name):
-            turned = psum.tile([P, 4, P], F32, tag="bank", name=name)
-            for t in range(4):
-                nc.tensor.transpose(turned[:, t, :], rows[:, t * P : (t + 1) * P], identity[:])
-            nc.scalar.copy(out=dst[:], in_=turned[:, :, first : first + dst.shape[2]])
-
-        def sort_bias(engine):
-            copy_on(
-                engine,
-                bias_sorted[:].rearrange("p (t x i) -> p t x i", t=4, i=4),
-                bias_rows[:].rearrange("p (x t i) -> p t x i", t=4, i=4),
-            )
-
-        def gate(jh, u):
-            z = psum.tile([P, HALF], F32, tag="bank", name=f"z{jh}{u}")
+        def message(jh, u, w2_q, h_q, state):
+            z = bank(4 * jh + u, [P, HALF], f"z{jh}{u}")
             m = slice(u * P, (u + 1) * P)
             for g in range(2):
                 nc.tensor.matmul_mx(
                     out=z[:],
                     lhsT=w2_q[g][0][:, m].bitcast(FP8X4),
                     lhsT_scale=w2_q[g][1][:, m],
-                    rhs=h_q[g, jh][0][:].bitcast(FP8X4),
-                    rhs_scale=h_q[g, jh][1][:],
+                    rhs=h_q[g][0][:].bitcast(FP8X4),
+                    rhs_scale=h_q[g][1][:],
                     start=(g == 0),
                     stop=(g == 1),
                 )
-            sig = stage.tile([P, HALF], F32, tag="sig", name=f"sig{jh}{u}", bufs=8)
-            nc.scalar.activation(out=sig[:], in_=z[:], func=ACT.Sigmoid, bias=c_sb[:, u, :])
-            sigs[jh, u] = sig
-
-        def message(jh, u):
-            res = stage.tile([P, HALF], F32, tag="res", name=f"res{jh}{u}", bufs=8)
-            nc.vector.tensor_tensor(res[:], states[u][:].indirect(list1[:, lcols(jh)]), sigs[jh, u][:], MULT)
+            sig = keep.tile([P, HALF], F32, name=f"sig{jh}{u}")
+            nc.scalar.activation(out=sig[:], in_=z[:], func=ACT.Sigmoid, bias=bias[:, u, C_ROW : C_ROW + 1])
+            res = keep.tile([P, HALF], F32, name=f"res{jh}{u}")
+            nc.vector.tensor_tensor(res[:], state[:].indirect(list1[:, lcols(jh)]), sig[:], MULT)
             nc.sync.dma_start(out=out[u * P : (u + 1) * P, cols(jh)], in_=res[:])
 
         nc.gpsimd.memset(tab2_sc[:], 0)
         nc.gpsimd.memset(tab_sc[:], 0)
         nc.gpsimd.memset(wb_sc_raw[:], 0)
+        nc.gpsimd.memset(b_rows[:], 0.0)
         nc.gpsimd.memset(bias_rows[:], 0.0)
         make_identity(nc, identity[:])
         nc.vector.memset(warm_in[:], 0.0)
         nc.scalar.activation(out=warm_out[:], in_=warm_in[:], func=ACT.Sigmoid)
+
         nc.sync.dma_start(list2[:], offs2)
         nc.sync.dma_start(list1[:], offs)
-        load_plane(nc.sync, tab2_sc, tab2_scales[0])
-        load_tab_scales(nc.sync)
+        load_plane(tab2_sc, tab2_scales[0])
+        tab2 = load_table(tab2_words[0], "tab2")
         nc.sync.dma_start(out=wb_raw[:], in_=wb_words[0].bitcast(I32))
-        load_plane(nc.sync, wb_sc_raw, wb_scales[0])
-        raw["A00"] = load_rows(wa[0:512, 0:512], "wA00")
-        tabs[2] = load_table(tab2_words[0], "tab2")
-        nc.sync.dma_start(out=bias_rows[0:2, :], in_=b.rearrange("(g x) -> g x", g=2))
-        nc.sync.dma_start(out=bias_rows[2:3, :], in_=c.rearrange("(g x) -> g x", g=1))
-        tabs[0] = load_table(tab_words[0], "tab0")
-        tabs[1] = load_table(tab_words[1], "tab1")
-        raw["A10"] = load_rows(wa[512:1024, 0:512], "wA10")
-        raw["A11"] = load_rows(wa[512:1024, 512:1024], "wA11")
-        raw["A01"] = load_rows(wa[0:512, 512:1024], "wA01")
-        raw["W0"] = load_w2(0)
-        raw["W1"] = load_w2(1)
-        states[0] = load_state(0)
-        states[1] = load_state(1)
-        states[2] = load_state(2)
-        states[3] = load_state(3)
-        sort_bias(nc.scalar)
-        turn(bias_sorted, 0, b_sb, "b_turned")
-        turn(bias_rows, 2, c_sb, "c_turned")
-        gather_scales(picked2_sc, tab2_sc, list2, None)
-        gather_scales(picked_sc, tab_sc, list1, None)
-        permute_wb()
-        grouped["A00"] = cast_wa(raw["A00"], [nc.scalar, nc.vector], "gA00")
-        wa_q[0, 0] = quantize(grouped["A00"], "qA00")
-        gather_words(2, 0)
-        gather_words(2, 1)
-        gather_words(0, None)
-        gather_words(1, None)
-        grouped["A10"] = cast_wa(raw["A10"], [nc.scalar, nc.vector], "gA10")
-        wa_q[1, 0] = quantize(grouped["A10"], "qA10")
-        pass_wb(0, 0, True, False)
-        pass_wb(0, 1, True, False)
-        pass_wa(0, 0, 0, False, False)
-        pass_wa(0, 0, 1, False, False)
-        pass_wa(1, 0, 0, False, True)
-        pass_wa(1, 0, 1, False, True)
-        grouped["A11"] = cast_wa(raw["A11"], [nc.scalar, nc.vector], "gA11")
-        wa_q[1, 1] = quantize(grouped["A11"], "qA11")
-        grouped["A01"] = cast_wa(raw["A01"], [nc.vector], "gA01")
-        wa_q[0, 1] = quantize(grouped["A01"], "qA01")
-        hs["00"] = relu(0, 0)
-        grouped["h00"] = interleave(hs["00"], [nc.vector], "hg00")
-        pass_wa(1, 1, 0, True, False)
-        pass_wb(1, 0, False, False)
-        pass_wa(0, 1, 0, False, True)
-        grouped["W0"] = interleave(raw["W0"], [nc.vector], "gW0")
-        h_q[0, 0] = quantize(grouped["h00"], "qh00")
-        w2_q[0] = quantize(grouped["W0"], "qW0")
-        hs["01"] = relu(0, 1)
-        hs["10"] = relu(1, 0)
-        pass_wa(0, 1, 1, True, False)
+        load_plane(wb_sc_raw, wb_scales[0])
+        wa00 = load_wa(0, 0)
+        load_tab_scales()
+        nc.sync.dma_start(out=b_rows[0:2, :], in_=b.rearrange("(g x) -> g x", g=2))
+        nc.sync.dma_start(out=bias_rows[C_ROW : C_ROW + 1, :], in_=c.rearrange("(g x) -> g x", g=1))
+        tab0 = load_table(tab_words[0], "tab0")
+        wa10 = load_wa(1, 0)
+        tab1 = load_table(tab_words[1], "tab1")
+        wa01 = load_wa(0, 1)
+        wa11 = load_wa(1, 1)
+        w20 = load_w2(0)
+        w21 = load_w2(1)
+        states = [load_state(u) for u in range(4)]
+
+        gather_scales(picked2_sc, tab2_sc, list2)
+        gather_words(picked[2], tab2, list2, None)
+        nc.vector.tensor_copy(
+            out=wb_codes[:].rearrange("p (g t x w) -> p g t x w", g=2, t=4, w=2),
+            in_=wb_raw[:].rearrange("p (g x t w) -> p g t x w", g=2, t=4, w=2),
+        )
+        nc.vector.tensor_copy(
+            out=wb_sc[:].rearrange("p (g t x) -> p g t x", g=2, t=4),
+            in_=wb_sc_raw[:].rearrange("p (g x t) -> p g t x", g=2, t=4),
+        )
+        gather_scales(picked_sc, tab_sc, list1)
+        g_wa00 = cast_wa(wa00, [nc.scalar], "ga", "g_wa00")
+        q_wa00 = quantize(g_wa00, "q_wa00", "tab_sc")
+
+        nc.scalar.copy(
+            out=bias_rows[0:C_ROW, :].rearrange("p (t x i) -> p t x i", t=4, i=4),
+            in_=b_rows[:].rearrange("p (x t i) -> p t x i", t=4, i=4),
+        )
+        turned = bank(7, [P, 4, P], "turned")
+        for t in range(4):
+            nc.tensor.transpose(turned[:, t, :], bias_rows[:, t * P : (t + 1) * P], identity[:])
+        nc.scalar.copy(out=bias[:], in_=turned[:, :, 0 : C_ROW + 1])
+
+        for jh in range(2):
+            gather_words(picked[0], tab0, list1, jh)
+        g_wa10 = cast_wa(wa10, [nc.scalar, nc.vector], "gb", "g_wa10")
+        q_wa10 = quantize(g_wa10, "q_wa10")
+        for jh in range(2):
+            gather_words(picked[1], tab1, list1, jh)
+        for jh in range(2):
+            open_banks(0, jh)
+            pass_wb(0, jh, True, False)
+        for jh in range(2):
+            pass_wa(q_wa00, 0, 0, jh, False, False)
+        for jh in range(2):
+            pass_wa(q_wa10, 1, 0, jh, False, True)
+
+        hs00 = relu(0, 0, "ga")
+        hs01 = relu(0, 1, "gb")
+        g_wa01 = cast_wa(wa01, [nc.vector], "tab0", "g_wa01")
+        q_wa01 = quantize(g_wa01, "q_wa01")
+        g_wa11 = cast_wa(wa11, [nc.vector], "tab2", "g_wa11")
+        q_wa11 = quantize(g_wa11, "q_wa11")
+        g_h00 = interleave(hs00, nc.vector, "wa11", "g_h00")
+        q_h00 = quantize(g_h00, "q_h00")
+        open_banks(1, 0)
+        pass_wb(1, 0, True, False)
+        pass_wa(q_wa01, 0, 1, 0, False, False)
+        pass_wa(q_wa11, 1, 1, 0, False, True)
+        open_banks(1, 1)
+        pass_wa(q_wa11, 1, 1, 1, True, False)
         pass_wb(1, 1, False, False)
-        pass_wa(1, 1, 1, False, True)
-        grouped["h01"] = interleave(hs["01"], [nc.vector], "hg01")
-        grouped["h10"] = interleave(hs["10"], [nc.vector], "hg10")
-        grouped["W1"] = interleave(raw["W1"], [nc.scalar, nc.vector], "gW1")
-        h_q[1, 0] = quantize(grouped["h10"], "qh10")
-        w2_q[1] = quantize(grouped["W1"], "qW1")
-        h_q[0, 1] = quantize(grouped["h01"], "qh01")
-        hs["11"] = relu(1, 1)
-        grouped["h11"] = interleave(hs["11"], [nc.vector], "hg11")
-        h_q[1, 1] = quantize(grouped["h11"], "qh11")
-        gate(0, 0)
-        message(0, 0)
-        gate(0, 1)
-        message(0, 1)
-        gate(0, 2)
-        message(0, 2)
-        gate(0, 3)
-        message(0, 3)
-        gate(1, 0)
-        message(1, 0)
-        gate(1, 1)
-        message(1, 1)
-        gate(1, 2)
-        message(1, 2)
-        gate(1, 3)
-        message(1, 3)
+        pass_wa(q_wa01, 0, 1, 1, False, True)
+
+        hs10 = relu(1, 0, "wa01")
+        g_w21 = interleave(w21, nc.scalar, "wa10", "g_w21")
+        hs11 = relu(1, 1, "w21")
+        g_w20 = interleave(w20, nc.vector, "wa00", "g_w20")
+        g_h10 = interleave(hs10, nc.vector, "w20", "g_h10")
+        q_w20 = quantize(g_w20, "q_w20")
+        q_w21 = quantize(g_w21, "q_w21")
+        q_h10 = quantize(g_h10, "q_h10")
+        g_h01 = interleave(hs01, nc.vector, "w20", "g_h01")
+        q_h01 = quantize(g_h01, "q_h01")
+        for u in range(4):
+            message(0, u, (q_w20, q_w21), (q_h00, q_h10), states[u])
+        g_h11 = interleave(hs11, nc.scalar, "q_h10", "g_h11")
+        q_h11 = quantize(g_h11, "q_h11")
+        for u in range(4):
+            message(1, u, (q_w20, q_w21), (q_h01, q_h11), states[u])

@@ -127,10 +127,15 @@ def tile_list_edge_gated_messages_kernel(
             )
             return grouped
 
-        def quantize(grouped, name, tag=None):
+        def quantize(grouped, name, tag=None, parts=1):
             codes = slot([P, HALF], U32, tag or name, name + "_codes")
             scales = keep.tile([P, HALF], U8, name=name + "_sc", align_bytes=64)
-            nc.vector.quantize_mx(out=codes[:].bitcast(FP8X4), scales=scales[:], in_=grouped[:])
+            share = HALF // parts
+            for s in range(parts):
+                m = slice(share * s, share * (s + 1))
+                nc.vector.quantize_mx(
+                    out=codes[:, m].bitcast(FP8X4), scales=scales[:, m], in_=grouped[:, 4 * m.start : 4 * m.stop]
+                )
             return codes, scales
 
         acc = {}
@@ -173,7 +178,7 @@ def tile_list_edge_gated_messages_kernel(
                 nc.scalar.activation(out=hs[:, t, :], in_=acc[g, jh, t][:], func=ACT.Relu, bias=bias[:, t, g : g + 1])
             return hs
 
-        def message(jh, u, w2_q, h_q, state):
+        def gate(jh, u, w2_q, h_q):
             z = bank(4 * jh + u, [P, HALF], f"z{jh}{u}")
             m = slice(u * P, (u + 1) * P)
             for g in range(2):
@@ -188,8 +193,11 @@ def tile_list_edge_gated_messages_kernel(
                 )
             sig = keep.tile([P, HALF], F32, name=f"sig{jh}{u}")
             nc.scalar.activation(out=sig[:], in_=z[:], func=ACT.Sigmoid, bias=bias[:, u, C_ROW : C_ROW + 1])
-            res = keep.tile([P, HALF], F32, name=f"res{jh}{u}")
-            nc.vector.tensor_tensor(res[:], state[:].indirect(list1[:, lcols(jh)]), sig[:], MULT)
+            return sig
+
+        def message(jh, u, sig, tag=None):
+            res = slot([P, HALF], F32, tag or f"res{jh}{u}", f"res{jh}{u}")
+            nc.vector.tensor_tensor(res[:], states[u][:].indirect(list1[:, lcols(jh)]), sig[:], MULT)
             nc.sync.dma_start(out=out[u * P : (u + 1) * P, cols(jh)], in_=res[:])
 
         nc.gpsimd.memset(tab2_sc[:], 0)
@@ -204,11 +212,11 @@ def tile_list_edge_gated_messages_kernel(
         nc.sync.dma_start(list2[:], offs2)
         nc.sync.dma_start(list1[:], offs)
         load_plane(tab2_sc, tab2_scales[0])
-        tab2 = load_table(tab2_words[0], "tab2")
+        load_tab_scales()
         nc.sync.dma_start(out=wb_raw[:], in_=wb_words[0].bitcast(I32))
         load_plane(wb_sc_raw, wb_scales[0])
+        tab2 = load_table(tab2_words[0], "tab2")
         wa00 = load_wa(0, 0)
-        load_tab_scales()
         nc.sync.dma_start(out=b_rows[0:2, :], in_=b.rearrange("(g x) -> g x", g=2))
         nc.sync.dma_start(out=bias_rows[C_ROW : C_ROW + 1, :], in_=c.rearrange("(g x) -> g x", g=1))
         tab0 = load_table(tab_words[0], "tab0")
@@ -221,7 +229,7 @@ def tile_list_edge_gated_messages_kernel(
         states = [load_state(u) for u in range(4)]
 
         gather_scales(picked2_sc, tab2_sc, list2)
-        gather_words(picked[2], tab2, list2, None)
+        gather_scales(picked_sc, tab_sc, list1)
         nc.vector.tensor_copy(
             out=wb_codes[:].rearrange("p (g t x w) -> p g t x w", g=2, t=4, w=2),
             in_=wb_raw[:].rearrange("p (g x t w) -> p g t x w", g=2, t=4, w=2),
@@ -230,9 +238,10 @@ def tile_list_edge_gated_messages_kernel(
             out=wb_sc[:].rearrange("p (g t x) -> p g t x", g=2, t=4),
             in_=wb_sc_raw[:].rearrange("p (g x t) -> p g t x", g=2, t=4),
         )
-        gather_scales(picked_sc, tab_sc, list1)
-        g_wa00 = cast_wa(wa00, [nc.scalar], "ga", "g_wa00")
-        q_wa00 = quantize(g_wa00, "q_wa00", "tab_sc")
+        for jh in range(2):
+            gather_words(picked[2], tab2, list2, jh)
+        g_wa00 = cast_wa(wa00, [nc.scalar, nc.vector], "ga", "g_wa00")
+        q_wa00 = quantize(g_wa00, "q_wa00")
 
         nc.scalar.copy(
             out=bias_rows[0:C_ROW, :].rearrange("p (t x i) -> p t x i", t=4, i=4),
@@ -261,8 +270,8 @@ def tile_list_edge_gated_messages_kernel(
         hs01 = relu(0, 1, "gb")
         g_wa01 = cast_wa(wa01, [nc.vector], "tab0", "g_wa01")
         q_wa01 = quantize(g_wa01, "q_wa01")
-        g_wa11 = cast_wa(wa11, [nc.vector], "tab2", "g_wa11")
-        q_wa11 = quantize(g_wa11, "q_wa11")
+        g_wa11 = cast_wa(wa11, [nc.vector, nc.vector], "tab2", "g_wa11")
+        q_wa11 = quantize(g_wa11, "q_wa11", parts=2)
         g_h00 = interleave(hs00, nc.vector, "wa11", "g_h00")
         q_h00 = quantize(g_h00, "q_h00")
         open_banks(1, 0)
@@ -276,17 +285,19 @@ def tile_list_edge_gated_messages_kernel(
 
         hs10 = relu(1, 0, "wa01")
         g_w21 = interleave(w21, nc.scalar, "wa10", "g_w21")
-        hs11 = relu(1, 1, "w21")
         g_w20 = interleave(w20, nc.vector, "wa00", "g_w20")
         g_h10 = interleave(hs10, nc.vector, "w20", "g_h10")
         q_w20 = quantize(g_w20, "q_w20")
-        q_w21 = quantize(g_w21, "q_w21")
         q_h10 = quantize(g_h10, "q_h10")
+        q_w21 = quantize(g_w21, "q_w21")
         g_h01 = interleave(hs01, nc.vector, "w20", "g_h01")
         q_h01 = quantize(g_h01, "q_h01")
-        for u in range(4):
-            message(0, u, (q_w20, q_w21), (q_h00, q_h10), states[u])
+        sigs = [gate(0, u, (q_w20, q_w21), (q_h00, q_h10)) for u in range(4)]
+        hs11 = relu(1, 1, "w21")
         g_h11 = interleave(hs11, nc.scalar, "q_h10", "g_h11")
+        for u in range(3):
+            message(0, u, sigs[u])
         q_h11 = quantize(g_h11, "q_h11")
+        message(0, 3, sigs[3], "q_h10")
         for u in range(4):
-            message(1, u, (q_w20, q_w21), (q_h01, q_h11), states[u])
+            message(1, u, gate(1, u, (q_w20, q_w21), (q_h01, q_h11)))

@@ -118,13 +118,16 @@ def tile_list_edge_gated_messages_kernel(
                 )
             return grouped
 
-        def interleave(raw, engine, tag, name):
-            grouped = slot([P, 4 * HALF], BF16, tag, name)
+        def interleave_columns(grouped, raw, engine, columns):
             copy_on(
                 engine,
-                grouped[:].rearrange("p (x i j) -> p x j i", i=4, j=4),
-                raw[:].rearrange("p j (x i) -> p x j i", i=4),
+                grouped[:, 4 * columns.start : 4 * columns.stop].rearrange("p (x i j) -> p x j i", i=4, j=4),
+                raw[:, :, columns].rearrange("p j (x i) -> p x j i", i=4),
             )
+
+        def interleave(raw, engine, tag, name):
+            grouped = slot([P, 4 * HALF], BF16, tag, name)
+            interleave_columns(grouped, raw, engine, slice(0, HALF))
             return grouped
 
         def quantize(grouped, name, tag=None, parts=1):
@@ -191,7 +194,7 @@ def tile_list_edge_gated_messages_kernel(
                     start=(g == 0),
                     stop=(g == 1),
                 )
-            sig = keep.tile([P, HALF], F32, name=f"sig{jh}{u}")
+            sig = slot([P, HALF], F32, f"sig{jh}{u}", f"sig{jh}{u}")
             nc.scalar.activation(out=sig[:], in_=z[:], func=ACT.Sigmoid, bias=bias[:, u, C_ROW : C_ROW + 1])
             return sig
 
@@ -292,12 +295,21 @@ def tile_list_edge_gated_messages_kernel(
         q_w21 = quantize(g_w21, "q_w21")
         g_h01 = interleave(hs01, nc.vector, "w20", "g_h01")
         q_h01 = quantize(g_h01, "q_h01")
-        sigs = [gate(0, u, (q_w20, q_w21), (q_h00, q_h10)) for u in range(4)]
+        q_w2 = (q_w20, q_w21)
+        sigs = {(0, 0): gate(0, 0, q_w2, (q_h00, q_h10))}
         hs11 = relu(1, 1, "w21")
-        g_h11 = interleave(hs11, nc.scalar, "q_h10", "g_h11")
-        for u in range(3):
-            message(0, u, sigs[u])
+        g_h11 = slot([P, 4 * HALF], BF16, "g_h11", "g_h11")
+        for s in range(2):
+            interleave_columns(g_h11, hs11, nc.scalar, slice(s * HALF // 2, (s + 1) * HALF // 2))
+            sigs[0, s + 1] = gate(0, s + 1, q_w2, (q_h00, q_h10))
+        sigs[0, 3] = gate(0, 3, q_w2, (q_h00, q_h10))
+        message(0, 0, sigs[0, 0])
+        message(0, 1, sigs[0, 1])
         q_h11 = quantize(g_h11, "q_h11")
-        message(0, 3, sigs[3], "q_h10")
+        message(0, 2, sigs[0, 2])
         for u in range(4):
-            message(1, u, gate(1, u, (q_w20, q_w21), (q_h01, q_h11)))
+            sigs[1, u] = gate(1, u, q_w2, (q_h01, q_h11))
+        for u in range(3):
+            message(1, u, sigs[1, u])
+        message(0, 3, sigs[0, 3], "sig11")
+        message(1, 3, sigs[1, 3])

@@ -1,7 +1,6 @@
 from contextlib import ExitStack
 
 import concourse.mybir as mybir
-from concourse.masks import make_identity
 
 F32 = mybir.dt.float32
 BF16 = mybir.dt.bfloat16
@@ -16,8 +15,10 @@ MULT = mybir.AluOpType.mult
 
 T, S, K, K2, H, N = 2048, 1024, 1024, 512, 1024, 512
 P = 128
-HALF = 512
-C_ROW = 32
+PACK = 4
+WIDTH = 512
+HALVES = (slice(0, WIDTH // 2), slice(WIDTH // 2, WIDTH))
+TAB_PLANES = (4, 8)
 FLOPS = 2 * S * (K * H + K2 * H + H * N)
 
 
@@ -27,289 +28,269 @@ def tile_list_edge_gated_messages_kernel(
     nc = tc.nc
     with ExitStack() as ctx:
         keep = ctx.enter_context(tc.tile_pool(name="keep", bufs=1))
-        slots = ctx.enter_context(tc.tile_pool(name="slots", bufs=1))
+        reuse = ctx.enter_context(tc.tile_pool(name="reuse", bufs=1))
         psum = ctx.enter_context(tc.psum_pool(name="psum", bufs=1))
 
-        def slot(shape, dtype, tag, name):
-            return slots.tile(shape, dtype, tag=tag, name=name, align_bytes=64)
+        def buffer(shape, dtype, name, takes=None):
+            return reuse.tile(shape, dtype, tag=takes or name, name=name, align_bytes=64)
 
-        def bank(i, shape, name):
-            return psum.tile(shape, F32, tag=f"bank{i}", name=name)
+        def bank(index, name):
+            return psum.tile([P, WIDTH], F32, tag=f"bank{index}", name=name)
+
+        def edges(e):
+            return slice(e * WIDTH, (e + 1) * WIDTH)
+
+        def entries(e):
+            return slice(e * WIDTH // 16, (e + 1) * WIDTH // 16)
 
         list1 = keep.tile([P, S // 16], U16, name="list1")
         list2 = keep.tile([P, S // 16], U16, name="list2")
-        tab_sc = slot([P, T // 4], I32, "tab_sc", "tab_sc")
-        tab2_sc = keep.tile([P, T // 4], I32, name="tab2_sc")
-        wb_sc_raw = slot([P, H // 4], I32, "wb_sc_raw", "wb_sc_raw")
-        wb_raw = keep.tile([P, H // 2], I32, name="wb_raw")
-        b_rows = keep.tile([C_ROW, HALF], F32, name="b_rows")
-        bias_rows = keep.tile([P, HALF], F32, name="bias_rows")
-        bias = keep.tile([P, 4, C_ROW + 1], F32, name="bias")
-        identity = keep.tile([P, P], F32, name="identity")
-        warm_in = keep.tile([P, 1], F32, name="warm_in")
-        warm_out = keep.tile([P, 1], F32, name="warm_out")
-        picked = {a: keep.tile([P, S], U32, name=f"picked{a}", align_bytes=64) for a in range(3)}
-        picked_sc = keep.tile([P, S], U8, name="picked_sc", align_bytes=64)
-        picked2_sc = keep.tile([P, S], U8, name="picked2_sc", align_bytes=64)
-        wb_codes = keep.tile([P, H // 2], I32, name="wb_codes", align_bytes=64)
-        wb_sc = keep.tile([P, H // 4], I32, name="wb_sc", align_bytes=64)
-
-        def cols(jh):
-            return slice(0, S) if jh is None else slice(jh * HALF, (jh + 1) * HALF)
-
-        def lcols(jh):
-            return slice(cols(jh).start // 16, cols(jh).stop // 16)
+        tab_planes = keep.tile([P, T // 4], I32, name="tab_planes")
+        tab2_plane = keep.tile([P, T // 4], I32, name="tab2_plane")
+        wb_plane_raw = keep.tile([P, H // 4], I32, name="wb_plane_raw")
+        wb_words_raw = keep.tile([P, H // 2], I32, name="wb_words_raw")
+        wb_plane = keep.tile([P, H], U8, name="wb_plane", align_bytes=64)
+        wb_codes = keep.tile([P, H], U16, name="wb_codes", align_bytes=64)
+        b_sb = keep.tile([P, 2, 2 * PACK], F32, name="b_sb")
+        c_sb = keep.tile([P, PACK], F32, name="c_sb")
+        v_codes = [keep.tile([P, S], U32, name=f"v_codes{a}", align_bytes=64) for a in range(2)]
+        v_planes = keep.tile([P, S], U8, name="v_planes", align_bytes=64)
+        v2_codes = keep.tile([P, S], U32, name="v2_codes", align_bytes=64)
+        v2_plane = keep.tile([P, S], U8, name="v2_plane", align_bytes=64)
 
         def load_table(words, name):
-            tile = slot([P, T], I32, name, name)
+            tile = buffer([P, T], I32, name)
             nc.sync.dma_start(out=tile[:], in_=words.rearrange("p t i -> p (t i)").bitcast(I32))
             return tile
 
-        def load_wa(a, g):
-            tile = slot([P, 4, HALF], F32, f"wa{a}{g}", f"wa{a}{g}")
-            rows = wa[a * HALF : (a + 1) * HALF, g * HALF : (g + 1) * HALF]
-            nc.sync.dma_start(out=tile[:], in_=rows.rearrange("(p j) x -> p j x", j=4))
+        def load_weight(rows, name):
+            tile = buffer([P, PACK, WIDTH], F32, name)
+            nc.sync.dma_start(out=tile[:], in_=rows.rearrange("(p j) x -> p j x", j=PACK))
             return tile
 
-        def load_w2(g):
-            tile = slot([P, 4, HALF], F32, f"w2{g}", f"w2{g}")
-            rows = w2[g * HALF : (g + 1) * HALF, :].rearrange("(x t i) n -> t x i n", t=4, i=4)
-            for t in range(4):
-                nc.sync.dma_start(out=tile[:, t, :], in_=rows[t])
-            return tile
+        def load_wa(a, g):
+            return load_weight(wa[a * WIDTH : (a + 1) * WIDTH, g * WIDTH : (g + 1) * WIDTH], f"wa{a}{g}")
 
         def load_plane(tile, scales):
             rows = scales.bitcast(I32).rearrange("(q r) x -> r q x", r=4)
             for r in range(4):
                 nc.sync.dma_start(out=tile[r:P:32, :], in_=rows[r])
 
-        def load_tab_scales():
+        def load_tab_planes():
             for q in range(4):
+                first = 32 * q + TAB_PLANES[0]
                 nc.sync.dma_start(
-                    out=tab_sc[32 * q + 4 : 32 * q + 12, :], in_=tab_scales.bitcast(I32)[:, 4 * q : 4 * q + 4, :]
+                    out=tab_planes[first : first + 8, :], in_=tab_scales.bitcast(I32)[:, 4 * q : 4 * q + 4, :]
                 )
 
         def load_state(u):
             state = keep.tile([P, T], F32, name=f"state{u}")
-            nc.sync.dma_start(out=state[:], in_=gT[u * P : (u + 1) * P, :])
+            nc.sync.dma_start(out=state[:], in_=gT.rearrange("(p u) x -> u p x", u=PACK)[u])
             return state
 
-        def gather_words(dst, table, lst, jh):
-            nc.vector.tensor_copy(out=dst[:, cols(jh)], in_=table[:].bitcast(U32).indirect(lst[:, lcols(jh)]))
+        def gather_words(dst, table, offsets):
+            for e in range(2):
+                nc.vector.tensor_copy(out=dst[:, edges(e)], in_=table[:].bitcast(U32).indirect(offsets[:, entries(e)]))
 
-        def gather_scales(dst, src, lst):
-            nc.vector.tensor_copy(out=dst[:], in_=src[:].bitcast(U8).indirect(lst[:]))
+        def gather_plane(dst, plane, offsets):
+            nc.vector.tensor_copy(out=dst[:], in_=plane[:].bitcast(U8).indirect(offsets[:]))
 
-        def copy_on(engine, out, in_):
-            if engine is nc.scalar:
-                nc.scalar.copy(out=out, in_=in_)
-            else:
-                nc.vector.tensor_copy(out=out, in_=in_)
-
-        def cast_wa(raw, engines, tag, name):
-            grouped = slot([P, 4 * HALF], BF16, tag, name)
-            share = 4 // len(engines)
-            for s, engine in enumerate(engines):
-                ts = slice(share * s, share * (s + 1))
-                copy_on(
-                    engine,
-                    grouped[:].rearrange("p (t x i j) -> p t x j i", t=4, i=4, j=4)[:, ts],
-                    raw[:].rearrange("p j (x t i) -> p t x j i", t=4, i=4)[:, ts],
-                )
-            return grouped
-
-        def interleave_columns(grouped, raw, engine, columns):
-            copy_on(
-                engine,
-                grouped[:, 4 * columns.start : 4 * columns.stop].rearrange("p (x i j) -> p x j i", i=4, j=4),
-                raw[:, :, columns].rearrange("p j (x i) -> p x j i", i=4),
+        def sort_columns(dst, src):
+            nc.vector.tensor_copy(
+                out=dst.rearrange("p (g t m) -> p g t m", g=2, t=PACK),
+                in_=src.rearrange("p (g m t) -> p g t m", g=2, t=PACK),
             )
 
-        def interleave(raw, engine, tag, name):
-            grouped = slot([P, 4 * HALF], BF16, tag, name)
-            interleave_columns(grouped, raw, engine, slice(0, HALF))
+        def copy_on(engine, dst, src):
+            if engine is nc.scalar:
+                nc.scalar.copy(out=dst, in_=src)
+            else:
+                nc.vector.tensor_copy(out=dst, in_=src)
+
+        def cast_weight(raw, engines, name, takes=None):
+            grouped = buffer([P, PACK * WIDTH], BF16, name, takes)
+            for s, engine in enumerate(engines):
+                pair = slice(2 * s, 2 * s + 2)
+                copy_on(
+                    engine,
+                    grouped[:].rearrange("p (t m j) -> p m j t", t=PACK, j=PACK)[:, :, :, pair],
+                    raw[:].rearrange("p j (m t) -> p m j t", t=PACK)[:, :, :, pair],
+                )
             return grouped
 
-        def quantize(grouped, name, tag=None, parts=1):
-            codes = slot([P, HALF], U32, tag or name, name + "_codes")
-            scales = keep.tile([P, HALF], U8, name=name + "_sc", align_bytes=64)
-            share = HALF // parts
-            for s in range(parts):
-                m = slice(share * s, share * (s + 1))
-                nc.vector.quantize_mx(
-                    out=codes[:, m].bitcast(FP8X4), scales=scales[:, m], in_=grouped[:, 4 * m.start : 4 * m.stop]
-                )
-            return codes, scales
+        def interleave_columns(grouped, hs, engine, columns):
+            copy_on(
+                engine,
+                grouped[:, PACK * columns.start : PACK * columns.stop].rearrange("p (x i t) -> p x t i", i=4, t=PACK),
+                hs[:, :, columns].rearrange("p t (x i) -> p x t i", i=4),
+            )
 
-        acc = {}
+        def interleave(hs, name, takes):
+            grouped = buffer([P, PACK * WIDTH], BF16, name, takes)
+            interleave_columns(grouped, hs, nc.vector, slice(0, WIDTH))
+            return grouped
 
-        def open_banks(g, jh):
-            for t in range(4):
-                acc[g, jh, t] = bank(4 * jh + t, [P, HALF], f"a{g}{jh}{t}")
+        def mx_tiles(name, takes=None):
+            codes = buffer([P, WIDTH], U32, name, takes)
+            plane = keep.tile([P, WIDTH], U8, name=name + "_plane", align_bytes=64)
+            return codes, plane
 
-        def pass_wa(quantized, a, g, jh, start, stop):
-            codes, scales = quantized
-            for t in range(4):
+        def quantize_columns(operand, grouped, columns):
+            codes, plane = operand
+            nc.vector.quantize_mx(
+                out=codes[:, columns].bitcast(FP8X4),
+                scales=plane[:, columns],
+                in_=grouped[:, PACK * columns.start : PACK * columns.stop],
+            )
+
+        def quantize(grouped, name, takes=None):
+            operand = mx_tiles(name, takes)
+            quantize_columns(operand, grouped, slice(0, WIDTH))
+            return operand
+
+        def open_banks(g, e):
+            return [bank(PACK * e + t, f"a{g}{e}{t}") for t in range(PACK)]
+
+        def pass_wa(banks, operand, a, e, start=False, stop=False):
+            codes, plane = operand
+            for t in range(PACK):
                 m = slice(t * P, (t + 1) * P)
                 nc.tensor.matmul_mx(
-                    out=acc[g, jh, t][:],
+                    out=banks[t][:],
                     lhsT=codes[:, m].bitcast(FP8X4),
-                    lhsT_scale=scales[:, m],
-                    rhs=picked[a][:, cols(jh)].bitcast(FP8X4),
-                    rhs_scale=picked_sc[4 + 4 * a : P, cols(jh)],
+                    lhsT_scale=plane[:, m],
+                    rhs=v_codes[a][:, edges(e)].bitcast(FP8X4),
+                    rhs_scale=v_planes[TAB_PLANES[a] : P, edges(e)],
                     start=start,
                     stop=stop,
                 )
 
-        def pass_wb(g, jh, start, stop):
-            for t in range(4):
-                m = slice(g * HALF + t * P, g * HALF + (t + 1) * P)
-                m2 = slice(2 * m.start, 2 * m.stop)
+        def pass_wb(banks, g, e, start=False):
+            for t in range(PACK):
+                first = g * WIDTH + t * P
                 nc.tensor.matmul_mx(
-                    out=acc[g, jh, t][:],
-                    lhsT=wb_codes[:].bitcast(U8)[:, m2].bitcast(FP4X4),
-                    lhsT_scale=wb_sc[:].bitcast(U8)[:, m],
-                    rhs=picked[2][:, cols(jh)].bitcast(FP8X4),
-                    rhs_scale=picked2_sc[:, cols(jh)],
+                    out=banks[t][:],
+                    lhsT=wb_codes[:].bitcast(U8)[:, 2 * first : 2 * (first + P)].bitcast(FP4X4),
+                    lhsT_scale=wb_plane[:, first : first + P],
+                    rhs=v2_codes[:, edges(e)].bitcast(FP8X4),
+                    rhs_scale=v2_plane[:, edges(e)],
                     start=start,
-                    stop=stop,
+                    stop=False,
                 )
 
-        def relu(g, jh, tag):
-            hs = slot([P, 4, HALF], BF16, tag, f"hs{g}{jh}")
-            for t in range(4):
-                nc.scalar.activation(out=hs[:, t, :], in_=acc[g, jh, t][:], func=ACT.Relu, bias=bias[:, t, g : g + 1])
+        def relu(banks, g, name, takes):
+            hs = buffer([P, PACK, WIDTH], BF16, name, takes)
+            for t in range(PACK):
+                nc.scalar.activation(out=hs[:, t, :], in_=banks[t][:], func=ACT.Relu, bias=b_sb[:, g, t : t + 1])
             return hs
 
-        def gate(jh, u, w2_q, h_q):
-            z = bank(4 * jh + u, [P, HALF], f"z{jh}{u}")
+        def gate(e, u, w2_mx, h_mx):
+            z = bank(PACK * e + u, f"z{e}{u}")
             m = slice(u * P, (u + 1) * P)
             for g in range(2):
                 nc.tensor.matmul_mx(
                     out=z[:],
-                    lhsT=w2_q[g][0][:, m].bitcast(FP8X4),
-                    lhsT_scale=w2_q[g][1][:, m],
-                    rhs=h_q[g][0][:].bitcast(FP8X4),
-                    rhs_scale=h_q[g][1][:],
+                    lhsT=w2_mx[g][0][:, m].bitcast(FP8X4),
+                    lhsT_scale=w2_mx[g][1][:, m],
+                    rhs=h_mx[g][0][:].bitcast(FP8X4),
+                    rhs_scale=h_mx[g][1][:],
                     start=(g == 0),
                     stop=(g == 1),
                 )
-            sig = slot([P, HALF], F32, f"sig{jh}{u}", f"sig{jh}{u}")
-            nc.scalar.activation(out=sig[:], in_=z[:], func=ACT.Sigmoid, bias=bias[:, u, C_ROW : C_ROW + 1])
+            sig = keep.tile([P, WIDTH], F32, name=f"sig{e}{u}")
+            nc.scalar.activation(out=sig[:], in_=z[:], func=ACT.Sigmoid, bias=c_sb[:, u : u + 1])
             return sig
 
-        def message(jh, u, sig, tag=None):
-            res = slot([P, HALF], F32, tag or f"res{jh}{u}", f"res{jh}{u}")
-            nc.vector.tensor_tensor(res[:], states[u][:].indirect(list1[:, lcols(jh)]), sig[:], MULT)
-            nc.sync.dma_start(out=out[u * P : (u + 1) * P, cols(jh)], in_=res[:])
+        def message(e, u, sig, takes=None):
+            res = buffer([P, WIDTH], F32, f"res{e}{u}", takes)
+            nc.vector.tensor_tensor(res[:], states[u][:].indirect(list1[:, entries(e)]), sig[:], MULT)
+            nc.sync.dma_start(out=out.rearrange("(p u) x -> u p x", u=PACK)[u][:, edges(e)], in_=res[:])
 
-        nc.gpsimd.memset(tab2_sc[:], 0)
-        nc.gpsimd.memset(tab_sc[:], 0)
-        nc.gpsimd.memset(wb_sc_raw[:], 0)
-        nc.gpsimd.memset(b_rows[:], 0.0)
-        nc.gpsimd.memset(bias_rows[:], 0.0)
-        make_identity(nc, identity[:])
-        nc.vector.memset(warm_in[:], 0.0)
-        nc.scalar.activation(out=warm_out[:], in_=warm_in[:], func=ACT.Sigmoid)
-
+        for plane_tile in (tab2_plane, tab_planes, wb_plane_raw):
+            nc.gpsimd.memset(plane_tile[:], 0)
         nc.sync.dma_start(list2[:], offs2)
         nc.sync.dma_start(list1[:], offs)
-        load_plane(tab2_sc, tab2_scales[0])
-        load_tab_scales()
-        nc.sync.dma_start(out=wb_raw[:], in_=wb_words[0].bitcast(I32))
-        load_plane(wb_sc_raw, wb_scales[0])
+        load_plane(tab2_plane, tab2_scales[0])
+        load_tab_planes()
+        nc.sync.dma_start(out=wb_words_raw[:], in_=wb_words[0].bitcast(I32))
+        load_plane(wb_plane_raw, wb_scales[0])
         tab2 = load_table(tab2_words[0], "tab2")
         wa00 = load_wa(0, 0)
-        nc.sync.dma_start(out=b_rows[0:2, :], in_=b.rearrange("(g x) -> g x", g=2))
-        nc.sync.dma_start(out=bias_rows[C_ROW : C_ROW + 1, :], in_=c.rearrange("(g x) -> g x", g=1))
+        nc.sync.dma_start(out=b_sb[:, :, 0:PACK], in_=b.rearrange("(g p t) -> p g t", g=2, t=PACK))
+        nc.sync.dma_start(out=c_sb[:], in_=c.rearrange("(p u) -> p u", u=PACK))
         tab0 = load_table(tab_words[0], "tab0")
         wa10 = load_wa(1, 0)
         tab1 = load_table(tab_words[1], "tab1")
         wa01 = load_wa(0, 1)
         wa11 = load_wa(1, 1)
-        w20 = load_w2(0)
-        w21 = load_w2(1)
-        states = [load_state(u) for u in range(4)]
+        w20 = load_weight(w2[0:WIDTH, :], "w20")
+        w21 = load_weight(w2[WIDTH:H, :], "w21")
+        states = [load_state(u) for u in range(PACK)]
 
-        gather_scales(picked2_sc, tab2_sc, list2)
-        gather_scales(picked_sc, tab_sc, list1)
-        nc.vector.tensor_copy(
-            out=wb_codes[:].rearrange("p (g t x w) -> p g t x w", g=2, t=4, w=2),
-            in_=wb_raw[:].rearrange("p (g x t w) -> p g t x w", g=2, t=4, w=2),
-        )
-        nc.vector.tensor_copy(
-            out=wb_sc[:].rearrange("p (g t x) -> p g t x", g=2, t=4),
-            in_=wb_sc_raw[:].rearrange("p (g x t) -> p g t x", g=2, t=4),
-        )
-        for jh in range(2):
-            gather_words(picked[2], tab2, list2, jh)
-        g_wa00 = cast_wa(wa00, [nc.scalar, nc.vector], "ga", "g_wa00")
-        q_wa00 = quantize(g_wa00, "q_wa00")
+        gather_plane(v2_plane, tab2_plane, list2)
+        gather_plane(v_planes, tab_planes, list1)
+        sort_columns(wb_codes[:], wb_words_raw[:].bitcast(U16))
+        sort_columns(wb_plane[:], wb_plane_raw[:].bitcast(U8))
+        gather_words(v2_codes, tab2, list2)
+        wa00_bf = cast_weight(wa00, (nc.scalar, nc.vector), "wa00_bf")
+        wa00_mx = quantize(wa00_bf, "wa00_mx")
+        gather_words(v_codes[0], tab0, list1)
+        wa10_bf = cast_weight(wa10, (nc.scalar, nc.vector), "wa10_bf")
+        wa10_mx = quantize(wa10_bf, "wa10_mx")
+        gather_words(v_codes[1], tab1, list1)
+        banks00 = open_banks(0, 0)
+        pass_wb(banks00, 0, 0, start=True)
+        pass_wa(banks00, wa00_mx, 0, 0)
+        banks01 = open_banks(0, 1)
+        pass_wa(banks01, wa00_mx, 0, 1, start=True)
+        pass_wb(banks01, 0, 1)
+        pass_wa(banks00, wa10_mx, 1, 0, stop=True)
+        pass_wa(banks01, wa10_mx, 1, 1, stop=True)
+        hs00 = relu(banks00, 0, "hs00", takes="wa00_bf")
+        hs01 = relu(banks01, 0, "hs01", takes="wa10_bf")
 
-        nc.scalar.copy(
-            out=bias_rows[0:C_ROW, :].rearrange("p (t x i) -> p t x i", t=4, i=4),
-            in_=b_rows[:].rearrange("p (x t i) -> p t x i", t=4, i=4),
-        )
-        turned = bank(7, [P, 4, P], "turned")
-        for t in range(4):
-            nc.tensor.transpose(turned[:, t, :], bias_rows[:, t * P : (t + 1) * P], identity[:])
-        nc.scalar.copy(out=bias[:], in_=turned[:, :, 0 : C_ROW + 1])
+        wa01_bf = cast_weight(wa01, (nc.vector, nc.vector), "wa01_bf", takes="tab0")
+        wa01_mx = quantize(wa01_bf, "wa01_mx")
+        wa11_bf = cast_weight(wa11, (nc.vector, nc.vector), "wa11_bf", takes="tab2")
+        wa11_mx = mx_tiles("wa11_mx")
+        for columns in HALVES:
+            quantize_columns(wa11_mx, wa11_bf, columns)
+        h00_bf = interleave(hs00, "h00_bf", takes="wa11")
+        h00_mx = quantize(h00_bf, "h00_mx")
+        banks10 = open_banks(1, 0)
+        pass_wb(banks10, 1, 0, start=True)
+        pass_wa(banks10, wa01_mx, 0, 0)
+        pass_wa(banks10, wa11_mx, 1, 0, stop=True)
+        banks11 = open_banks(1, 1)
+        pass_wa(banks11, wa11_mx, 1, 1, start=True)
+        pass_wb(banks11, 1, 1)
+        pass_wa(banks11, wa01_mx, 0, 1, stop=True)
+        hs10 = relu(banks10, 1, "hs10", takes="wa01")
 
-        for jh in range(2):
-            gather_words(picked[0], tab0, list1, jh)
-        g_wa10 = cast_wa(wa10, [nc.scalar, nc.vector], "gb", "g_wa10")
-        q_wa10 = quantize(g_wa10, "q_wa10")
-        for jh in range(2):
-            gather_words(picked[1], tab1, list1, jh)
-        for jh in range(2):
-            open_banks(0, jh)
-            pass_wb(0, jh, True, False)
-        for jh in range(2):
-            pass_wa(q_wa00, 0, 0, jh, False, False)
-        for jh in range(2):
-            pass_wa(q_wa10, 1, 0, jh, False, True)
+        w21_bf = cast_weight(w21, (nc.scalar, nc.scalar), "w21_bf", takes="wa11_mx")
+        w20_bf = cast_weight(w20, (nc.vector, nc.vector), "w20_bf", takes="wa00_bf")
+        h01_bf = interleave(hs01, "h01_bf", takes="tab2")
+        h10_bf = interleave(hs10, "h10_bf", takes="w20")
+        w2_mx = (mx_tiles("w20_mx", takes="wa10_bf"), mx_tiles("w21_mx"))
+        quantize_columns(w2_mx[0], w20_bf, HALVES[0])
+        h10_mx = quantize(h10_bf, "h10_mx")
+        quantize_columns(w2_mx[1], w21_bf, HALVES[0])
+        quantize_columns(w2_mx[0], w20_bf, HALVES[1])
+        quantize_columns(w2_mx[1], w21_bf, HALVES[1])
+        h01_mx = quantize(h01_bf, "h01_mx", takes="w20")
 
-        hs00 = relu(0, 0, "ga")
-        hs01 = relu(0, 1, "gb")
-        g_wa01 = cast_wa(wa01, [nc.vector], "tab0", "g_wa01")
-        q_wa01 = quantize(g_wa01, "q_wa01")
-        g_wa11 = cast_wa(wa11, [nc.vector, nc.vector], "tab2", "g_wa11")
-        q_wa11 = quantize(g_wa11, "q_wa11", parts=2)
-        g_h00 = interleave(hs00, nc.vector, "wa11", "g_h00")
-        q_h00 = quantize(g_h00, "q_h00")
-        open_banks(1, 0)
-        pass_wb(1, 0, True, False)
-        pass_wa(q_wa01, 0, 1, 0, False, False)
-        pass_wa(q_wa11, 1, 1, 0, False, True)
-        open_banks(1, 1)
-        pass_wa(q_wa11, 1, 1, 1, True, False)
-        pass_wb(1, 1, False, False)
-        pass_wa(q_wa01, 0, 1, 1, False, True)
+        h0_mx = (h00_mx, h10_mx)
+        sigs = [gate(0, u, w2_mx, h0_mx) for u in range(2)]
+        hs11 = relu(banks11, 1, "hs11", takes="wa11_mx")
+        sigs.append(gate(0, 2, w2_mx, h0_mx))
+        h11_bf = buffer([P, PACK * WIDTH], BF16, "h11_bf")
+        interleave_columns(h11_bf, hs11, nc.scalar, HALVES[0])
+        sigs.append(gate(0, 3, w2_mx, h0_mx))
+        for u in range(PACK - 1):
+            message(0, u, sigs[u])
+        interleave_columns(h11_bf, hs11, nc.vector, HALVES[1])
+        h11_mx = quantize(h11_bf, "h11_mx")
+        message(0, PACK - 1, sigs[PACK - 1], takes="wa11_mx")
 
-        hs10 = relu(1, 0, "wa01")
-        g_w21 = interleave(w21, nc.scalar, "wa10", "g_w21")
-        g_w20 = interleave(w20, nc.vector, "wa00", "g_w20")
-        g_h10 = interleave(hs10, nc.vector, "w20", "g_h10")
-        q_w20 = quantize(g_w20, "q_w20")
-        q_h10 = quantize(g_h10, "q_h10")
-        q_w21 = quantize(g_w21, "q_w21")
-        g_h01 = interleave(hs01, nc.vector, "w20", "g_h01")
-        q_h01 = quantize(g_h01, "q_h01")
-        q_w2 = (q_w20, q_w21)
-        sigs = {(0, 0): gate(0, 0, q_w2, (q_h00, q_h10))}
-        hs11 = relu(1, 1, "w21")
-        g_h11 = slot([P, 4 * HALF], BF16, "g_h11", "g_h11")
-        for s in range(2):
-            interleave_columns(g_h11, hs11, nc.scalar, slice(s * HALF // 2, (s + 1) * HALF // 2))
-            sigs[0, s + 1] = gate(0, s + 1, q_w2, (q_h00, q_h10))
-        sigs[0, 3] = gate(0, 3, q_w2, (q_h00, q_h10))
-        message(0, 0, sigs[0, 0])
-        message(0, 1, sigs[0, 1])
-        q_h11 = quantize(g_h11, "q_h11")
-        message(0, 2, sigs[0, 2])
-        for u in range(4):
-            sigs[1, u] = gate(1, u, q_w2, (q_h01, q_h11))
-        for u in range(3):
-            message(1, u, sigs[1, u])
-        message(0, 3, sigs[0, 3], "sig11")
-        message(1, 3, sigs[1, 3])
+        for u in range(PACK):
+            message(1, u, gate(1, u, w2_mx, (h01_mx, h11_mx)))

@@ -208,42 +208,44 @@ def tile_list_edge_gated_messages_kernel(
 
         for plane_tile in (tab2_plane, tab_planes, wb_plane_raw):
             nc.gpsimd.memset(plane_tile[:], 0)
+        nc.sync.dma_start(out=wb_words_raw[:], in_=wb_words[0].bitcast(I32))
         nc.sync.dma_start(list2[:], offs2)
         nc.sync.dma_start(list1[:], offs)
         load_plane(tab2_plane, tab2_scales[0])
         load_tab_planes()
-        nc.sync.dma_start(out=wb_words_raw[:], in_=wb_words[0].bitcast(I32))
         load_plane(wb_plane_raw, wb_scales[0])
         tab2 = load_table(tab2_words[0], "tab2")
         wa00 = load_wa(0, 0)
+        tab0 = load_table(tab_words[0], "tab0")
+        tab1 = load_table(tab_words[1], "tab1")
         nc.sync.dma_start(out=b_sb[:, :, 0:PACK], in_=b.rearrange("(g p t) -> p g t", g=2, t=PACK))
         nc.sync.dma_start(out=c_sb[:], in_=c.rearrange("(p u) -> p u", u=PACK))
-        tab0 = load_table(tab_words[0], "tab0")
         wa10 = load_wa(1, 0)
-        tab1 = load_table(tab_words[1], "tab1")
         wa01 = load_wa(0, 1)
         wa11 = load_wa(1, 1)
         w20 = load_weight(w2[0:WIDTH, :], "w20")
         w21 = load_weight(w2[WIDTH:H, :], "w21")
         states = [load_state(u) for u in range(PACK)]
 
+        sort_columns(wb_codes[:], wb_words_raw[:].bitcast(U16))
         gather_plane(v2_plane, tab2_plane, list2)
         gather_plane(v_planes, tab_planes, list1)
-        sort_columns(wb_codes[:], wb_words_raw[:].bitcast(U16))
         sort_columns(wb_plane[:], wb_plane_raw[:].bitcast(U8))
         gather_words(v2_codes, tab2, list2)
-        wa00_bf = cast_weight(wa00, (nc.scalar, nc.vector), "wa00_bf")
+        wa00_bf = cast_weight(wa00, (nc.scalar, nc.scalar), "wa00_bf")
         wa00_mx = quantize(wa00_bf, "wa00_mx")
         gather_words(v_codes[0], tab0, list1)
-        wa10_bf = cast_weight(wa10, (nc.scalar, nc.vector), "wa10_bf")
-        wa10_mx = quantize(wa10_bf, "wa10_mx")
         gather_words(v_codes[1], tab1, list1)
+        wa10_bf = cast_weight(wa10, (nc.scalar, nc.vector), "wa10_bf")
+        wa10_mx = mx_tiles("wa10_mx")
+        for columns in HALVES:
+            quantize_columns(wa10_mx, wa10_bf, columns)
         banks00 = open_banks(0, 0)
         pass_wb(banks00, 0, 0, start=True)
-        pass_wa(banks00, wa00_mx, 0, 0)
         banks01 = open_banks(0, 1)
-        pass_wa(banks01, wa00_mx, 0, 1, start=True)
-        pass_wb(banks01, 0, 1)
+        pass_wb(banks01, 0, 1, start=True)
+        pass_wa(banks00, wa00_mx, 0, 0)
+        pass_wa(banks01, wa00_mx, 0, 1)
         pass_wa(banks00, wa10_mx, 1, 0, stop=True)
         pass_wa(banks01, wa10_mx, 1, 1, stop=True)
         hs00 = relu(banks00, 0, "hs00", takes="wa00_bf")

@@ -18,7 +18,8 @@ P = 128
 PACK = 4
 WIDTH = 512
 HALVES = (slice(0, WIDTH // 2), slice(WIDTH // 2, WIDTH))
-TAB_PLANES = (4, 8)
+V_PLANE = 4
+ROWS = 16
 FLOPS = 2 * S * (K * H + K2 * H + H * N)
 
 
@@ -45,52 +46,43 @@ def tile_list_edge_gated_messages_kernel(
 
         list1 = keep.tile([P, S // 16], U16, name="list1")
         list2 = keep.tile([P, S // 16], U16, name="list2")
-        tab_planes = keep.tile([P, T // 4], I32, name="tab_planes")
-        tab2_plane = keep.tile([P, T // 4], I32, name="tab2_plane")
-        wb_plane_raw = keep.tile([P, H // 4], I32, name="wb_plane_raw")
-        wb_words_raw = keep.tile([P, H // 2], I32, name="wb_words_raw")
-        wb_plane = keep.tile([P, H], U8, name="wb_plane", align_bytes=64)
+        tab_rows = buffer([P, T // 4], I32, "tab_rows")
+        tab2_rows = buffer([P, T // 4], I32, "tab2_rows")
+        wb_rows = keep.tile([P, H // 4], I32, name="wb_rows")
+        wb_words_raw = buffer([P, H // 2], I32, "wb_words_raw")
         wb_codes = keep.tile([P, H], U16, name="wb_codes", align_bytes=64)
         b_sb = keep.tile([P, 2, 2 * PACK], F32, name="b_sb")
         c_sb = keep.tile([P, PACK], F32, name="c_sb")
-        v_codes = [keep.tile([P, S], U32, name=f"v_codes{a}", align_bytes=64) for a in range(2)]
-        v_planes = keep.tile([P, S], U8, name="v_planes", align_bytes=64)
+        v_rows = buffer([P, S], U8, "v_rows")
+        v2_rows = keep.tile([P, S], U8, name="v2_rows", align_bytes=64)
+        pair_rows = keep.tile([P, S + H], U8, name="pair_rows", align_bytes=64)
+        v_planes = keep.tile([P, 2 * S // 4], I32, name="v_planes", align_bytes=64)
+        pair_planes = keep.tile([P, (S + H) // 4], I32, name="pair_planes", align_bytes=64)
+        v2_plane = pair_planes[:].bitcast(U8)[:, 0:S]
+        wb_plane = pair_planes[:].bitcast(U8)[:, S : S + H]
         v2_codes = keep.tile([P, S], U32, name="v2_codes", align_bytes=64)
-        v2_plane = keep.tile([P, S], U8, name="v2_plane", align_bytes=64)
+        v_codes = {}
 
-        def load_table(words, name):
-            tile = buffer([P, T], I32, name)
+        def load_table(words, name, takes=None):
+            tile = buffer([P, T], I32, name, takes)
             nc.sync.dma_start(out=tile[:], in_=words.rearrange("p t i -> p (t i)").bitcast(I32))
             return tile
 
-        def load_weight(rows, name):
-            tile = buffer([P, PACK, WIDTH], F32, name)
+        def load_weight(rows, name, takes=None):
+            tile = buffer([P, PACK, WIDTH], F32, name, takes)
             nc.sync.dma_start(out=tile[:], in_=rows.rearrange("(p j) x -> p j x", j=PACK))
             return tile
 
-        def load_wa(a, g):
-            return load_weight(wa[a * WIDTH : (a + 1) * WIDTH, g * WIDTH : (g + 1) * WIDTH], f"wa{a}{g}")
+        def load_wa(a, g, takes=None):
+            return load_weight(wa[a * WIDTH : (a + 1) * WIDTH, g * WIDTH : (g + 1) * WIDTH], f"wa{a}{g}", takes)
 
-        def load_plane(tile, scales):
-            rows = scales.bitcast(I32).rearrange("(q r) x -> r q x", r=4)
-            for r in range(4):
-                nc.sync.dma_start(out=tile[r:P:32, :], in_=rows[r])
-
-        def load_tab_planes():
-            for q in range(4):
-                first = 32 * q + TAB_PLANES[0]
-                nc.sync.dma_start(
-                    out=tab_planes[first : first + 8, :], in_=tab_scales.bitcast(I32)[:, 4 * q : 4 * q + 4, :]
-                )
-
-        def load_state(u):
-            state = keep.tile([P, T], F32, name=f"state{u}")
+        def load_state(u, takes):
+            state = buffer([P, T], F32, f"state{u}", takes)
             nc.sync.dma_start(out=state[:], in_=gT.rearrange("(p u) x -> u p x", u=PACK)[u])
             return state
 
-        def gather_words(dst, table, offsets):
-            for e in range(2):
-                nc.vector.tensor_copy(out=dst[:, edges(e)], in_=table[:].bitcast(U32).indirect(offsets[:, entries(e)]))
+        def gather_words(dst, table, offsets, e):
+            nc.vector.tensor_copy(out=dst, in_=table[:].bitcast(U32).indirect(offsets[:, entries(e)]))
 
         def gather_plane(dst, plane, offsets):
             nc.vector.tensor_copy(out=dst[:], in_=plane[:].bitcast(U8).indirect(offsets[:]))
@@ -127,7 +119,8 @@ def tile_list_edge_gated_messages_kernel(
 
         def interleave(hs, name, takes):
             grouped = buffer([P, PACK * WIDTH], BF16, name, takes)
-            interleave_columns(grouped, hs, nc.vector, slice(0, WIDTH))
+            for columns in HALVES:
+                interleave_columns(grouped, hs, nc.vector, columns)
             return grouped
 
         def mx_tiles(name, takes=None):
@@ -145,7 +138,8 @@ def tile_list_edge_gated_messages_kernel(
 
         def quantize(grouped, name, takes=None):
             operand = mx_tiles(name, takes)
-            quantize_columns(operand, grouped, slice(0, WIDTH))
+            for columns in HALVES:
+                quantize_columns(operand, grouped, columns)
             return operand
 
         def open_banks(g, e):
@@ -159,8 +153,8 @@ def tile_list_edge_gated_messages_kernel(
                     out=banks[t][:],
                     lhsT=codes[:, m].bitcast(FP8X4),
                     lhsT_scale=plane[:, m],
-                    rhs=v_codes[a][:, edges(e)].bitcast(FP8X4),
-                    rhs_scale=v_planes[TAB_PLANES[a] : P, edges(e)],
+                    rhs=v_codes[a, e].bitcast(FP8X4),
+                    rhs_scale=v_planes[:].bitcast(U8)[V_PLANE:P, a * S + e * WIDTH : a * S + (e + 1) * WIDTH],
                     start=start,
                     stop=stop,
                 )
@@ -178,11 +172,9 @@ def tile_list_edge_gated_messages_kernel(
                     stop=False,
                 )
 
-        def relu(banks, g, name, takes):
-            hs = buffer([P, PACK, WIDTH], BF16, name, takes)
+        def relu(banks, g, hs):
             for t in range(PACK):
                 nc.scalar.activation(out=hs[:, t, :], in_=banks[t][:], func=ACT.Relu, bias=b_sb[:, g, t : t + 1])
-            return hs
 
         def gate(e, u, w2_mx, h_mx):
             z = bank(PACK * e + u, f"z{e}{u}")
@@ -206,40 +198,63 @@ def tile_list_edge_gated_messages_kernel(
             nc.vector.tensor_tensor(res[:], states[u][:].indirect(list1[:, entries(e)]), sig[:], MULT)
             nc.sync.dma_start(out=out.rearrange("(p u) x -> u p x", u=PACK)[u][:, edges(e)], in_=res[:])
 
-        for plane_tile in (tab2_plane, tab_planes, wb_plane_raw):
-            nc.gpsimd.memset(plane_tile[:], 0)
-        nc.sync.dma_start(out=wb_words_raw[:], in_=wb_words[0].bitcast(I32))
+        nc.gpsimd.memset(tab2_rows[0 : P - ROWS, :], 0)
+        nc.gpsimd.memset(wb_rows[0 : P - ROWS, :], 0)
+        nc.gpsimd.memset(tab_rows[0 : P - 2 * ROWS, :], 0)
+        nc.gpsimd.memset(pair_planes[:], 0)
+        nc.gpsimd.memset(v_planes[:], 0)
+        warm = keep.tile([P, 2], F32, name="warm")
+        nc.vector.memset(warm[:, 0:1], 0.0)
+        nc.scalar.activation(out=warm[:, 1:2], in_=warm[:, 0:1], func=ACT.Sigmoid)
         nc.sync.dma_start(list2[:], offs2)
+        nc.sync.dma_start(out=tab2_rows[P - ROWS : P, :], in_=tab2_scales[0].bitcast(I32))
+        nc.sync.dma_start(out=wb_rows[P - ROWS : P, :], in_=wb_scales[0].bitcast(I32))
+        nc.sync.dma_start(out=wb_words_raw[:], in_=wb_words[0].bitcast(I32))
         nc.sync.dma_start(list1[:], offs)
-        load_plane(tab2_plane, tab2_scales[0])
-        load_tab_planes()
-        load_plane(wb_plane_raw, wb_scales[0])
+        nc.sync.dma_start(out=tab_rows[P - 2 * ROWS : P, :], in_=tab_scales.bitcast(I32).rearrange("a q x -> q a x"))
         tab2 = load_table(tab2_words[0], "tab2")
         wa00 = load_wa(0, 0)
-        tab0 = load_table(tab_words[0], "tab0")
-        tab1 = load_table(tab_words[1], "tab1")
         nc.sync.dma_start(out=b_sb[:, :, 0:PACK], in_=b.rearrange("(g p t) -> p g t", g=2, t=PACK))
         nc.sync.dma_start(out=c_sb[:], in_=c.rearrange("(p u) -> p u", u=PACK))
-        wa10 = load_wa(1, 0)
-        wa01 = load_wa(0, 1)
-        wa11 = load_wa(1, 1)
-        w20 = load_weight(w2[0:WIDTH, :], "w20")
-        w21 = load_weight(w2[WIDTH:H, :], "w21")
-        states = [load_state(u) for u in range(PACK)]
 
+        gather_plane(v2_rows, tab2_rows, list2)
+        tab0 = load_table(tab_words[0], "tab0", takes="tab2_rows")
+        sort_columns(pair_rows[:, S : S + H], wb_rows[:].bitcast(U8))
+        nc.vector.tensor_copy(out=pair_rows[:, 0:S].bitcast(I32), in_=v2_rows[:].bitcast(I32))
+        for r in range(4):
+            nc.sync.dma_start(out=pair_planes[r:P:32, :], in_=pair_rows[:].bitcast(I32)[P - ROWS + r : P : 4, :])
         sort_columns(wb_codes[:], wb_words_raw[:].bitcast(U16))
-        gather_plane(v2_plane, tab2_plane, list2)
-        gather_plane(v_planes, tab_planes, list1)
-        sort_columns(wb_plane[:], wb_plane_raw[:].bitcast(U8))
-        gather_words(v2_codes, tab2, list2)
+        wa10 = load_wa(1, 0, takes="wb_words_raw")
+        gather_plane(v_rows, tab_rows, list1)
+        for q in range(4):
+            first = P - 2 * ROWS + 8 * q
+            nc.sync.dma_start(
+                out=v_planes[32 * q + V_PLANE : 32 * q + V_PLANE + 4, :], in_=v_rows[:].bitcast(I32)[first : first + 8, :]
+            )
+        tab1 = load_table(tab_words[1], "tab1", takes="tab_rows")
+
+        for e in range(2):
+            gather_words(v2_codes[:, edges(e)], tab2, list2, e)
+        wa01 = load_wa(0, 1, takes="tab2")
         wa00_bf = cast_weight(wa00, (nc.scalar, nc.scalar), "wa00_bf")
         wa00_mx = quantize(wa00_bf, "wa00_mx")
-        gather_words(v_codes[0], tab0, list1)
-        gather_words(v_codes[1], tab1, list1)
-        wa10_bf = cast_weight(wa10, (nc.scalar, nc.vector), "wa10_bf")
-        wa10_mx = mx_tiles("wa10_mx")
-        for columns in HALVES:
-            quantize_columns(wa10_mx, wa10_bf, columns)
+        wa11 = load_wa(1, 1, takes="wa00_bf")
+        v0_codes = buffer([P, S], U32, "v0_codes", takes="wa00")
+        for e in range(2):
+            v_codes[0, e] = v0_codes[:, edges(e)]
+            gather_words(v_codes[0, e], tab0, list1, e)
+        w20 = load_weight(w2[0:WIDTH, :], "w20", takes="tab2_rows")
+        wa10_bf = cast_weight(wa10, (nc.scalar, nc.scalar), "wa10_bf")
+        v10_codes = buffer([P, WIDTH], U32, "v10_codes")
+        v_codes[1, 0] = v10_codes[:]
+        gather_words(v_codes[1, 0], tab1, list1, 0)
+        wa10_mx = quantize(wa10_bf, "wa10_mx")
+        w21 = load_weight(w2[WIDTH:H, :], "w21", takes="wa10_bf")
+        v11_codes = buffer([P, WIDTH], U32, "v11_codes", takes="wb_words_raw")
+        v_codes[1, 1] = v11_codes[:]
+        gather_words(v_codes[1, 1], tab1, list1, 1)
+        states = [load_state(0, takes="tab_rows")]
+        wa01_bf = cast_weight(wa01, (nc.scalar, nc.scalar), "wa01_bf")
         banks00 = open_banks(0, 0)
         pass_wb(banks00, 0, 0, start=True)
         banks01 = open_banks(0, 1)
@@ -248,17 +263,16 @@ def tile_list_edge_gated_messages_kernel(
         pass_wa(banks01, wa00_mx, 0, 1)
         pass_wa(banks00, wa10_mx, 1, 0, stop=True)
         pass_wa(banks01, wa10_mx, 1, 1, stop=True)
-        hs00 = relu(banks00, 0, "hs00", takes="wa00_bf")
-        hs01 = relu(banks01, 0, "hs01", takes="wa10_bf")
+        hs0 = buffer([P, 2 * PACK, WIDTH], BF16, "hs0", takes="tab2")
+        hs00, hs01 = hs0[:, 0:PACK, :], hs0[:, PACK : 2 * PACK, :]
+        relu(banks00, 0, hs00)
+        relu(banks01, 0, hs01)
 
-        wa01_bf = cast_weight(wa01, (nc.vector, nc.vector), "wa01_bf", takes="tab0")
+        wa11_bf = cast_weight(wa11, (nc.vector, nc.vector), "wa11_bf")
         wa01_mx = quantize(wa01_bf, "wa01_mx")
-        wa11_bf = cast_weight(wa11, (nc.vector, nc.vector), "wa11_bf", takes="tab2")
-        wa11_mx = mx_tiles("wa11_mx")
-        for columns in HALVES:
-            quantize_columns(wa11_mx, wa11_bf, columns)
-        h00_bf = interleave(hs00, "h00_bf", takes="wa11")
-        h00_mx = quantize(h00_bf, "h00_mx")
+        states.append(load_state(1, takes="wa01_bf"))
+        wa11_mx = quantize(wa11_bf, "wa11_mx")
+        states.append(load_state(2, takes="wa11_bf"))
         banks10 = open_banks(1, 0)
         pass_wb(banks10, 1, 0, start=True)
         pass_wa(banks10, wa01_mx, 0, 0)
@@ -267,32 +281,36 @@ def tile_list_edge_gated_messages_kernel(
         pass_wa(banks11, wa11_mx, 1, 1, start=True)
         pass_wb(banks11, 1, 1)
         pass_wa(banks11, wa01_mx, 0, 1, stop=True)
-        hs10 = relu(banks10, 1, "hs10", takes="wa01")
+        hs10 = buffer([P, PACK, WIDTH], BF16, "hs10")
+        relu(banks10, 1, hs10)
+        hs11 = buffer([P, PACK, WIDTH], BF16, "hs11")
+        relu(banks11, 1, hs11)
 
-        w21_bf = cast_weight(w21, (nc.scalar, nc.scalar), "w21_bf", takes="wa11_mx")
-        w20_bf = cast_weight(w20, (nc.vector, nc.vector), "w20_bf", takes="wa00_bf")
-        h01_bf = interleave(hs01, "h01_bf", takes="tab2")
-        h10_bf = interleave(hs10, "h10_bf", takes="w20")
-        w2_mx = (mx_tiles("w20_mx", takes="wa10_bf"), mx_tiles("w21_mx"))
-        quantize_columns(w2_mx[0], w20_bf, HALVES[0])
-        h10_mx = quantize(h10_bf, "h10_mx")
+        w20_bf = cast_weight(w20, (nc.vector, nc.vector), "w20_bf")
+        states.append(load_state(3, takes="tab2_rows"))
+        h00_bf = interleave(hs00, "h00_bf", takes="wa00_bf")
+        w20_mx = quantize(w20_bf, "w20_mx")
+        h00_mx = quantize(h00_bf, "h00_mx")
+        w21_bf = cast_weight(w21, (nc.vector, nc.vector), "w21_bf")
+        w2_mx = (w20_mx, mx_tiles("w21_mx"))
         quantize_columns(w2_mx[1], w21_bf, HALVES[0])
-        quantize_columns(w2_mx[0], w20_bf, HALVES[1])
+        h10_bf = interleave(hs10, "h10_bf", takes=None)
+        h10_mx = quantize(h10_bf, "h10_mx")
         quantize_columns(w2_mx[1], w21_bf, HALVES[1])
-        h01_mx = quantize(h01_bf, "h01_mx", takes="w20")
+        h01_bf = interleave(hs01, "h01_bf", takes="hs10")
+        h01_mx = quantize(h01_bf, "h01_mx")
 
         h0_mx = (h00_mx, h10_mx)
         sigs = [gate(0, u, w2_mx, h0_mx) for u in range(2)]
-        hs11 = relu(banks11, 1, "hs11", takes="wa11_mx")
-        sigs.append(gate(0, 2, w2_mx, h0_mx))
-        h11_bf = buffer([P, PACK * WIDTH], BF16, "h11_bf")
+        h11_bf = buffer([P, PACK * WIDTH], BF16, "h11_bf", takes="hs10")
         interleave_columns(h11_bf, hs11, nc.scalar, HALVES[0])
+        sigs.append(gate(0, 2, w2_mx, h0_mx))
+        interleave_columns(h11_bf, hs11, nc.scalar, HALVES[1])
         sigs.append(gate(0, 3, w2_mx, h0_mx))
         for u in range(PACK - 1):
             message(0, u, sigs[u])
-        interleave_columns(h11_bf, hs11, nc.vector, HALVES[1])
         h11_mx = quantize(h11_bf, "h11_mx")
-        message(0, PACK - 1, sigs[PACK - 1], takes="wa11_mx")
+        message(0, PACK - 1, sigs[PACK - 1])
 
         for u in range(PACK):
             message(1, u, gate(1, u, w2_mx, (h01_mx, h11_mx)))

@@ -52,7 +52,6 @@ def tile_list_edge_gated_messages_kernel(
         wb_words_raw = buffer([P, H // 2], I32, "wb_words_raw")
         wb_codes = keep.tile([P, H], U16, name="wb_codes", align_bytes=64)
         b_sb = keep.tile([P, 2, 2 * PACK], F32, name="b_sb")
-        c_sb = keep.tile([P, PACK], F32, name="c_sb")
         v_rows = buffer([P, S], U8, "v_rows")
         v2_rows = keep.tile([P, S], U8, name="v2_rows", align_bytes=64)
         pair_rows = keep.tile([P, S + H], U8, name="pair_rows", align_bytes=64)
@@ -172,8 +171,8 @@ def tile_list_edge_gated_messages_kernel(
                     stop=False,
                 )
 
-        def relu(banks, g, hs):
-            for t in range(PACK):
+        def relu(banks, g, hs, slots=range(PACK)):
+            for t in slots:
                 nc.scalar.activation(out=hs[:, t, :], in_=banks[t][:], func=ACT.Relu, bias=b_sb[:, g, t : t + 1])
 
         def gate(e, u, w2_mx, h_mx):
@@ -215,7 +214,6 @@ def tile_list_edge_gated_messages_kernel(
         tab2 = load_table(tab2_words[0], "tab2")
         wa00 = load_wa(0, 0)
         nc.sync.dma_start(out=b_sb[:, :, 0:PACK], in_=b.rearrange("(g p t) -> p g t", g=2, t=PACK))
-        nc.sync.dma_start(out=c_sb[:], in_=c.rearrange("(p u) -> p u", u=PACK))
 
         gather_plane(v2_rows, tab2_rows, list2)
         tab0 = load_table(tab_words[0], "tab0", takes="tab2_rows")
@@ -226,7 +224,7 @@ def tile_list_edge_gated_messages_kernel(
         sort_columns(wb_codes[:], wb_words_raw[:].bitcast(U16))
         wa10 = load_wa(1, 0, takes="wb_words_raw")
         gather_plane(v_rows, tab_rows, list1)
-        for q in range(4):
+        for q in (0, 2, 1, 3):
             first = P - 2 * ROWS + 8 * q
             nc.sync.dma_start(
                 out=v_planes[32 * q + V_PLANE : 32 * q + V_PLANE + 4, :], in_=v_rows[:].bitcast(I32)[first : first + 8, :]
@@ -244,17 +242,19 @@ def tile_list_edge_gated_messages_kernel(
             v_codes[0, e] = v0_codes[:, edges(e)]
             gather_words(v_codes[0, e], tab0, list1, e)
         w20 = load_weight(w2[0:WIDTH, :], "w20", takes="tab2_rows")
-        wa10_bf = cast_weight(wa10, (nc.scalar, nc.scalar), "wa10_bf")
-        v10_codes = buffer([P, WIDTH], U32, "v10_codes")
-        v_codes[1, 0] = v10_codes[:]
-        gather_words(v_codes[1, 0], tab1, list1, 0)
+        wa10_bf = cast_weight(wa10, (nc.scalar, nc.vector), "wa10_bf")
         wa10_mx = quantize(wa10_bf, "wa10_mx")
         w21 = load_weight(w2[WIDTH:H, :], "w21", takes="wa10_bf")
-        v11_codes = buffer([P, WIDTH], U32, "v11_codes", takes="wb_words_raw")
-        v_codes[1, 1] = v11_codes[:]
-        gather_words(v_codes[1, 1], tab1, list1, 1)
-        states = [load_state(0, takes="tab_rows")]
-        wa01_bf = cast_weight(wa01, (nc.scalar, nc.scalar), "wa01_bf")
+        v1_codes = buffer([P, S], U32, "v1_codes")
+        for e in range(2):
+            v_codes[1, e] = v1_codes[:, edges(e)]
+            gather_words(v_codes[1, e], tab1, list1, e)
+        c_sb = buffer([P, PACK], F32, "c_sb", takes="tab_rows")
+        nc.sync.dma_start(out=c_sb[:], in_=c.rearrange("(p u) -> p u", u=PACK))
+        wa01_bf = cast_weight(wa01, (nc.vector, nc.vector), "wa01_bf")
+        states = [load_state(0, takes="tab2")]
+        wa01_mx = quantize(wa01_bf, "wa01_mx")
+        states.append(load_state(1, takes="wa01_bf"))
         banks00 = open_banks(0, 0)
         pass_wb(banks00, 0, 0, start=True)
         banks01 = open_banks(0, 1)
@@ -263,14 +263,12 @@ def tile_list_edge_gated_messages_kernel(
         pass_wa(banks01, wa00_mx, 0, 1)
         pass_wa(banks00, wa10_mx, 1, 0, stop=True)
         pass_wa(banks01, wa10_mx, 1, 1, stop=True)
-        hs0 = buffer([P, 2 * PACK, WIDTH], BF16, "hs0", takes="tab2")
+        hs0 = buffer([P, 2 * PACK, WIDTH], BF16, "hs0")
         hs00, hs01 = hs0[:, 0:PACK, :], hs0[:, PACK : 2 * PACK, :]
         relu(banks00, 0, hs00)
         relu(banks01, 0, hs01)
 
         wa11_bf = cast_weight(wa11, (nc.vector, nc.vector), "wa11_bf")
-        wa01_mx = quantize(wa01_bf, "wa01_mx")
-        states.append(load_state(1, takes="wa01_bf"))
         wa11_mx = quantize(wa11_bf, "wa11_mx")
         states.append(load_state(2, takes="wa11_bf"))
         banks10 = open_banks(1, 0)
@@ -283,34 +281,35 @@ def tile_list_edge_gated_messages_kernel(
         pass_wa(banks11, wa01_mx, 0, 1, stop=True)
         hs10 = buffer([P, PACK, WIDTH], BF16, "hs10")
         relu(banks10, 1, hs10)
-        hs11 = buffer([P, PACK, WIDTH], BF16, "hs11")
-        relu(banks11, 1, hs11)
+        w21_bf = cast_weight(w21, (nc.scalar, nc.scalar), "w21_bf", takes="wa11_mx")
+        hs11 = buffer([P, PACK, WIDTH], BF16, "hs11", takes="wa10_bf")
+        relu(banks11, 1, hs11, range(2))
 
+        h00_bf = interleave(hs00, "h00_bf", takes="wa00_bf")
         w20_bf = cast_weight(w20, (nc.vector, nc.vector), "w20_bf")
         states.append(load_state(3, takes="tab2_rows"))
-        h00_bf = interleave(hs00, "h00_bf", takes="wa00_bf")
-        w20_mx = quantize(w20_bf, "w20_mx")
         h00_mx = quantize(h00_bf, "h00_mx")
-        w21_bf = cast_weight(w21, (nc.vector, nc.vector), "w21_bf")
-        w2_mx = (w20_mx, mx_tiles("w21_mx"))
-        quantize_columns(w2_mx[1], w21_bf, HALVES[0])
+        w2_mx = (quantize(w20_bf, "w20_mx"), mx_tiles("w21_mx"))
         h10_bf = interleave(hs10, "h10_bf", takes=None)
         h10_mx = quantize(h10_bf, "h10_mx")
-        quantize_columns(w2_mx[1], w21_bf, HALVES[1])
+        quantize_columns(w2_mx[1], w21_bf, HALVES[0])
         h01_bf = interleave(hs01, "h01_bf", takes="hs10")
+        quantize_columns(w2_mx[1], w21_bf, HALVES[1])
         h01_mx = quantize(h01_bf, "h01_mx")
 
         h0_mx = (h00_mx, h10_mx)
-        sigs = [gate(0, u, w2_mx, h0_mx) for u in range(2)]
+        sigs = [gate(0, 0, w2_mx, h0_mx)]
+        relu(banks11, 1, hs11, range(2, PACK))
+        sigs.append(gate(0, 1, w2_mx, h0_mx))
         h11_bf = buffer([P, PACK * WIDTH], BF16, "h11_bf", takes="hs10")
         interleave_columns(h11_bf, hs11, nc.scalar, HALVES[0])
-        sigs.append(gate(0, 2, w2_mx, h0_mx))
-        interleave_columns(h11_bf, hs11, nc.scalar, HALVES[1])
-        sigs.append(gate(0, 3, w2_mx, h0_mx))
-        for u in range(PACK - 1):
+        sigs.extend(gate(0, u, w2_mx, h0_mx) for u in range(2, PACK))
+        for u in range(2):
             message(0, u, sigs[u])
+        interleave_columns(h11_bf, hs11, nc.vector, HALVES[1])
         h11_mx = quantize(h11_bf, "h11_mx")
-        message(0, PACK - 1, sigs[PACK - 1])
+        for u in range(2, PACK):
+            message(0, u, sigs[u])
 
         for u in range(PACK):
             message(1, u, gate(1, u, w2_mx, (h01_mx, h11_mx)))

@@ -18,6 +18,7 @@ P = 128
 PACK = 4
 WIDTH = 512
 HALVES = (slice(0, WIDTH // 2), slice(WIDTH // 2, WIDTH))
+WHOLE = (slice(0, WIDTH),)
 V_PLANE = 4
 ROWS = 16
 FLOPS = 2 * S * (K * H + K2 * H + H * N)
@@ -51,7 +52,6 @@ def tile_list_edge_gated_messages_kernel(
         wb_rows = keep.tile([P, H // 4], I32, name="wb_rows")
         wb_words_raw = buffer([P, H // 2], I32, "wb_words_raw")
         wb_codes = keep.tile([P, H], U16, name="wb_codes", align_bytes=64)
-        b_sb = keep.tile([P, 2, 2 * PACK], F32, name="b_sb")
         v_rows = buffer([P, S], U8, "v_rows")
         v2_rows = keep.tile([P, S], U8, name="v2_rows", align_bytes=64)
         pair_rows = keep.tile([P, S + H], U8, name="pair_rows", align_bytes=64)
@@ -135,9 +135,9 @@ def tile_list_edge_gated_messages_kernel(
                 in_=grouped[:, PACK * columns.start : PACK * columns.stop],
             )
 
-        def quantize(grouped, name, takes=None):
+        def quantize(grouped, name, takes=None, parts=HALVES):
             operand = mx_tiles(name, takes)
-            for columns in HALVES:
+            for columns in parts:
                 quantize_columns(operand, grouped, columns)
             return operand
 
@@ -175,8 +175,8 @@ def tile_list_edge_gated_messages_kernel(
             for t in slots:
                 nc.scalar.activation(out=hs[:, t, :], in_=banks[t][:], func=ACT.Relu, bias=b_sb[:, g, t : t + 1])
 
-        def gate(e, u, w2_mx, h_mx):
-            z = bank(PACK * e + u, f"z{e}{u}")
+        def gate(e, u, w2_mx, h_mx, index=None):
+            z = bank(PACK * e + u if index is None else index, f"z{e}{u}")
             m = slice(u * P, (u + 1) * P)
             for g in range(2):
                 nc.tensor.matmul_mx(
@@ -213,7 +213,6 @@ def tile_list_edge_gated_messages_kernel(
         nc.sync.dma_start(out=tab_rows[P - 2 * ROWS : P, :], in_=tab_scales.bitcast(I32).rearrange("a q x -> q a x"))
         tab2 = load_table(tab2_words[0], "tab2")
         wa00 = load_wa(0, 0)
-        nc.sync.dma_start(out=b_sb[:, :, 0:PACK], in_=b.rearrange("(g p t) -> p g t", g=2, t=PACK))
 
         gather_plane(v2_rows, tab2_rows, list2)
         tab0 = load_table(tab_words[0], "tab0", takes="tab2_rows")
@@ -231,11 +230,14 @@ def tile_list_edge_gated_messages_kernel(
             )
         tab1 = load_table(tab_words[1], "tab1", takes="tab_rows")
 
+        b_sb = buffer([P, 2, 2 * PACK], F32, "b_sb", takes="v_rows")
+        nc.sync.dma_start(out=b_sb[:, :, 0:PACK], in_=b.rearrange("(g p t) -> p g t", g=2, t=PACK))
+
         for e in range(2):
             gather_words(v2_codes[:, edges(e)], tab2, list2, e)
         wa01 = load_wa(0, 1, takes="tab2")
         wa00_bf = cast_weight(wa00, (nc.scalar, nc.scalar), "wa00_bf")
-        wa00_mx = quantize(wa00_bf, "wa00_mx")
+        wa00_mx = quantize(wa00_bf, "wa00_mx", parts=WHOLE)
         wa11 = load_wa(1, 1, takes="wa00_bf")
         v0_codes = buffer([P, S], U32, "v0_codes", takes="wa00")
         for e in range(2):
@@ -288,14 +290,14 @@ def tile_list_edge_gated_messages_kernel(
         h00_bf = interleave(hs00, "h00_bf", takes="wa00_bf")
         w20_bf = cast_weight(w20, (nc.vector, nc.vector), "w20_bf")
         states.append(load_state(3, takes="tab2_rows"))
-        h00_mx = quantize(h00_bf, "h00_mx")
-        w2_mx = (quantize(w20_bf, "w20_mx"), mx_tiles("w21_mx"))
+        h00_mx = quantize(h00_bf, "h00_mx", parts=WHOLE)
+        w2_mx = (quantize(w20_bf, "w20_mx", parts=WHOLE), mx_tiles("w21_mx"))
         h10_bf = interleave(hs10, "h10_bf", takes=None)
         h10_mx = quantize(h10_bf, "h10_mx")
         quantize_columns(w2_mx[1], w21_bf, HALVES[0])
         h01_bf = interleave(hs01, "h01_bf", takes="hs10")
         quantize_columns(w2_mx[1], w21_bf, HALVES[1])
-        h01_mx = quantize(h01_bf, "h01_mx")
+        h01_mx = quantize(h01_bf, "h01_mx", parts=WHOLE)
 
         h0_mx = (h00_mx, h10_mx)
         sigs = [gate(0, 0, w2_mx, h0_mx)]
@@ -303,13 +305,15 @@ def tile_list_edge_gated_messages_kernel(
         sigs.append(gate(0, 1, w2_mx, h0_mx))
         h11_bf = buffer([P, PACK * WIDTH], BF16, "h11_bf", takes="hs10")
         interleave_columns(h11_bf, hs11, nc.scalar, HALVES[0])
-        sigs.extend(gate(0, u, w2_mx, h0_mx) for u in range(2, PACK))
+        sigs.append(gate(0, 2, w2_mx, h0_mx))
         for u in range(2):
             message(0, u, sigs[u])
         interleave_columns(h11_bf, hs11, nc.vector, HALVES[1])
         h11_mx = quantize(h11_bf, "h11_mx")
+        message(0, 2, sigs[2])
+        h1_mx = (h01_mx, h11_mx)
+        for u in range(2):
+            message(1, u, gate(1, u, w2_mx, h1_mx))
+        message(0, 3, gate(0, 3, w2_mx, h0_mx, index=PACK + 1))
         for u in range(2, PACK):
-            message(0, u, sigs[u])
-
-        for u in range(PACK):
-            message(1, u, gate(1, u, w2_mx, (h01_mx, h11_mx)))
+            message(1, u, gate(1, u, w2_mx, h1_mx))

@@ -21,6 +21,7 @@ HALVES = (slice(0, WIDTH // 2), slice(WIDTH // 2, WIDTH))
 WHOLE = (slice(0, WIDTH),)
 V_PLANE = 4
 ROWS = 16
+KIB = 1024
 FLOPS = 2 * S * (K * H + K2 * H + H * N)
 
 
@@ -30,11 +31,13 @@ def tile_list_edge_gated_messages_kernel(
     nc = tc.nc
     with ExitStack() as ctx:
         keep = ctx.enter_context(tc.tile_pool(name="keep", bufs=1))
-        reuse = ctx.enter_context(tc.tile_pool(name="reuse", bufs=1))
+        arena = ctx.enter_context(tc.tile_pool(name="arena", bufs=1))
         psum = ctx.enter_context(tc.psum_pool(name="psum", bufs=1))
 
-        def buffer(shape, dtype, name, takes=None):
-            return reuse.tile(shape, dtype, tag=takes or name, name=name, align_bytes=64)
+        def place(shape, dtype, name, at=None):
+            if at is None:
+                return keep.tile(shape, dtype, name=name, align_bytes=64)
+            return arena.tile(shape, dtype, name=name, align_bytes=64, offset=at)
 
         def bank(index, name):
             return psum.tile([P, WIDTH], F32, tag=f"bank{index}", name=name)
@@ -45,38 +48,50 @@ def tile_list_edge_gated_messages_kernel(
         def entries(e):
             return slice(e * WIDTH // 16, (e + 1) * WIDTH // 16)
 
+        AT_WA01, AT_TAB2, AT_WA11 = 0, 4 * KIB, 8 * KIB
+        AT_W20, AT_TAB0, AT_W21 = 16 * KIB, 20 * KIB, 24 * KIB
+        AT_B, AT_TAB1 = 32 * KIB, 33 * KIB
+        AT_WA10 = 41 * KIB
+        AT_WA10_BF = 49 * KIB
+        AT_HS10 = 53 * KIB
+        AT_WA11_MX = 57 * KIB
+        AT_WA00 = 61 * KIB
+        AT_WA11_BF = 69 * KIB
+        AT_SIG02 = 77 * KIB
+        AT_RES10, AT_SIG03, AT_RES11 = 79 * KIB, 80 * KIB, 81 * KIB
+
         list1 = keep.tile([P, S // 16], U16, name="list1")
         list2 = keep.tile([P, S // 16], U16, name="list2")
-        tab_rows = buffer([P, T // 4], I32, "tab_rows")
-        tab2_rows = buffer([P, T // 4], I32, "tab2_rows")
-        wb_rows = keep.tile([P, H // 4], I32, name="wb_rows")
-        wb_words_raw = buffer([P, H // 2], I32, "wb_words_raw")
-        wb_codes = keep.tile([P, H], U16, name="wb_codes", align_bytes=64)
-        v_rows = buffer([P, S], U8, "v_rows")
-        v2_rows = keep.tile([P, S], U8, name="v2_rows", align_bytes=64)
-        pair_rows = keep.tile([P, S + H], U8, name="pair_rows", align_bytes=64)
-        v_planes = keep.tile([P, 2 * S // 4], I32, name="v_planes", align_bytes=64)
-        pair_planes = keep.tile([P, (S + H) // 4], I32, name="pair_planes", align_bytes=64)
+        tab_rows = place([P, T // 4], I32, "tab_rows", AT_B)
+        tab2_rows = place([P, T // 4], I32, "tab2_rows", AT_TAB0)
+        wb_rows = place([P, H // 4], I32, "wb_rows")
+        wb_words_raw = place([P, H // 2], I32, "wb_words_raw")
+        wb_codes = place([P, H], U16, "wb_codes")
+        v_rows = place([P, S], U8, "v_rows")
+        v2_rows = place([P, S], U8, "v2_rows", AT_WA10)
+        pair_rows = place([P, S + H], U8, "pair_rows")
+        v_planes = place([P, 2 * S // 4], I32, "v_planes")
+        pair_planes = place([P, (S + H) // 4], I32, "pair_planes")
         v2_plane = pair_planes[:].bitcast(U8)[:, 0:S]
         wb_plane = pair_planes[:].bitcast(U8)[:, S : S + H]
-        v2_codes = keep.tile([P, S], U32, name="v2_codes", align_bytes=64)
+        v2_codes = place([P, S], U32, "v2_codes")
         v_codes = {}
 
-        def load_table(words, name, takes=None):
-            tile = buffer([P, T], I32, name, takes)
+        def load_table(words, name, at):
+            tile = place([P, T], I32, name, at)
             nc.sync.dma_start(out=tile[:], in_=words.rearrange("p t i -> p (t i)").bitcast(I32))
             return tile
 
-        def load_weight(rows, name, takes=None):
-            tile = buffer([P, PACK, WIDTH], F32, name, takes)
+        def load_weight(rows, name, at):
+            tile = place([P, PACK, WIDTH], F32, name, at)
             nc.sync.dma_start(out=tile[:], in_=rows.rearrange("(p j) x -> p j x", j=PACK))
             return tile
 
-        def load_wa(a, g, takes=None):
-            return load_weight(wa[a * WIDTH : (a + 1) * WIDTH, g * WIDTH : (g + 1) * WIDTH], f"wa{a}{g}", takes)
+        def load_wa(a, g, at):
+            return load_weight(wa[a * WIDTH : (a + 1) * WIDTH, g * WIDTH : (g + 1) * WIDTH], f"wa{a}{g}", at)
 
-        def load_state(u, takes):
-            state = buffer([P, T], F32, f"state{u}", takes)
+        def load_state(u, at):
+            state = place([P, T], F32, f"state{u}", at)
             nc.sync.dma_start(out=state[:], in_=gT.rearrange("(p u) x -> u p x", u=PACK)[u])
             return state
 
@@ -86,27 +101,31 @@ def tile_list_edge_gated_messages_kernel(
         def gather_plane(dst, plane, offsets):
             nc.vector.tensor_copy(out=dst[:], in_=plane[:].bitcast(U8).indirect(offsets[:]))
 
-        def sort_columns(dst, src):
-            nc.vector.tensor_copy(
-                out=dst.rearrange("p (g t m) -> p g t m", g=2, t=PACK),
-                in_=src.rearrange("p (g m t) -> p g t m", g=2, t=PACK),
-            )
-
         def copy_on(engine, dst, src):
             if engine is nc.scalar:
                 nc.scalar.copy(out=dst, in_=src)
             else:
                 nc.vector.tensor_copy(out=dst, in_=src)
 
-        def cast_weight(raw, engines, name, takes=None):
-            grouped = buffer([P, PACK * WIDTH], BF16, name, takes)
-            for s, engine in enumerate(engines):
-                pair = slice(2 * s, 2 * s + 2)
-                copy_on(
-                    engine,
-                    grouped[:].rearrange("p (t m j) -> p m j t", t=PACK, j=PACK)[:, :, :, pair],
-                    raw[:].rearrange("p j (m t) -> p m j t", t=PACK)[:, :, :, pair],
-                )
+        def sort_columns(engine, dst, src):
+            copy_on(
+                engine,
+                dst.rearrange("p (g t m) -> p g t m", g=2, t=PACK),
+                src.rearrange("p (g m t) -> p g t m", g=2, t=PACK),
+            )
+
+        def cast_slots(grouped, raw, engine, s):
+            pair = slice(2 * s, 2 * s + 2)
+            copy_on(
+                engine,
+                grouped[:].rearrange("p (t m j) -> p m j t", t=PACK, j=PACK)[:, :, :, pair],
+                raw[:].rearrange("p j (m t) -> p m j t", t=PACK)[:, :, :, pair],
+            )
+
+        def cast_weight(raw, engine, name, at=None):
+            grouped = place([P, PACK * WIDTH], BF16, name, at)
+            for s in range(2):
+                cast_slots(grouped, raw, engine, s)
             return grouped
 
         def interleave_columns(grouped, hs, engine, columns):
@@ -116,16 +135,14 @@ def tile_list_edge_gated_messages_kernel(
                 hs[:, :, columns].rearrange("p t (x i) -> p x t i", i=4),
             )
 
-        def interleave(hs, name, takes):
-            grouped = buffer([P, PACK * WIDTH], BF16, name, takes)
+        def interleave(hs, name, at=None):
+            grouped = place([P, PACK * WIDTH], BF16, name, at)
             for columns in HALVES:
                 interleave_columns(grouped, hs, nc.vector, columns)
             return grouped
 
-        def mx_tiles(name, takes=None):
-            codes = buffer([P, WIDTH], U32, name, takes)
-            plane = keep.tile([P, WIDTH], U8, name=name + "_plane", align_bytes=64)
-            return codes, plane
+        def mx_tiles(name, at=None):
+            return place([P, WIDTH], U32, name, at), place([P, WIDTH], U8, name + "_plane")
 
         def quantize_columns(operand, grouped, columns):
             codes, plane = operand
@@ -135,8 +152,8 @@ def tile_list_edge_gated_messages_kernel(
                 in_=grouped[:, PACK * columns.start : PACK * columns.stop],
             )
 
-        def quantize(grouped, name, takes=None, parts=HALVES):
-            operand = mx_tiles(name, takes)
+        def quantize(grouped, name, at=None, parts=HALVES):
+            operand = mx_tiles(name, at)
             for columns in parts:
                 quantize_columns(operand, grouped, columns)
             return operand
@@ -175,25 +192,32 @@ def tile_list_edge_gated_messages_kernel(
             for t in slots:
                 nc.scalar.activation(out=hs[:, t, :], in_=banks[t][:], func=ACT.Relu, bias=b_sb[:, g, t : t + 1])
 
-        def gate(e, u, w2_mx, h_mx, index=None):
-            z = bank(PACK * e + u if index is None else index, f"z{e}{u}")
+        def pass_w2(z, g, u, h_mx):
             m = slice(u * P, (u + 1) * P)
-            for g in range(2):
-                nc.tensor.matmul_mx(
-                    out=z[:],
-                    lhsT=w2_mx[g][0][:, m].bitcast(FP8X4),
-                    lhsT_scale=w2_mx[g][1][:, m],
-                    rhs=h_mx[g][0][:].bitcast(FP8X4),
-                    rhs_scale=h_mx[g][1][:],
-                    start=(g == 0),
-                    stop=(g == 1),
-                )
-            sig = keep.tile([P, WIDTH], F32, name=f"sig{e}{u}")
+            nc.tensor.matmul_mx(
+                out=z[:],
+                lhsT=w2_mx[g][0][:, m].bitcast(FP8X4),
+                lhsT_scale=w2_mx[g][1][:, m],
+                rhs=h_mx[0][:].bitcast(FP8X4),
+                rhs_scale=h_mx[1][:],
+                start=(g == 0),
+                stop=(g == 1),
+            )
+
+        def open_gates(e, h_mx):
+            zs = [bank(PACK * e + u, f"z{e}{u}") for u in range(PACK)]
+            for u in range(PACK):
+                pass_w2(zs[u], 0, u, h_mx)
+            return zs
+
+        def gate(e, u, z, h_mx, at=None):
+            pass_w2(z, 1, u, h_mx)
+            sig = place([P, WIDTH], F32, f"sig{e}{u}", at)
             nc.scalar.activation(out=sig[:], in_=z[:], func=ACT.Sigmoid, bias=c_sb[:, u : u + 1])
             return sig
 
-        def message(e, u, sig, takes=None):
-            res = buffer([P, WIDTH], F32, f"res{e}{u}", takes)
+        def message(e, u, sig, at=None):
+            res = place([P, WIDTH], F32, f"res{e}{u}", at)
             nc.vector.tensor_tensor(res[:], states[u][:].indirect(list1[:, entries(e)]), sig[:], MULT)
             nc.sync.dma_start(out=out.rearrange("(p u) x -> u p x", u=PACK)[u][:, edges(e)], in_=res[:])
 
@@ -211,52 +235,53 @@ def tile_list_edge_gated_messages_kernel(
         nc.sync.dma_start(out=wb_words_raw[:], in_=wb_words[0].bitcast(I32))
         nc.sync.dma_start(list1[:], offs)
         nc.sync.dma_start(out=tab_rows[P - 2 * ROWS : P, :], in_=tab_scales.bitcast(I32).rearrange("a q x -> q a x"))
-        tab2 = load_table(tab2_words[0], "tab2")
-        wa00 = load_wa(0, 0)
+        tab2 = load_table(tab2_words[0], "tab2", AT_TAB2)
+        wa00 = load_wa(0, 0, AT_WA00)
 
         gather_plane(v2_rows, tab2_rows, list2)
-        tab0 = load_table(tab_words[0], "tab0", takes="tab2_rows")
-        sort_columns(pair_rows[:, S : S + H], wb_rows[:].bitcast(U8))
+        tab0 = load_table(tab_words[0], "tab0", AT_TAB0)
+        sort_columns(nc.vector, pair_rows[:, S : S + H], wb_rows[:].bitcast(U8))
         nc.vector.tensor_copy(out=pair_rows[:, 0:S].bitcast(I32), in_=v2_rows[:].bitcast(I32))
         for r in range(4):
             nc.sync.dma_start(out=pair_planes[r:P:32, :], in_=pair_rows[:].bitcast(I32)[P - ROWS + r : P : 4, :])
-        sort_columns(wb_codes[:], wb_words_raw[:].bitcast(U16))
-        wa10 = load_wa(1, 0, takes="wb_words_raw")
+        wa10 = load_wa(1, 0, AT_WA10)
+        sort_columns(nc.scalar, wb_codes[:], wb_words_raw[:].bitcast(U16))
         gather_plane(v_rows, tab_rows, list1)
         for q in (0, 2, 1, 3):
             first = P - 2 * ROWS + 8 * q
             nc.sync.dma_start(
                 out=v_planes[32 * q + V_PLANE : 32 * q + V_PLANE + 4, :], in_=v_rows[:].bitcast(I32)[first : first + 8, :]
             )
-        tab1 = load_table(tab_words[1], "tab1", takes="tab_rows")
-
-        b_sb = buffer([P, 2, 2 * PACK], F32, "b_sb", takes="v_rows")
+        tab1 = load_table(tab_words[1], "tab1", AT_TAB1)
+        b_sb = place([P, 2, 2 * PACK], F32, "b_sb", AT_B)
         nc.sync.dma_start(out=b_sb[:, :, 0:PACK], in_=b.rearrange("(g p t) -> p g t", g=2, t=PACK))
 
         for e in range(2):
             gather_words(v2_codes[:, edges(e)], tab2, list2, e)
-        wa01 = load_wa(0, 1, takes="tab2")
-        wa00_bf = cast_weight(wa00, (nc.scalar, nc.scalar), "wa00_bf")
+        wa01 = load_wa(0, 1, AT_WA01)
+        wa11 = load_wa(1, 1, AT_WA11)
+        wa00_bf = cast_weight(wa00, nc.scalar, "wa00_bf")
         wa00_mx = quantize(wa00_bf, "wa00_mx", parts=WHOLE)
-        wa11 = load_wa(1, 1, takes="wa00_bf")
-        v0_codes = buffer([P, S], U32, "v0_codes", takes="wa00")
+        v0_codes = place([P, S], U32, "v0_codes")
         for e in range(2):
             v_codes[0, e] = v0_codes[:, edges(e)]
             gather_words(v_codes[0, e], tab0, list1, e)
-        w20 = load_weight(w2[0:WIDTH, :], "w20", takes="tab2_rows")
-        wa10_bf = cast_weight(wa10, (nc.scalar, nc.vector), "wa10_bf")
+        w20 = load_weight(w2[0:WIDTH, :], "w20", AT_W20)
+        w21 = load_weight(w2[WIDTH:H, :], "w21", AT_W21)
+        wa10_bf = place([P, PACK * WIDTH], BF16, "wa10_bf", AT_WA10_BF)
+        cast_slots(wa10_bf, wa10, nc.scalar, 0)
+        cast_slots(wa10_bf, wa10, nc.vector, 1)
         wa10_mx = quantize(wa10_bf, "wa10_mx")
-        w21 = load_weight(w2[WIDTH:H, :], "w21", takes="wa10_bf")
-        v1_codes = buffer([P, S], U32, "v1_codes")
+        c_sb = place([P, PACK], F32, "c_sb", AT_WA10_BF)
+        nc.sync.dma_start(out=c_sb[:], in_=c.rearrange("(p u) -> p u", u=PACK))
+        v1_codes = place([P, S], U32, "v1_codes")
         for e in range(2):
             v_codes[1, e] = v1_codes[:, edges(e)]
             gather_words(v_codes[1, e], tab1, list1, e)
-        c_sb = buffer([P, PACK], F32, "c_sb", takes="tab_rows")
-        nc.sync.dma_start(out=c_sb[:], in_=c.rearrange("(p u) -> p u", u=PACK))
-        wa01_bf = cast_weight(wa01, (nc.vector, nc.vector), "wa01_bf")
-        states = [load_state(0, takes="tab2")]
+        states = [load_state(0, AT_TAB1)]
+        wa01_bf = cast_weight(wa01, nc.vector, "wa01_bf")
+        states.append(load_state(1, AT_WA01))
         wa01_mx = quantize(wa01_bf, "wa01_mx")
-        states.append(load_state(1, takes="wa01_bf"))
         banks00 = open_banks(0, 0)
         pass_wb(banks00, 0, 0, start=True)
         banks01 = open_banks(0, 1)
@@ -265,14 +290,14 @@ def tile_list_edge_gated_messages_kernel(
         pass_wa(banks01, wa00_mx, 0, 1)
         pass_wa(banks00, wa10_mx, 1, 0, stop=True)
         pass_wa(banks01, wa10_mx, 1, 1, stop=True)
-        hs0 = buffer([P, 2 * PACK, WIDTH], BF16, "hs0")
-        hs00, hs01 = hs0[:, 0:PACK, :], hs0[:, PACK : 2 * PACK, :]
+        hs00 = place([P, PACK, WIDTH], BF16, "hs00")
+        hs01 = place([P, PACK, WIDTH], BF16, "hs01")
         relu(banks00, 0, hs00)
         relu(banks01, 0, hs01)
 
-        wa11_bf = cast_weight(wa11, (nc.vector, nc.vector), "wa11_bf")
-        wa11_mx = quantize(wa11_bf, "wa11_mx")
-        states.append(load_state(2, takes="wa11_bf"))
+        wa11_bf = cast_weight(wa11, nc.vector, "wa11_bf", AT_WA11_BF)
+        wa11_mx = quantize(wa11_bf, "wa11_mx", AT_WA11_MX)
+        states.append(load_state(2, AT_WA11_BF))
         banks10 = open_banks(1, 0)
         pass_wb(banks10, 1, 0, start=True)
         pass_wa(banks10, wa01_mx, 0, 0)
@@ -281,39 +306,37 @@ def tile_list_edge_gated_messages_kernel(
         pass_wa(banks11, wa11_mx, 1, 1, start=True)
         pass_wb(banks11, 1, 1)
         pass_wa(banks11, wa01_mx, 0, 1, stop=True)
-        hs10 = buffer([P, PACK, WIDTH], BF16, "hs10")
+        hs10 = place([P, PACK, WIDTH], BF16, "hs10", AT_HS10)
         relu(banks10, 1, hs10)
-        w21_bf = cast_weight(w21, (nc.scalar, nc.scalar), "w21_bf", takes="wa11_mx")
-        hs11 = buffer([P, PACK, WIDTH], BF16, "hs11", takes="wa10_bf")
+        w21_bf = cast_weight(w21, nc.scalar, "w21_bf", AT_WA11_MX)
+        hs11 = place([P, PACK, WIDTH], BF16, "hs11", AT_W21)
         relu(banks11, 1, hs11, range(2))
 
-        h00_bf = interleave(hs00, "h00_bf", takes="wa00_bf")
-        w20_bf = cast_weight(w20, (nc.vector, nc.vector), "w20_bf")
-        states.append(load_state(3, takes="tab2_rows"))
+        h00_bf = interleave(hs00, "h00_bf", AT_WA11)
+        w20_bf = cast_weight(w20, nc.vector, "w20_bf")
+        states.append(load_state(3, AT_W20))
         h00_mx = quantize(h00_bf, "h00_mx", parts=WHOLE)
         w2_mx = (quantize(w20_bf, "w20_mx", parts=WHOLE), mx_tiles("w21_mx"))
-        h10_bf = interleave(hs10, "h10_bf", takes=None)
+        z0 = open_gates(0, h00_mx)
+        h10_bf = interleave(hs10, "h10_bf")
         h10_mx = quantize(h10_bf, "h10_mx")
         quantize_columns(w2_mx[1], w21_bf, HALVES[0])
-        h01_bf = interleave(hs01, "h01_bf", takes="hs10")
+        h01_bf = interleave(hs01, "h01_bf", AT_HS10)
         quantize_columns(w2_mx[1], w21_bf, HALVES[1])
         h01_mx = quantize(h01_bf, "h01_mx", parts=WHOLE)
 
-        h0_mx = (h00_mx, h10_mx)
-        sigs = [gate(0, 0, w2_mx, h0_mx)]
+        sigs = [gate(0, 0, z0[0], h10_mx)]
         relu(banks11, 1, hs11, range(2, PACK))
-        sigs.append(gate(0, 1, w2_mx, h0_mx))
-        h11_bf = buffer([P, PACK * WIDTH], BF16, "h11_bf", takes="hs10")
-        interleave_columns(h11_bf, hs11, nc.scalar, HALVES[0])
-        sigs.append(gate(0, 2, w2_mx, h0_mx))
-        for u in range(2):
+        sigs.append(gate(0, 1, z0[1], h10_mx))
+        sigs.append(gate(0, 2, z0[2], h10_mx, AT_SIG02))
+        h11_bf = place([P, PACK * WIDTH], BF16, "h11_bf")
+        for columns in HALVES:
+            interleave_columns(h11_bf, hs11, nc.scalar, columns)
+        sigs.append(gate(0, 3, z0[3], h10_mx, AT_SIG03))
+        z1 = open_gates(1, h01_mx)
+        for u in range(3):
             message(0, u, sigs[u])
-        interleave_columns(h11_bf, hs11, nc.vector, HALVES[1])
-        h11_mx = quantize(h11_bf, "h11_mx")
-        message(0, 2, sigs[2])
-        h1_mx = (h01_mx, h11_mx)
-        for u in range(2):
-            message(1, u, gate(1, u, w2_mx, h1_mx))
-        message(0, 3, gate(0, 3, w2_mx, h0_mx, index=PACK + 1))
-        for u in range(2, PACK):
-            message(1, u, gate(1, u, w2_mx, h1_mx))
+        h11_mx = quantize(h11_bf, "h11_mx", AT_SIG02, parts=WHOLE)
+        message(0, 3, sigs[3])
+        for u, at in enumerate((AT_RES10, AT_RES11, None, None)):
+            message(1, u, gate(1, u, z1[u], h11_mx), at)

@@ -57,7 +57,7 @@ def tile_list_edge_gated_messages_kernel(
         AT_WA11_MX = 57 * KIB
         AT_WA00 = 61 * KIB
         AT_WA11_BF = 69 * KIB
-        AT_SIG02 = 77 * KIB
+        AT_SIG10, AT_SIG11 = 77 * KIB, 83 * KIB
         AT_RES10, AT_SIG03, AT_RES11 = 79 * KIB, 80 * KIB, 81 * KIB
 
         list1 = keep.tile([P, S // 16], U16, name="list1")
@@ -114,48 +114,51 @@ def tile_list_edge_gated_messages_kernel(
                 src.rearrange("p (g m t) -> p g t m", g=2, t=PACK),
             )
 
-        def cast_slots(grouped, raw, engine, s):
+        def cast_slots(dst, raw, engine, s):
             pair = slice(2 * s, 2 * s + 2)
             copy_on(
                 engine,
-                grouped[:].rearrange("p (t m j) -> p m j t", t=PACK, j=PACK)[:, :, :, pair],
+                dst.rearrange("p (t m j) -> p m j t", t=2, j=PACK),
                 raw[:].rearrange("p j (m t) -> p m j t", t=PACK)[:, :, :, pair],
             )
 
         def cast_weight(raw, engine, name, at=None):
             grouped = place([P, PACK * WIDTH], BF16, name, at)
             for s in range(2):
-                cast_slots(grouped, raw, engine, s)
+                cast_slots(words(grouped, HALVES[s]), raw, engine, s)
             return grouped
 
-        def interleave_columns(grouped, hs, engine, columns):
+        def words(grouped, columns):
+            return grouped[:, PACK * columns.start : PACK * columns.stop]
+
+        def interleave_columns(dst, hs, engine, columns):
             copy_on(
                 engine,
-                grouped[:, PACK * columns.start : PACK * columns.stop].rearrange("p (x i t) -> p x t i", i=4, t=PACK),
+                dst.rearrange("p (x i t) -> p x t i", i=4, t=PACK),
                 hs[:, :, columns].rearrange("p t (x i) -> p x t i", i=4),
             )
 
         def interleave(hs, name, at=None):
             grouped = place([P, PACK * WIDTH], BF16, name, at)
             for columns in HALVES:
-                interleave_columns(grouped, hs, nc.vector, columns)
+                interleave_columns(words(grouped, columns), hs, nc.vector, columns)
             return grouped
 
         def mx_tiles(name, at=None):
             return place([P, WIDTH], U32, name, at), place([P, WIDTH], U8, name + "_plane")
 
-        def quantize_columns(operand, grouped, columns):
+        def quantize_columns(operand, src, columns):
             codes, plane = operand
             nc.vector.quantize_mx(
                 out=codes[:, columns].bitcast(FP8X4),
                 scales=plane[:, columns],
-                in_=grouped[:, PACK * columns.start : PACK * columns.stop],
+                in_=src,
             )
 
         def quantize(grouped, name, at=None, parts=HALVES):
             operand = mx_tiles(name, at)
             for columns in parts:
-                quantize_columns(operand, grouped, columns)
+                quantize_columns(operand, words(grouped, columns), columns)
             return operand
 
         def open_banks(g, e):
@@ -262,16 +265,19 @@ def tile_list_edge_gated_messages_kernel(
         wa11 = load_wa(1, 1, AT_WA11)
         wa00_bf = cast_weight(wa00, nc.scalar, "wa00_bf")
         wa00_mx = quantize(wa00_bf, "wa00_mx", parts=WHOLE)
-        v0_codes = place([P, S], U32, "v0_codes")
-        for e in range(2):
-            v_codes[0, e] = v0_codes[:, edges(e)]
-            gather_words(v_codes[0, e], tab0, list1, e)
+        v_codes[0, 0] = place([P, WIDTH], U32, "v00_codes")[:]
+        gather_words(v_codes[0, 0], tab0, list1, 0)
+        v_codes[0, 1] = place([P, WIDTH], U32, "v01_codes")[:]
+        gather_words(v_codes[0, 1], tab0, list1, 1)
         w20 = load_weight(w2[0:WIDTH, :], "w20", AT_W20)
         w21 = load_weight(w2[WIDTH:H, :], "w21", AT_W21)
-        wa10_bf = place([P, PACK * WIDTH], BF16, "wa10_bf", AT_WA10_BF)
-        cast_slots(wa10_bf, wa10, nc.scalar, 0)
-        cast_slots(wa10_bf, wa10, nc.vector, 1)
-        wa10_mx = quantize(wa10_bf, "wa10_mx")
+        wa10_first = place([P, PACK * WIDTH // 2], BF16, "wa10_first", AT_WA10_BF)
+        wa10_second = place([P, PACK * WIDTH // 2], BF16, "wa10_second", AT_WA10_BF + 2 * KIB)
+        cast_slots(wa10_first[:], wa10, nc.scalar, 0)
+        cast_slots(wa10_second[:], wa10, nc.vector, 1)
+        wa10_mx = mx_tiles("wa10_mx")
+        quantize_columns(wa10_mx, wa10_first[:], HALVES[0])
+        quantize_columns(wa10_mx, wa10_second[:], HALVES[1])
         c_sb = place([P, PACK], F32, "c_sb", AT_WA10_BF)
         nc.sync.dma_start(out=c_sb[:], in_=c.rearrange("(p u) -> p u", u=PACK))
         v1_codes = place([P, S], U32, "v1_codes")
@@ -294,6 +300,8 @@ def tile_list_edge_gated_messages_kernel(
         hs01 = place([P, PACK, WIDTH], BF16, "hs01")
         relu(banks00, 0, hs00)
         relu(banks01, 0, hs01)
+        h00_first = place([P, PACK * WIDTH // 2], BF16, "h00_first")
+        interleave_columns(h00_first[:], hs00, nc.vector, HALVES[0])
 
         wa11_bf = cast_weight(wa11, nc.vector, "wa11_bf", AT_WA11_BF)
         wa11_mx = quantize(wa11_bf, "wa11_mx", AT_WA11_MX)
@@ -312,31 +320,37 @@ def tile_list_edge_gated_messages_kernel(
         hs11 = place([P, PACK, WIDTH], BF16, "hs11", AT_W21)
         relu(banks11, 1, hs11, range(2))
 
-        h00_bf = interleave(hs00, "h00_bf", AT_WA11)
+        h00_second = place([P, PACK * WIDTH // 2], BF16, "h00_second", AT_WA11)
+        interleave_columns(h00_second[:], hs00, nc.vector, HALVES[1])
         w20_bf = cast_weight(w20, nc.vector, "w20_bf")
         states.append(load_state(3, AT_W20))
-        h00_mx = quantize(h00_bf, "h00_mx", parts=WHOLE)
+        h00_mx = mx_tiles("h00_mx", AT_WA11 + 2 * KIB)
+        quantize_columns(h00_mx, h00_first[:], HALVES[0])
+        quantize_columns(h00_mx, h00_second[:], HALVES[1])
         w2_mx = (quantize(w20_bf, "w20_mx", parts=WHOLE), mx_tiles("w21_mx"))
         z0 = open_gates(0, h00_mx)
         h10_bf = interleave(hs10, "h10_bf")
         h10_mx = quantize(h10_bf, "h10_mx")
-        quantize_columns(w2_mx[1], w21_bf, HALVES[0])
+        quantize_columns(w2_mx[1], words(w21_bf, HALVES[0]), HALVES[0])
         h01_bf = interleave(hs01, "h01_bf", AT_HS10)
-        quantize_columns(w2_mx[1], w21_bf, HALVES[1])
+        quantize_columns(w2_mx[1], words(w21_bf, HALVES[1]), HALVES[1])
         h01_mx = quantize(h01_bf, "h01_mx", parts=WHOLE)
 
         sigs = [gate(0, 0, z0[0], h10_mx)]
         relu(banks11, 1, hs11, range(2, PACK))
         sigs.append(gate(0, 1, z0[1], h10_mx))
-        sigs.append(gate(0, 2, z0[2], h10_mx, AT_SIG02))
         h11_bf = place([P, PACK * WIDTH], BF16, "h11_bf")
-        for columns in HALVES:
-            interleave_columns(h11_bf, hs11, nc.scalar, columns)
+        interleave_columns(words(h11_bf, HALVES[0]), hs11, nc.scalar, HALVES[0])
+        sigs.append(gate(0, 2, z0[2], h10_mx))
         sigs.append(gate(0, 3, z0[3], h10_mx, AT_SIG03))
         z1 = open_gates(1, h01_mx)
-        for u in range(3):
+        message(0, 0, sigs[0])
+        interleave_columns(words(h11_bf, HALVES[1]), hs11, nc.vector, HALVES[1])
+        message(0, 1, sigs[1])
+        h11_mx = quantize(h11_bf, "h11_mx", parts=WHOLE)
+        for u in range(2, PACK):
             message(0, u, sigs[u])
-        h11_mx = quantize(h11_bf, "h11_mx", AT_SIG02, parts=WHOLE)
-        message(0, 3, sigs[3])
-        for u, at in enumerate((AT_RES10, AT_RES11, None, None)):
+        message(1, 0, gate(1, 0, z1[0], h11_mx, AT_SIG10), AT_RES10)
+        message(1, 1, gate(1, 1, z1[1], h11_mx, AT_SIG11), AT_RES11)
+        for u, at in ((2, AT_SIG10), (3, AT_SIG11)):
             message(1, u, gate(1, u, z1[u], h11_mx), at)

@@ -57,8 +57,7 @@ def tile_list_edge_gated_messages_kernel(
         AT_WA11_MX = 57 * KIB
         AT_WA00 = 61 * KIB
         AT_WA11_BF = 69 * KIB
-        AT_SIG10, AT_SIG11 = 77 * KIB, 83 * KIB
-        AT_RES10, AT_SIG03, AT_RES11 = 79 * KIB, 80 * KIB, 81 * KIB
+        AT_SIG11 = 77 * KIB
 
         list1 = keep.tile([P, S // 16], U16, name="list1")
         list2 = keep.tile([P, S // 16], U16, name="list2")
@@ -338,19 +337,16 @@ def tile_list_edge_gated_messages_kernel(
 
         sigs = [gate(0, 0, z0[0], h10_mx)]
         relu(banks11, 1, hs11, range(2, PACK))
-        sigs.append(gate(0, 1, z0[1], h10_mx))
         h11_bf = place([P, PACK * WIDTH], BF16, "h11_bf")
         interleave_columns(words(h11_bf, HALVES[0]), hs11, nc.scalar, HALVES[0])
-        sigs.append(gate(0, 2, z0[2], h10_mx))
-        sigs.append(gate(0, 3, z0[3], h10_mx, AT_SIG03))
         z1 = open_gates(1, h01_mx)
         message(0, 0, sigs[0])
         interleave_columns(words(h11_bf, HALVES[1]), hs11, nc.vector, HALVES[1])
-        message(0, 1, sigs[1])
-        h11_mx = quantize(h11_bf, "h11_mx", parts=WHOLE)
-        for u in range(2, PACK):
-            message(0, u, sigs[u])
-        message(1, 0, gate(1, 0, z1[0], h11_mx, AT_SIG10), AT_RES10)
-        message(1, 1, gate(1, 1, z1[1], h11_mx, AT_SIG11), AT_RES11)
-        for u, at in ((2, AT_SIG10), (3, AT_SIG11)):
-            message(1, u, gate(1, u, z1[u], h11_mx), at)
+        h11_mx = quantize(h11_bf, "h11_mx")
+        for u in range(1, 3):
+            message(0, u, gate(0, u, z0[u], h10_mx))
+        message(1, 0, gate(1, 0, z1[0], h11_mx))
+        message(1, 1, gate(1, 1, z1[1], h11_mx, AT_SIG11))
+        message(1, 2, gate(1, 2, z1[2], h11_mx))
+        message(0, 3, gate(0, 3, z0[3], h10_mx), AT_SIG11)
+        message(1, 3, gate(1, 3, z1[3], h11_mx))

@@ -56,8 +56,9 @@ def tile_list_edge_gated_messages_kernel(
         AT_HS10 = 53 * KIB
         AT_WA11_MX = 57 * KIB
         AT_WA00 = 61 * KIB
-        AT_WA11_BF = 69 * KIB
-        AT_SIG11 = 77 * KIB
+        AT_H01_FIRST, AT_WA11_BF, AT_STATE2 = 68 * KIB, 69 * KIB, 70 * KIB
+        AT_SIG11 = 87 * KIB
+        AT_WA01_BF = 79 * KIB
 
         list1 = keep.tile([P, S // 16], U16, name="list1")
         list2 = keep.tile([P, S // 16], U16, name="list2")
@@ -74,7 +75,7 @@ def tile_list_edge_gated_messages_kernel(
         v2_plane = pair_planes[:].bitcast(U8)[:, 0:S]
         wb_plane = pair_planes[:].bitcast(U8)[:, S : S + H]
         v2_codes = place([P, S], U32, "v2_codes")
-        v_codes = {}
+        v_codes = [place([P, S], U32, f"v{a}_codes") for a in range(2)]
 
         def load_table(words, name, at):
             tile = place([P, T], I32, name, at)
@@ -91,11 +92,12 @@ def tile_list_edge_gated_messages_kernel(
 
         def load_state(u, at):
             state = place([P, T], F32, f"state{u}", at)
-            nc.sync.dma_start(out=state[:], in_=gT.rearrange("(p u) x -> u p x", u=PACK)[u])
+            nc.sync.dma_start(out=state[:], in_=gT[u * P : (u + 1) * P, :])
             return state
 
-        def gather_words(dst, table, offsets, e):
-            nc.vector.tensor_copy(out=dst, in_=table[:].bitcast(U32).indirect(offsets[:, entries(e)]))
+        def gather_words(codes, table, offsets, columns):
+            picked = table[:].bitcast(U32).indirect(offsets[:, columns.start // 16 : columns.stop // 16])
+            nc.vector.tensor_copy(out=codes[:, columns], in_=picked)
 
         def gather_plane(dst, plane, offsets):
             nc.vector.tensor_copy(out=dst[:], in_=plane[:].bitcast(U8).indirect(offsets[:]))
@@ -120,6 +122,19 @@ def tile_list_edge_gated_messages_kernel(
                 dst.rearrange("p (t m j) -> p m j t", t=2, j=PACK),
                 raw[:].rearrange("p j (m t) -> p m j t", t=PACK)[:, :, :, pair],
             )
+
+        def cast_columns(dst, raw, engine, columns):
+            copy_on(
+                engine,
+                dst.rearrange("p (x i j) -> p x j i", i=2, j=PACK),
+                raw[:, :, columns].rearrange("p j (x i) -> p x j i", i=2),
+            )
+
+        def cast_plain(raw, engine, name, at=None):
+            grouped = place([P, PACK * WIDTH], BF16, name, at)
+            for columns in HALVES:
+                cast_columns(words(grouped, columns), raw, engine, columns)
+            return grouped
 
         def cast_weight(raw, engine, name, at=None):
             grouped = place([P, PACK * WIDTH], BF16, name, at)
@@ -160,39 +175,46 @@ def tile_list_edge_gated_messages_kernel(
                 quantize_columns(operand, words(grouped, columns), columns)
             return operand
 
-        def open_banks(g, e):
-            return [bank(PACK * e + t, f"a{g}{e}{t}") for t in range(PACK)]
+        def whole_sums(g, e):
+            return [(bank(PACK * e + t, f"a{g}{e}{t}")[:], t, edges(e)) for t in range(PACK)]
 
-        def pass_wa(banks, operand, a, e, start=False, stop=False):
+        def quarter_sums(q):
+            sums = []
+            for s in range(2):
+                shared = bank(2 * q + s, f"a0q{q}{s}")
+                sums += [(shared[:, HALVES[i]], 2 * s + i, HALVES[q]) for i in range(2)]
+            return sums
+
+        def pass_wa(sums, operand, a, start=False, stop=False, shared=False):
             codes, plane = operand
-            for t in range(PACK):
+            for acc, t, columns in sums:
                 m = slice(t * P, (t + 1) * P)
                 nc.tensor.matmul_mx(
-                    out=banks[t][:],
+                    out=acc,
                     lhsT=codes[:, m].bitcast(FP8X4),
                     lhsT_scale=plane[:, m],
-                    rhs=v_codes[a, e].bitcast(FP8X4),
-                    rhs_scale=v_planes[:].bitcast(U8)[V_PLANE:P, a * S + e * WIDTH : a * S + (e + 1) * WIDTH],
+                    rhs=v_codes[a][:, columns].bitcast(FP8X4),
+                    rhs_scale=v_planes[:].bitcast(U8)[V_PLANE:P, a * S + columns.start : a * S + columns.stop],
                     start=start,
-                    stop=stop,
+                    stop=stop and (not shared or t % 2 == 1),
                 )
 
-        def pass_wb(banks, g, e, start=False):
-            for t in range(PACK):
+        def pass_wb(sums, g, start=False, shared=False):
+            for acc, t, columns in sums:
                 first = g * WIDTH + t * P
                 nc.tensor.matmul_mx(
-                    out=banks[t][:],
+                    out=acc,
                     lhsT=wb_codes[:].bitcast(U8)[:, 2 * first : 2 * (first + P)].bitcast(FP4X4),
                     lhsT_scale=wb_plane[:, first : first + P],
-                    rhs=v2_codes[:, edges(e)].bitcast(FP8X4),
-                    rhs_scale=v2_plane[:, edges(e)],
-                    start=start,
+                    rhs=v2_codes[:, columns].bitcast(FP8X4),
+                    rhs_scale=v2_plane[:, columns],
+                    start=start and (not shared or t % 2 == 0),
                     stop=False,
                 )
 
-        def relu(banks, g, hs, slots=range(PACK)):
-            for t in slots:
-                nc.scalar.activation(out=hs[:, t, :], in_=banks[t][:], func=ACT.Relu, bias=b_sb[:, g, t : t + 1])
+        def relu(sums, g, hs):
+            for acc, t, columns in sums:
+                nc.scalar.activation(out=hs[:, t, :], in_=acc, func=ACT.Relu, bias=b_sb[:, g, t : t + 1])
 
         def pass_w2(z, g, u, h_mx):
             m = slice(u * P, (u + 1) * P)
@@ -206,11 +228,10 @@ def tile_list_edge_gated_messages_kernel(
                 stop=(g == 1),
             )
 
-        def open_gates(e, h_mx):
-            zs = [bank(PACK * e + u, f"z{e}{u}") for u in range(PACK)]
-            for u in range(PACK):
-                pass_w2(zs[u], 0, u, h_mx)
-            return zs
+        def open_gate(e, u, index, h_mx):
+            z = bank(index, f"z{e}{u}")
+            pass_w2(z, 0, u, h_mx)
+            return z
 
         def gate(e, u, z, h_mx, at=None):
             pass_w2(z, 1, u, h_mx)
@@ -221,7 +242,7 @@ def tile_list_edge_gated_messages_kernel(
         def message(e, u, sig, at=None):
             res = place([P, WIDTH], F32, f"res{e}{u}", at)
             nc.vector.tensor_tensor(res[:], states[u][:].indirect(list1[:, entries(e)]), sig[:], MULT)
-            nc.sync.dma_start(out=out.rearrange("(p u) x -> u p x", u=PACK)[u][:, edges(e)], in_=res[:])
+            nc.sync.dma_start(out=out[u * P : (u + 1) * P, edges(e)], in_=res[:])
 
         nc.gpsimd.memset(tab2_rows[0 : P - ROWS, :], 0)
         nc.gpsimd.memset(wb_rows[0 : P - ROWS, :], 0)
@@ -259,15 +280,13 @@ def tile_list_edge_gated_messages_kernel(
         nc.sync.dma_start(out=b_sb[:, :, 0:PACK], in_=b.rearrange("(g p t) -> p g t", g=2, t=PACK))
 
         for e in range(2):
-            gather_words(v2_codes[:, edges(e)], tab2, list2, e)
+            gather_words(v2_codes, tab2, list2, edges(e))
         wa01 = load_wa(0, 1, AT_WA01)
         wa11 = load_wa(1, 1, AT_WA11)
         wa00_bf = cast_weight(wa00, nc.scalar, "wa00_bf")
         wa00_mx = quantize(wa00_bf, "wa00_mx", parts=WHOLE)
-        v_codes[0, 0] = place([P, WIDTH], U32, "v00_codes")[:]
-        gather_words(v_codes[0, 0], tab0, list1, 0)
-        v_codes[0, 1] = place([P, WIDTH], U32, "v01_codes")[:]
-        gather_words(v_codes[0, 1], tab0, list1, 1)
+        for e in range(2):
+            gather_words(v_codes[0], tab0, list1, edges(e))
         w20 = load_weight(w2[0:WIDTH, :], "w20", AT_W20)
         w21 = load_weight(w2[WIDTH:H, :], "w21", AT_W21)
         wa10_first = place([P, PACK * WIDTH // 2], BF16, "wa10_first", AT_WA10_BF)
@@ -278,75 +297,84 @@ def tile_list_edge_gated_messages_kernel(
         quantize_columns(wa10_mx, wa10_first[:], HALVES[0])
         quantize_columns(wa10_mx, wa10_second[:], HALVES[1])
         c_sb = place([P, PACK], F32, "c_sb", AT_WA10_BF)
-        nc.sync.dma_start(out=c_sb[:], in_=c.rearrange("(p u) -> p u", u=PACK))
-        v1_codes = place([P, S], U32, "v1_codes")
-        for e in range(2):
-            v_codes[1, e] = v1_codes[:, edges(e)]
-            gather_words(v_codes[1, e], tab1, list1, e)
+        with nc.allow_non_contiguous_dma(reason="one bias a partition and gate"):
+            nc.sync.dma_start(out=c_sb[:], in_=c.rearrange("(u p) -> p u", u=PACK))
+        for columns in (*HALVES, edges(1)):
+            gather_words(v_codes[1], tab1, list1, columns)
         states = [load_state(0, AT_TAB1)]
-        wa01_bf = cast_weight(wa01, nc.vector, "wa01_bf")
-        states.append(load_state(1, AT_WA01))
+        wa01_bf = cast_weight(wa01, nc.vector, "wa01_bf", AT_WA01_BF)
         wa01_mx = quantize(wa01_bf, "wa01_mx")
-        banks00 = open_banks(0, 0)
-        pass_wb(banks00, 0, 0, start=True)
-        banks01 = open_banks(0, 1)
-        pass_wb(banks01, 0, 1, start=True)
-        pass_wa(banks00, wa00_mx, 0, 0)
-        pass_wa(banks01, wa00_mx, 0, 1)
-        pass_wa(banks00, wa10_mx, 1, 0, stop=True)
-        pass_wa(banks01, wa10_mx, 1, 1, stop=True)
-        hs00 = place([P, PACK, WIDTH], BF16, "hs00")
+        states.append(load_state(1, AT_WA01_BF))
+        quarters = [quarter_sums(q) for q in range(2)]
+        sums01 = whole_sums(0, 1)
+        for sums in quarters:
+            pass_wb(sums, 0, start=True, shared=True)
+        pass_wb(sums01, 0, start=True)
+        for sums in (*quarters, sums01):
+            pass_wa(sums, wa00_mx, 0)
+        for sums in quarters:
+            pass_wa(sums, wa10_mx, 1, stop=True, shared=True)
+        pass_wa(sums01, wa10_mx, 1, stop=True)
+        hs00 = [place([P, PACK, WIDTH // 2], BF16, f"hs00{q}") for q in range(2)]
+        for q in range(2):
+            relu(quarters[q], 0, hs00[q])
         hs01 = place([P, PACK, WIDTH], BF16, "hs01")
-        relu(banks00, 0, hs00)
-        relu(banks01, 0, hs01)
-        h00_first = place([P, PACK * WIDTH // 2], BF16, "h00_first")
-        interleave_columns(h00_first[:], hs00, nc.vector, HALVES[0])
+        relu(sums01, 0, hs01)
+        h00_first = place([P, PACK * WIDTH // 2], BF16, "h00_first", AT_WA01)
+        interleave_columns(h00_first[:], hs00[0], nc.vector, HALVES[0])
 
         wa11_bf = cast_weight(wa11, nc.vector, "wa11_bf", AT_WA11_BF)
         wa11_mx = quantize(wa11_bf, "wa11_mx", AT_WA11_MX)
-        states.append(load_state(2, AT_WA11_BF))
-        banks10 = open_banks(1, 0)
-        pass_wb(banks10, 1, 0, start=True)
-        pass_wa(banks10, wa01_mx, 0, 0)
-        pass_wa(banks10, wa11_mx, 1, 0, stop=True)
-        banks11 = open_banks(1, 1)
-        pass_wa(banks11, wa11_mx, 1, 1, start=True)
-        pass_wb(banks11, 1, 1)
-        pass_wa(banks11, wa01_mx, 0, 1, stop=True)
+        states.append(load_state(2, AT_STATE2))
+        sums10 = whole_sums(1, 0)
+        pass_wb(sums10, 1, start=True)
+        pass_wa(sums10, wa01_mx, 0)
+        pass_wa(sums10, wa11_mx, 1, stop=True)
+        sums11 = whole_sums(1, 1)
+        pass_wa(sums11, wa11_mx, 1, start=True)
+        pass_wb(sums11, 1)
+        pass_wa(sums11, wa01_mx, 0, stop=True)
         hs10 = place([P, PACK, WIDTH], BF16, "hs10", AT_HS10)
-        relu(banks10, 1, hs10)
-        w21_bf = cast_weight(w21, nc.scalar, "w21_bf", AT_WA11_MX)
+        relu(sums10, 1, hs10)
+        w21_bf = cast_plain(w21, nc.scalar, "w21_bf", AT_WA11_MX)
         hs11 = place([P, PACK, WIDTH], BF16, "hs11", AT_W21)
-        relu(banks11, 1, hs11, range(2))
+        relu(sums11[:2], 1, hs11)
 
         h00_second = place([P, PACK * WIDTH // 2], BF16, "h00_second", AT_WA11)
-        interleave_columns(h00_second[:], hs00, nc.vector, HALVES[1])
-        w20_bf = cast_weight(w20, nc.vector, "w20_bf")
+        interleave_columns(h00_second[:], hs00[1], nc.vector, HALVES[0])
+        w20_bf = cast_plain(w20, nc.vector, "w20_bf")
         states.append(load_state(3, AT_W20))
         h00_mx = mx_tiles("h00_mx", AT_WA11 + 2 * KIB)
         quantize_columns(h00_mx, h00_first[:], HALVES[0])
         quantize_columns(h00_mx, h00_second[:], HALVES[1])
         w2_mx = (quantize(w20_bf, "w20_mx", parts=WHOLE), mx_tiles("w21_mx"))
-        z0 = open_gates(0, h00_mx)
+        h01_first = place([P, PACK * WIDTH // 2], BF16, "h01_first", AT_H01_FIRST)
+        interleave_columns(h01_first[:], hs01, nc.vector, HALVES[0])
+        z0 = [open_gate(0, u, u, h00_mx) for u in range(2)]
         h10_bf = interleave(hs10, "h10_bf")
         h10_mx = quantize(h10_bf, "h10_mx")
         quantize_columns(w2_mx[1], words(w21_bf, HALVES[0]), HALVES[0])
-        h01_bf = interleave(hs01, "h01_bf", AT_HS10)
+        h01_second = place([P, PACK * WIDTH // 2], BF16, "h01_second", AT_HS10)
+        interleave_columns(h01_second[:], hs01, nc.vector, HALVES[1])
         quantize_columns(w2_mx[1], words(w21_bf, HALVES[1]), HALVES[1])
-        h01_mx = quantize(h01_bf, "h01_mx", parts=WHOLE)
+        h01_mx = mx_tiles("h01_mx", AT_HS10 + 2 * KIB)
+        quantize_columns(h01_mx, h01_first[:], HALVES[0])
+        quantize_columns(h01_mx, h01_second[:], HALVES[1])
 
         sigs = [gate(0, 0, z0[0], h10_mx)]
-        relu(banks11, 1, hs11, range(2, PACK))
+        relu(sums11[2:], 1, hs11)
+        sigs.append(gate(0, 1, z0[1], h10_mx))
         h11_bf = place([P, PACK * WIDTH], BF16, "h11_bf")
         interleave_columns(words(h11_bf, HALVES[0]), hs11, nc.scalar, HALVES[0])
-        z1 = open_gates(1, h01_mx)
+        z1 = [open_gate(1, u, PACK + u, h01_mx) for u in range(PACK)]
         message(0, 0, sigs[0])
         interleave_columns(words(h11_bf, HALVES[1]), hs11, nc.vector, HALVES[1])
-        h11_mx = quantize(h11_bf, "h11_mx")
-        for u in range(1, 3):
-            message(0, u, gate(0, u, z0[u], h10_mx))
+        message(0, 1, sigs[1])
+        h11_mx = quantize(h11_bf, "h11_mx", parts=WHOLE)
+        message(0, 2, gate(0, 2, open_gate(0, 2, 1, h00_mx), h10_mx))
+        last = open_gate(0, 3, 1, h00_mx)
         message(1, 0, gate(1, 0, z1[0], h11_mx))
         message(1, 1, gate(1, 1, z1[1], h11_mx, AT_SIG11))
         message(1, 2, gate(1, 2, z1[2], h11_mx))
-        message(0, 3, gate(0, 3, z0[3], h10_mx), AT_SIG11)
+        message(0, 3, gate(0, 3, last, h10_mx), AT_SIG11)
         message(1, 3, gate(1, 3, z1[3], h11_mx))

@@ -57,7 +57,8 @@ def tile_list_edge_gated_messages_kernel(
         AT_WA11_MX = 57 * KIB
         AT_WA00 = 61 * KIB
         AT_H01_FIRST, AT_WA11_BF, AT_STATE2 = 68 * KIB, 69 * KIB, 70 * KIB
-        AT_SIG11 = 87 * KIB
+        AT_SIG01, AT_SIG10, AT_SIG11 = 87 * KIB, 89 * KIB, 91 * KIB
+        AT_RES10, AT_SIG03, AT_RES11 = 93 * KIB, 94 * KIB, 95 * KIB
         AT_WA01_BF = 79 * KIB
 
         list1 = keep.tile([P, S // 16], U16, name="list1")
@@ -350,7 +351,7 @@ def tile_list_edge_gated_messages_kernel(
         w2_mx = (quantize(w20_bf, "w20_mx", parts=WHOLE), mx_tiles("w21_mx"))
         h01_first = place([P, PACK * WIDTH // 2], BF16, "h01_first", AT_H01_FIRST)
         interleave_columns(h01_first[:], hs01, nc.vector, HALVES[0])
-        z0 = [open_gate(0, u, u, h00_mx) for u in range(2)]
+        z0 = [open_gate(0, u, u, h00_mx) for u in range(PACK)]
         h10_bf = interleave(hs10, "h10_bf")
         h10_mx = quantize(h10_bf, "h10_mx")
         quantize_columns(w2_mx[1], words(w21_bf, HALVES[0]), HALVES[0])
@@ -363,18 +364,21 @@ def tile_list_edge_gated_messages_kernel(
 
         sigs = [gate(0, 0, z0[0], h10_mx)]
         relu(sums11[2:], 1, hs11)
-        sigs.append(gate(0, 1, z0[1], h10_mx))
-        h11_bf = place([P, PACK * WIDTH], BF16, "h11_bf")
-        interleave_columns(words(h11_bf, HALVES[0]), hs11, nc.scalar, HALVES[0])
+        sigs.append(gate(0, 1, z0[1], h10_mx, AT_SIG01))
+        h11_bf = [place([P, PACK * WIDTH // 2], BF16, f"h11_bf{i}") for i in range(2)]
+        interleave_columns(h11_bf[0][:], hs11, nc.scalar, HALVES[0])
+        sigs.append(gate(0, 2, z0[2], h10_mx))
+        sigs.append(gate(0, 3, z0[3], h10_mx, AT_SIG03))
         z1 = [open_gate(1, u, PACK + u, h01_mx) for u in range(PACK)]
         message(0, 0, sigs[0])
-        interleave_columns(words(h11_bf, HALVES[1]), hs11, nc.vector, HALVES[1])
+        interleave_columns(h11_bf[1][:], hs11, nc.vector, HALVES[1])
         message(0, 1, sigs[1])
-        h11_mx = quantize(h11_bf, "h11_mx", parts=WHOLE)
-        message(0, 2, gate(0, 2, open_gate(0, 2, 1, h00_mx), h10_mx))
-        last = open_gate(0, 3, 1, h00_mx)
-        message(1, 0, gate(1, 0, z1[0], h11_mx))
-        message(1, 1, gate(1, 1, z1[1], h11_mx, AT_SIG11))
-        message(1, 2, gate(1, 2, z1[2], h11_mx))
-        message(0, 3, gate(0, 3, last, h10_mx), AT_SIG11)
-        message(1, 3, gate(1, 3, z1[3], h11_mx))
+        h11_mx = mx_tiles("h11_mx", AT_SIG01)
+        for i in (1, 0):
+            quantize_columns(h11_mx, h11_bf[i][:], HALVES[i])
+        for u in range(2, PACK):
+            message(0, u, sigs[u])
+        message(1, 0, gate(1, 0, z1[0], h11_mx, AT_SIG10), AT_RES10)
+        message(1, 1, gate(1, 1, z1[1], h11_mx, AT_SIG11), AT_RES11)
+        for u, at in ((2, AT_SIG10), (3, AT_SIG11)):
+            message(1, u, gate(1, u, z1[u], h11_mx), at)

@@ -45,9 +45,6 @@ def tile_list_edge_gated_messages_kernel(
         def edges(e):
             return slice(e * WIDTH, (e + 1) * WIDTH)
 
-        def entries(e):
-            return slice(e * WIDTH // 16, (e + 1) * WIDTH // 16)
-
         AT_WA01, AT_TAB2, AT_WA11 = 0, 4 * KIB, 8 * KIB
         AT_W20, AT_TAB0, AT_W21 = 16 * KIB, 20 * KIB, 24 * KIB
         AT_B, AT_TAB1 = 32 * KIB, 33 * KIB
@@ -55,11 +52,10 @@ def tile_list_edge_gated_messages_kernel(
         AT_WA10_BF = 49 * KIB
         AT_HS10 = 53 * KIB
         AT_WA11_MX = 57 * KIB
-        AT_WA00 = 61 * KIB
-        AT_H01_FIRST, AT_WA11_BF, AT_STATE2 = 68 * KIB, 69 * KIB, 70 * KIB
-        AT_SIG01, AT_SIG10, AT_SIG11 = 87 * KIB, 89 * KIB, 91 * KIB
-        AT_RES10, AT_SIG03, AT_RES11 = 93 * KIB, 94 * KIB, 95 * KIB
-        AT_WA01_BF = 79 * KIB
+        AT_H01_FIRST, AT_WA11_BF, AT_STATE2 = 61 * KIB, 62 * KIB, 63 * KIB
+        AT_WA01_BF = 71 * KIB
+        AT_RES10, AT_SIG03, AT_RES11 = 79 * KIB, 80 * KIB, 81 * KIB
+        AT_SIG13 = 83 * KIB
 
         list1 = keep.tile([P, S // 16], U16, name="list1")
         list2 = keep.tile([P, S // 16], U16, name="list2")
@@ -78,17 +74,17 @@ def tile_list_edge_gated_messages_kernel(
         v2_codes = place([P, S], U32, "v2_codes")
         v_codes = [place([P, S], U32, f"v{a}_codes") for a in range(2)]
 
-        def load_table(words, name, at):
+        def load_table(packed, name, at):
             tile = place([P, T], I32, name, at)
-            nc.sync.dma_start(out=tile[:], in_=words.rearrange("p t i -> p (t i)").bitcast(I32))
+            nc.sync.dma_start(out=tile[:], in_=packed.rearrange("p t i -> p (t i)").bitcast(I32))
             return tile
 
-        def load_weight(rows, name, at):
+        def load_weight(rows, name, at=None):
             tile = place([P, PACK, WIDTH], F32, name, at)
             nc.sync.dma_start(out=tile[:], in_=rows.rearrange("(p j) x -> p j x", j=PACK))
             return tile
 
-        def load_wa(a, g, at):
+        def load_wa(a, g, at=None):
             return load_weight(wa[a * WIDTH : (a + 1) * WIDTH, g * WIDTH : (g + 1) * WIDTH], f"wa{a}{g}", at)
 
         def load_state(u, at):
@@ -96,8 +92,14 @@ def tile_list_edge_gated_messages_kernel(
             nc.sync.dma_start(out=state[:], in_=gT[u * P : (u + 1) * P, :])
             return state
 
+        def entries(offsets, columns):
+            return offsets[:, columns.start // 16 : columns.stop // 16]
+
+        def values(grouped, columns):
+            return grouped[:, PACK * columns.start : PACK * columns.stop]
+
         def gather_words(codes, table, offsets, columns):
-            picked = table[:].bitcast(U32).indirect(offsets[:, columns.start // 16 : columns.stop // 16])
+            picked = table[:].bitcast(U32).indirect(entries(offsets, columns))
             nc.vector.tensor_copy(out=codes[:, columns], in_=picked)
 
         def gather_plane(dst, plane, offsets):
@@ -131,20 +133,17 @@ def tile_list_edge_gated_messages_kernel(
                 raw[:, :, columns].rearrange("p j (x i) -> p x j i", i=2),
             )
 
-        def cast_plain(raw, engine, name, at=None):
+        def cast_w2(raw, engine, name, at=None, parts=HALVES):
             grouped = place([P, PACK * WIDTH], BF16, name, at)
-            for columns in HALVES:
-                cast_columns(words(grouped, columns), raw, engine, columns)
+            for columns in parts:
+                cast_columns(values(grouped, columns), raw, engine, columns)
             return grouped
 
-        def cast_weight(raw, engine, name, at=None):
+        def cast_wa(raw, engine, name, at=None):
             grouped = place([P, PACK * WIDTH], BF16, name, at)
             for s in range(2):
-                cast_slots(words(grouped, HALVES[s]), raw, engine, s)
+                cast_slots(values(grouped, HALVES[s]), raw, engine, s)
             return grouped
-
-        def words(grouped, columns):
-            return grouped[:, PACK * columns.start : PACK * columns.stop]
 
         def interleave_columns(dst, hs, engine, columns):
             copy_on(
@@ -153,27 +152,20 @@ def tile_list_edge_gated_messages_kernel(
                 hs[:, :, columns].rearrange("p t (x i) -> p x t i", i=4),
             )
 
-        def interleave(hs, name, at=None):
-            grouped = place([P, PACK * WIDTH], BF16, name, at)
-            for columns in HALVES:
-                interleave_columns(words(grouped, columns), hs, nc.vector, columns)
-            return grouped
+        def half_tile(name, at=None):
+            return place([P, PACK * WIDTH // 2], BF16, name, at)
 
         def mx_tiles(name, at=None):
             return place([P, WIDTH], U32, name, at), place([P, WIDTH], U8, name + "_plane")
 
         def quantize_columns(operand, src, columns):
             codes, plane = operand
-            nc.vector.quantize_mx(
-                out=codes[:, columns].bitcast(FP8X4),
-                scales=plane[:, columns],
-                in_=src,
-            )
+            nc.vector.quantize_mx(out=codes[:, columns].bitcast(FP8X4), scales=plane[:, columns], in_=src)
 
         def quantize(grouped, name, at=None, parts=HALVES):
             operand = mx_tiles(name, at)
             for columns in parts:
-                quantize_columns(operand, words(grouped, columns), columns)
+                quantize_columns(operand, values(grouped, columns), columns)
             return operand
 
         def whole_sums(g, e):
@@ -182,8 +174,8 @@ def tile_list_edge_gated_messages_kernel(
         def quarter_sums(q):
             sums = []
             for s in range(2):
-                shared = bank(2 * q + s, f"a0q{q}{s}")
-                sums += [(shared[:, HALVES[i]], 2 * s + i, HALVES[q]) for i in range(2)]
+                both = bank(2 * q + s, f"a0q{q}{s}")
+                sums += [(both[:, HALVES[i]], 2 * s + i, HALVES[q]) for i in range(2)]
             return sums
 
         def pass_wa(sums, operand, a, start=False, stop=False, shared=False):
@@ -229,21 +221,24 @@ def tile_list_edge_gated_messages_kernel(
                 stop=(g == 1),
             )
 
-        def open_gate(e, u, index, h_mx):
-            z = bank(index, f"z{e}{u}")
+        def open_gate(e, u, h_mx):
+            z = bank(PACK * e + u, f"z{e}{u}")
             pass_w2(z, 0, u, h_mx)
             return z
 
-        def gate(e, u, z, h_mx, at=None):
+        def close_gate(e, u, z, h_mx, at=None):
             pass_w2(z, 1, u, h_mx)
             sig = place([P, WIDTH], F32, f"sig{e}{u}", at)
             nc.scalar.activation(out=sig[:], in_=z[:], func=ACT.Sigmoid, bias=c_sb[:, u : u + 1])
             return sig
 
-        def message(e, u, sig, at=None):
+        def message(e, u, sig, at=None, parts=WHOLE):
             res = place([P, WIDTH], F32, f"res{e}{u}", at)
-            nc.vector.tensor_tensor(res[:], states[u][:].indirect(list1[:, entries(e)]), sig[:], MULT)
-            nc.sync.dma_start(out=out[u * P : (u + 1) * P, edges(e)], in_=res[:])
+            for part in parts:
+                columns = slice(e * WIDTH + part.start, e * WIDTH + part.stop)
+                picked = states[u][:].indirect(entries(list1, columns))
+                nc.vector.tensor_tensor(res[:, part], picked, sig[:, part], MULT)
+                nc.sync.dma_start(out=out[u * P : (u + 1) * P, columns], in_=res[:, part])
 
         nc.gpsimd.memset(tab2_rows[0 : P - ROWS, :], 0)
         nc.gpsimd.memset(wb_rows[0 : P - ROWS, :], 0)
@@ -260,7 +255,7 @@ def tile_list_edge_gated_messages_kernel(
         nc.sync.dma_start(list1[:], offs)
         nc.sync.dma_start(out=tab_rows[P - 2 * ROWS : P, :], in_=tab_scales.bitcast(I32).rearrange("a q x -> q a x"))
         tab2 = load_table(tab2_words[0], "tab2", AT_TAB2)
-        wa00 = load_wa(0, 0, AT_WA00)
+        wa00 = load_wa(0, 0)
 
         gather_plane(v2_rows, tab2_rows, list2)
         tab0 = load_table(tab_words[0], "tab0", AT_TAB0)
@@ -271,11 +266,10 @@ def tile_list_edge_gated_messages_kernel(
         wa10 = load_wa(1, 0, AT_WA10)
         sort_columns(nc.scalar, wb_codes[:], wb_words_raw[:].bitcast(U16))
         gather_plane(v_rows, tab_rows, list1)
-        for q in (0, 2, 1, 3):
-            first = P - 2 * ROWS + 8 * q
-            nc.sync.dma_start(
-                out=v_planes[32 * q + V_PLANE : 32 * q + V_PLANE + 4, :], in_=v_rows[:].bitcast(I32)[first : first + 8, :]
-            )
+        for quadrant in (0, 2, 1, 3):
+            first = P - 2 * ROWS + 8 * quadrant
+            row = 32 * quadrant + V_PLANE
+            nc.sync.dma_start(out=v_planes[row : row + 4, :], in_=v_rows[:].bitcast(I32)[first : first + 8, :])
         tab1 = load_table(tab_words[1], "tab1", AT_TAB1)
         b_sb = place([P, 2, 2 * PACK], F32, "b_sb", AT_B)
         nc.sync.dma_start(out=b_sb[:, :, 0:PACK], in_=b.rearrange("(g p t) -> p g t", g=2, t=PACK))
@@ -284,14 +278,14 @@ def tile_list_edge_gated_messages_kernel(
             gather_words(v2_codes, tab2, list2, edges(e))
         wa01 = load_wa(0, 1, AT_WA01)
         wa11 = load_wa(1, 1, AT_WA11)
-        wa00_bf = cast_weight(wa00, nc.scalar, "wa00_bf")
+        wa00_bf = cast_wa(wa00, nc.scalar, "wa00_bf")
         wa00_mx = quantize(wa00_bf, "wa00_mx", parts=WHOLE)
         for e in range(2):
             gather_words(v_codes[0], tab0, list1, edges(e))
         w20 = load_weight(w2[0:WIDTH, :], "w20", AT_W20)
         w21 = load_weight(w2[WIDTH:H, :], "w21", AT_W21)
-        wa10_first = place([P, PACK * WIDTH // 2], BF16, "wa10_first", AT_WA10_BF)
-        wa10_second = place([P, PACK * WIDTH // 2], BF16, "wa10_second", AT_WA10_BF + 2 * KIB)
+        wa10_first = half_tile("wa10_first", AT_WA10_BF)
+        wa10_second = half_tile("wa10_second", AT_WA10_BF + 2 * KIB)
         cast_slots(wa10_first[:], wa10, nc.scalar, 0)
         cast_slots(wa10_second[:], wa10, nc.vector, 1)
         wa10_mx = mx_tiles("wa10_mx")
@@ -303,7 +297,7 @@ def tile_list_edge_gated_messages_kernel(
         for columns in (*HALVES, edges(1)):
             gather_words(v_codes[1], tab1, list1, columns)
         states = [load_state(0, AT_TAB1)]
-        wa01_bf = cast_weight(wa01, nc.vector, "wa01_bf", AT_WA01_BF)
+        wa01_bf = cast_wa(wa01, nc.vector, "wa01_bf", AT_WA01_BF)
         wa01_mx = quantize(wa01_bf, "wa01_mx")
         states.append(load_state(1, AT_WA01_BF))
         quarters = [quarter_sums(q) for q in range(2)]
@@ -321,10 +315,10 @@ def tile_list_edge_gated_messages_kernel(
             relu(quarters[q], 0, hs00[q])
         hs01 = place([P, PACK, WIDTH], BF16, "hs01")
         relu(sums01, 0, hs01)
-        h00_first = place([P, PACK * WIDTH // 2], BF16, "h00_first", AT_WA01)
+        h00_first = half_tile("h00_first", AT_WA01)
         interleave_columns(h00_first[:], hs00[0], nc.vector, HALVES[0])
 
-        wa11_bf = cast_weight(wa11, nc.vector, "wa11_bf", AT_WA11_BF)
+        wa11_bf = cast_wa(wa11, nc.vector, "wa11_bf", AT_WA11_BF)
         wa11_mx = quantize(wa11_bf, "wa11_mx", AT_WA11_MX)
         states.append(load_state(2, AT_STATE2))
         sums10 = whole_sums(1, 0)
@@ -337,48 +331,48 @@ def tile_list_edge_gated_messages_kernel(
         pass_wa(sums11, wa01_mx, 0, stop=True)
         hs10 = place([P, PACK, WIDTH], BF16, "hs10", AT_HS10)
         relu(sums10, 1, hs10)
-        w21_bf = cast_plain(w21, nc.scalar, "w21_bf", AT_WA11_MX)
+        w21_bf = cast_w2(w21, nc.scalar, "w21_bf", AT_WA11_MX)
         hs11 = place([P, PACK, WIDTH], BF16, "hs11", AT_W21)
         relu(sums11[:2], 1, hs11)
 
-        h00_second = place([P, PACK * WIDTH // 2], BF16, "h00_second", AT_WA11)
+        h00_second = half_tile("h00_second", AT_WA11)
         interleave_columns(h00_second[:], hs00[1], nc.vector, HALVES[0])
-        w20_bf = cast_plain(w20, nc.vector, "w20_bf")
+        w20_bf = cast_w2(w20, nc.vector, "w20_bf", parts=WHOLE)
         states.append(load_state(3, AT_W20))
         h00_mx = mx_tiles("h00_mx", AT_WA11 + 2 * KIB)
         quantize_columns(h00_mx, h00_first[:], HALVES[0])
         quantize_columns(h00_mx, h00_second[:], HALVES[1])
         w2_mx = (quantize(w20_bf, "w20_mx", parts=WHOLE), mx_tiles("w21_mx"))
-        h01_first = place([P, PACK * WIDTH // 2], BF16, "h01_first", AT_H01_FIRST)
+        h01_first = half_tile("h01_first", AT_H01_FIRST)
         interleave_columns(h01_first[:], hs01, nc.vector, HALVES[0])
-        z0 = [open_gate(0, u, u, h00_mx) for u in range(PACK)]
-        h10_bf = interleave(hs10, "h10_bf")
+        z0 = [open_gate(0, u, h00_mx) for u in range(PACK)]
+        h10_bf = place([P, PACK * WIDTH], BF16, "h10_bf")
+        for columns in HALVES:
+            interleave_columns(values(h10_bf, columns), hs10, nc.vector, columns)
         h10_mx = quantize(h10_bf, "h10_mx")
-        quantize_columns(w2_mx[1], words(w21_bf, HALVES[0]), HALVES[0])
-        h01_second = place([P, PACK * WIDTH // 2], BF16, "h01_second", AT_HS10)
+        quantize_columns(w2_mx[1], values(w21_bf, HALVES[0]), HALVES[0])
+        h01_second = half_tile("h01_second", AT_HS10)
         interleave_columns(h01_second[:], hs01, nc.vector, HALVES[1])
-        quantize_columns(w2_mx[1], words(w21_bf, HALVES[1]), HALVES[1])
+        quantize_columns(w2_mx[1], values(w21_bf, HALVES[1]), HALVES[1])
         h01_mx = mx_tiles("h01_mx", AT_HS10 + 2 * KIB)
         quantize_columns(h01_mx, h01_first[:], HALVES[0])
         quantize_columns(h01_mx, h01_second[:], HALVES[1])
 
-        sigs = [gate(0, 0, z0[0], h10_mx)]
+        sigs = [close_gate(0, 0, z0[0], h10_mx)]
         relu(sums11[2:], 1, hs11)
-        sigs.append(gate(0, 1, z0[1], h10_mx, AT_SIG01))
-        h11_bf = [place([P, PACK * WIDTH // 2], BF16, f"h11_bf{i}") for i in range(2)]
-        interleave_columns(h11_bf[0][:], hs11, nc.scalar, HALVES[0])
-        sigs.append(gate(0, 2, z0[2], h10_mx))
-        sigs.append(gate(0, 3, z0[3], h10_mx, AT_SIG03))
-        z1 = [open_gate(1, u, PACK + u, h01_mx) for u in range(PACK)]
+        sigs.append(close_gate(0, 1, z0[1], h10_mx))
         message(0, 0, sigs[0])
-        interleave_columns(h11_bf[1][:], hs11, nc.vector, HALVES[1])
+        h11_bf = place([P, PACK * WIDTH], BF16, "h11_bf")
+        interleave_columns(values(h11_bf, HALVES[1]), hs11, nc.vector, HALVES[1])
+        interleave_columns(values(h11_bf, HALVES[0]), hs11, nc.scalar, HALVES[0])
+        sigs.append(close_gate(0, 2, z0[2], h10_mx))
+        sigs.append(close_gate(0, 3, z0[3], h10_mx, AT_SIG03))
+        z1 = [open_gate(1, u, h01_mx) for u in range(PACK)]
         message(0, 1, sigs[1])
-        h11_mx = mx_tiles("h11_mx", AT_SIG01)
-        for i in (1, 0):
-            quantize_columns(h11_mx, h11_bf[i][:], HALVES[i])
+        h11_mx = quantize(h11_bf, "h11_mx", parts=WHOLE)
         for u in range(2, PACK):
             message(0, u, sigs[u])
-        message(1, 0, gate(1, 0, z1[0], h11_mx, AT_SIG10), AT_RES10)
-        message(1, 1, gate(1, 1, z1[1], h11_mx, AT_SIG11), AT_RES11)
-        for u, at in ((2, AT_SIG10), (3, AT_SIG11)):
-            message(1, u, gate(1, u, z1[u], h11_mx), at)
+        message(1, 3, close_gate(1, 3, z1[3], h11_mx, AT_SIG13))
+        message(1, 0, close_gate(1, 0, z1[0], h11_mx), AT_RES10)
+        message(1, 1, close_gate(1, 1, z1[1], h11_mx), AT_RES11)
+        message(1, 2, close_gate(1, 2, z1[2], h11_mx), AT_SIG13, parts=HALVES)

from contextlib import ExitStack

import concourse.mybir as mybir

F32 = mybir.dt.float32
BF16 = mybir.dt.bfloat16
I32 = mybir.dt.int32
U32 = mybir.dt.uint32
U16 = mybir.dt.uint16
U8 = mybir.dt.uint8
FP8X4 = mybir.dt.float8_e4m3fn_x4
FP4X4 = mybir.dt.float4_e2m1fn_x4
ACT = mybir.ActivationFunctionType
MULT = mybir.AluOpType.mult

T, S, K, K2, H, N = 2048, 1024, 1024, 512, 1024, 512
P = 128
PACK = 4
WIDTH = 512
HALVES = (slice(0, WIDTH // 2), slice(WIDTH // 2, WIDTH))
WHOLE = (slice(0, WIDTH),)
V_PLANE = 4
ROWS = 16
KIB = 1024
FLOPS = 2 * S * (K * H + K2 * H + H * N)


def tile_list_edge_gated_messages_kernel(
    tc, tab_words, tab_scales, tab2_words, tab2_scales, offs, offs2, wa, wb_words, wb_scales, b, w2, c, gT, out
):
    nc = tc.nc
    with ExitStack() as ctx:
        keep = ctx.enter_context(tc.tile_pool(name="keep", bufs=1))
        arena = ctx.enter_context(tc.tile_pool(name="arena", bufs=1))
        psum = ctx.enter_context(tc.psum_pool(name="psum", bufs=1))

        def place(shape, dtype, name, at=None):
            if at is None:
                return keep.tile(shape, dtype, name=name, align_bytes=64)
            return arena.tile(shape, dtype, name=name, align_bytes=64, offset=at)

        def bank(index, name):
            return psum.tile([P, WIDTH], F32, tag=f"bank{index}", name=name)

        def edges(e):
            return slice(e * WIDTH, (e + 1) * WIDTH)

        AT_WA01, AT_TAB2, AT_WA11 = 0, 4 * KIB, 8 * KIB
        AT_W20, AT_TAB0, AT_W21 = 16 * KIB, 20 * KIB, 24 * KIB
        AT_B, AT_TAB1 = 32 * KIB, 33 * KIB
        AT_WA10 = 41 * KIB
        AT_WA10_BF = 49 * KIB
        AT_HS10 = 53 * KIB
        AT_WA11_MX = 57 * KIB
        AT_H01_FIRST, AT_WA11_BF, AT_STATE2 = 61 * KIB, 62 * KIB, 63 * KIB
        AT_WA01_BF = 71 * KIB
        AT_RES10, AT_SIG03, AT_RES11 = 79 * KIB, 80 * KIB, 81 * KIB
        AT_SIG13 = 83 * KIB

        list1 = keep.tile([P, S // 16], U16, name="list1")
        list2 = keep.tile([P, S // 16], U16, name="list2")
        tab_rows = place([P, T // 4], I32, "tab_rows", AT_B)
        tab2_rows = place([P, T // 4], I32, "tab2_rows", AT_TAB0)
        wb_rows = place([P, H // 4], I32, "wb_rows")
        wb_words_raw = place([P, H // 2], I32, "wb_words_raw")
        wb_codes = place([P, H], U16, "wb_codes")
        v_rows = place([P, S], U8, "v_rows")
        v2_rows = place([P, S], U8, "v2_rows", AT_WA10)
        pair_rows = place([P, S + H], U8, "pair_rows")
        v_planes = place([P, 2 * S // 4], I32, "v_planes")
        pair_planes = place([P, (S + H) // 4], I32, "pair_planes")
        v2_plane = pair_planes[:].bitcast(U8)[:, 0:S]
        wb_plane = pair_planes[:].bitcast(U8)[:, S : S + H]
        v2_codes = place([P, S], U32, "v2_codes")
        v_codes = [place([P, S], U32, f"v{a}_codes") for a in range(2)]

        def load_table(packed, name, at):
            tile = place([P, T], I32, name, at)
            nc.sync.dma_start(out=tile[:], in_=packed.rearrange("p t i -> p (t i)").bitcast(I32))
            return tile

        def load_weight(rows, name, at=None):
            tile = place([P, PACK, WIDTH], F32, name, at)
            nc.sync.dma_start(out=tile[:], in_=rows.rearrange("(p j) x -> p j x", j=PACK))
            return tile

        def load_wa(a, g, at=None):
            return load_weight(wa[a * WIDTH : (a + 1) * WIDTH, g * WIDTH : (g + 1) * WIDTH], f"wa{a}{g}", at)

        def load_state(u, at):
            state = place([P, T], F32, f"state{u}", at)
            nc.sync.dma_start(out=state[:], in_=gT[u * P : (u + 1) * P, :])
            return state

        def entries(offsets, columns):
            return offsets[:, columns.start // 16 : columns.stop // 16]

        def values(grouped, columns):
            return grouped[:, PACK * columns.start : PACK * columns.stop]

        def gather_words(codes, table, offsets, columns):
            picked = table[:].bitcast(U32).indirect(entries(offsets, columns))
            nc.vector.tensor_copy(out=codes[:, columns], in_=picked)

        def gather_plane(dst, plane, offsets):
            nc.vector.tensor_copy(out=dst[:], in_=plane[:].bitcast(U8).indirect(offsets[:]))

        def copy_on(engine, dst, src):
            if engine is nc.scalar:
                nc.scalar.copy(out=dst, in_=src)
            else:
                nc.vector.tensor_copy(out=dst, in_=src)

        def sort_columns(engine, dst, src):
            copy_on(
                engine,
                dst.rearrange("p (g t m) -> p g t m", g=2, t=PACK),
                src.rearrange("p (g m t) -> p g t m", g=2, t=PACK),
            )

        def cast_slots(dst, raw, engine, s):
            pair = slice(2 * s, 2 * s + 2)
            copy_on(
                engine,
                dst.rearrange("p (t m j) -> p m j t", t=2, j=PACK),
                raw[:].rearrange("p j (m t) -> p m j t", t=PACK)[:, :, :, pair],
            )

        def cast_columns(dst, raw, engine, columns):
            copy_on(
                engine,
                dst.rearrange("p (x i j) -> p x j i", i=2, j=PACK),
                raw[:, :, columns].rearrange("p j (x i) -> p x j i", i=2),
            )

        def cast_w2(raw, engine, name, at=None, parts=HALVES):
            grouped = place([P, PACK * WIDTH], BF16, name, at)
            for columns in parts:
                cast_columns(values(grouped, columns), raw, engine, columns)
            return grouped

        def cast_wa(raw, engine, name, at=None):
            grouped = place([P, PACK * WIDTH], BF16, name, at)
            for s in range(2):
                cast_slots(values(grouped, HALVES[s]), raw, engine, s)
            return grouped

        def interleave_columns(dst, hs, engine, columns):
            copy_on(
                engine,
                dst.rearrange("p (x i t) -> p x t i", i=4, t=PACK),
                hs[:, :, columns].rearrange("p t (x i) -> p x t i", i=4),
            )

        def half_tile(name, at=None):
            return place([P, PACK * WIDTH // 2], BF16, name, at)

        def mx_tiles(name, at=None):
            return place([P, WIDTH], U32, name, at), place([P, WIDTH], U8, name + "_plane")

        def quantize_columns(operand, src, columns):
            codes, plane = operand
            nc.vector.quantize_mx(out=codes[:, columns].bitcast(FP8X4), scales=plane[:, columns], in_=src)

        def quantize(grouped, name, at=None, parts=HALVES):
            operand = mx_tiles(name, at)
            for columns in parts:
                quantize_columns(operand, values(grouped, columns), columns)
            return operand

        def whole_sums(g, e):
            return [(bank(PACK * e + t, f"a{g}{e}{t}")[:], t, edges(e)) for t in range(PACK)]

        def quarter_sums(q):
            sums = []
            for s in range(2):
                both = bank(2 * q + s, f"a0q{q}{s}")
                sums += [(both[:, HALVES[i]], 2 * s + i, HALVES[q]) for i in range(2)]
            return sums

        def pass_wa(sums, operand, a, start=False, stop=False, shared=False):
            codes, plane = operand
            for acc, t, columns in sums:
                m = slice(t * P, (t + 1) * P)
                nc.tensor.matmul_mx(
                    out=acc,
                    lhsT=codes[:, m].bitcast(FP8X4),
                    lhsT_scale=plane[:, m],
                    rhs=v_codes[a][:, columns].bitcast(FP8X4),
                    rhs_scale=v_planes[:].bitcast(U8)[V_PLANE:P, a * S + columns.start : a * S + columns.stop],
                    start=start,
                    stop=stop and (not shared or t % 2 == 1),
                )

        def pass_wb(sums, g, start=False, shared=False):
            for acc, t, columns in sums:
                first = g * WIDTH + t * P
                nc.tensor.matmul_mx(
                    out=acc,
                    lhsT=wb_codes[:].bitcast(U8)[:, 2 * first : 2 * (first + P)].bitcast(FP4X4),
                    lhsT_scale=wb_plane[:, first : first + P],
                    rhs=v2_codes[:, columns].bitcast(FP8X4),
                    rhs_scale=v2_plane[:, columns],
                    start=start and (not shared or t % 2 == 0),
                    stop=False,
                )

        def relu(sums, g, hs):
            for acc, t, columns in sums:
                nc.scalar.activation(out=hs[:, t, :], in_=acc, func=ACT.Relu, bias=b_sb[:, g, t : t + 1])

        def pass_w2(z, g, u, h_mx):
            m = slice(u * P, (u + 1) * P)
            nc.tensor.matmul_mx(
                out=z[:],
                lhsT=w2_mx[g][0][:, m].bitcast(FP8X4),
                lhsT_scale=w2_mx[g][1][:, m],
                rhs=h_mx[0][:].bitcast(FP8X4),
                rhs_scale=h_mx[1][:],
                start=(g == 0),
                stop=(g == 1),
            )

        def open_gate(e, u, h_mx):
            z = bank(PACK * e + u, f"z{e}{u}")
            pass_w2(z, 0, u, h_mx)
            return z

        def close_gate(e, u, z, h_mx, at=None):
            pass_w2(z, 1, u, h_mx)
            sig = place([P, WIDTH], F32, f"sig{e}{u}", at)
            nc.scalar.activation(out=sig[:], in_=z[:], func=ACT.Sigmoid, bias=c_sb[:, u : u + 1])
            return sig

        def message(e, u, sig, at=None, parts=WHOLE):
            res = place([P, WIDTH], F32, f"res{e}{u}", at)
            for part in parts:
                columns = slice(e * WIDTH + part.start, e * WIDTH + part.stop)
                picked = states[u][:].indirect(entries(list1, columns))
                nc.vector.tensor_tensor(res[:, part], picked, sig[:, part], MULT)
                nc.sync.dma_start(out=out[u * P : (u + 1) * P, columns], in_=res[:, part])

        nc.gpsimd.memset(tab2_rows[0 : P - ROWS, :], 0)
        nc.gpsimd.memset(wb_rows[0 : P - ROWS, :], 0)
        nc.gpsimd.memset(tab_rows[0 : P - 2 * ROWS, :], 0)
        nc.gpsimd.memset(pair_planes[:], 0)
        nc.gpsimd.memset(v_planes[:], 0)
        warm = keep.tile([P, 2], F32, name="warm")
        nc.vector.memset(warm[:, 0:1], 0.0)
        nc.scalar.activation(out=warm[:, 1:2], in_=warm[:, 0:1], func=ACT.Sigmoid)
        nc.sync.dma_start(list2[:], offs2)
        nc.sync.dma_start(out=tab2_rows[P - ROWS : P, :], in_=tab2_scales[0].bitcast(I32))
        nc.sync.dma_start(out=wb_rows[P - ROWS : P, :], in_=wb_scales[0].bitcast(I32))
        nc.sync.dma_start(out=wb_words_raw[:], in_=wb_words[0].bitcast(I32))
        nc.sync.dma_start(list1[:], offs)
        nc.sync.dma_start(out=tab_rows[P - 2 * ROWS : P, :], in_=tab_scales.bitcast(I32).rearrange("a q x -> q a x"))
        tab2 = load_table(tab2_words[0], "tab2", AT_TAB2)
        wa00 = load_wa(0, 0)

        gather_plane(v2_rows, tab2_rows, list2)
        tab0 = load_table(tab_words[0], "tab0", AT_TAB0)
        sort_columns(nc.vector, pair_rows[:, S : S + H], wb_rows[:].bitcast(U8))
        nc.vector.tensor_copy(out=pair_rows[:, 0:S].bitcast(I32), in_=v2_rows[:].bitcast(I32))
        for r in range(4):
            nc.sync.dma_start(out=pair_planes[r:P:32, :], in_=pair_rows[:].bitcast(I32)[P - ROWS + r : P : 4, :])
        wa10 = load_wa(1, 0, AT_WA10)
        sort_columns(nc.scalar, wb_codes[:], wb_words_raw[:].bitcast(U16))
        gather_plane(v_rows, tab_rows, list1)
        for quadrant in (0, 2, 1, 3):
            first = P - 2 * ROWS + 8 * quadrant
            row = 32 * quadrant + V_PLANE
            nc.sync.dma_start(out=v_planes[row : row + 4, :], in_=v_rows[:].bitcast(I32)[first : first + 8, :])
        tab1 = load_table(tab_words[1], "tab1", AT_TAB1)
        b_sb = place([P, 2, 2 * PACK], F32, "b_sb", AT_B)
        nc.sync.dma_start(out=b_sb[:, :, 0:PACK], in_=b.rearrange("(g p t) -> p g t", g=2, t=PACK))

        for e in range(2):
            gather_words(v2_codes, tab2, list2, edges(e))
        wa01 = load_wa(0, 1, AT_WA01)
        wa11 = load_wa(1, 1, AT_WA11)
        wa00_bf = cast_wa(wa00, nc.scalar, "wa00_bf")
        wa00_mx = quantize(wa00_bf, "wa00_mx", parts=WHOLE)
        for e in range(2):
            gather_words(v_codes[0], tab0, list1, edges(e))
        w20 = load_weight(w2[0:WIDTH, :], "w20", AT_W20)
        w21 = load_weight(w2[WIDTH:H, :], "w21", AT_W21)
        wa10_first = half_tile("wa10_first", AT_WA10_BF)
        wa10_second = half_tile("wa10_second", AT_WA10_BF + 2 * KIB)
        cast_slots(wa10_first[:], wa10, nc.scalar, 0)
        cast_slots(wa10_second[:], wa10, nc.vector, 1)
        wa10_mx = mx_tiles("wa10_mx")
        quantize_columns(wa10_mx, wa10_first[:], HALVES[0])
        quantize_columns(wa10_mx, wa10_second[:], HALVES[1])
        c_sb = place([P, PACK], F32, "c_sb", AT_WA10_BF)
        with nc.allow_non_contiguous_dma(reason="one bias a partition and gate"):
            nc.sync.dma_start(out=c_sb[:], in_=c.rearrange("(u p) -> p u", u=PACK))
        for columns in (*HALVES, edges(1)):
            gather_words(v_codes[1], tab1, list1, columns)
        states = [load_state(0, AT_TAB1)]
        wa01_bf = cast_wa(wa01, nc.vector, "wa01_bf", AT_WA01_BF)
        wa01_mx = quantize(wa01_bf, "wa01_mx")
        states.append(load_state(1, AT_WA01_BF))
        quarters = [quarter_sums(q) for q in range(2)]
        sums01 = whole_sums(0, 1)
        for sums in quarters:
            pass_wb(sums, 0, start=True, shared=True)
        pass_wb(sums01, 0, start=True)
        for sums in (*quarters, sums01):
            pass_wa(sums, wa00_mx, 0)
        for sums in quarters:
            pass_wa(sums, wa10_mx, 1, stop=True, shared=True)
        pass_wa(sums01, wa10_mx, 1, stop=True)
        hs00 = [place([P, PACK, WIDTH // 2], BF16, f"hs00{q}") for q in range(2)]
        for q in range(2):
            relu(quarters[q], 0, hs00[q])
        hs01 = place([P, PACK, WIDTH], BF16, "hs01")
        relu(sums01, 0, hs01)
        h00_first = half_tile("h00_first", AT_WA01)
        interleave_columns(h00_first[:], hs00[0], nc.vector, HALVES[0])

        wa11_bf = cast_wa(wa11, nc.vector, "wa11_bf", AT_WA11_BF)
        wa11_mx = quantize(wa11_bf, "wa11_mx", AT_WA11_MX)
        states.append(load_state(2, AT_STATE2))
        sums10 = whole_sums(1, 0)
        pass_wb(sums10, 1, start=True)
        pass_wa(sums10, wa01_mx, 0)
        pass_wa(sums10, wa11_mx, 1, stop=True)
        sums11 = whole_sums(1, 1)
        pass_wa(sums11, wa11_mx, 1, start=True)
        pass_wb(sums11, 1)
        pass_wa(sums11, wa01_mx, 0, stop=True)
        hs10 = place([P, PACK, WIDTH], BF16, "hs10", AT_HS10)
        relu(sums10, 1, hs10)
        w21_bf = cast_w2(w21, nc.scalar, "w21_bf", AT_WA11_MX)
        hs11 = place([P, PACK, WIDTH], BF16, "hs11", AT_W21)
        relu(sums11[:2], 1, hs11)

        h00_second = half_tile("h00_second", AT_WA11)
        interleave_columns(h00_second[:], hs00[1], nc.vector, HALVES[0])
        w20_bf = cast_w2(w20, nc.vector, "w20_bf", parts=WHOLE)
        states.append(load_state(3, AT_W20))
        h00_mx = mx_tiles("h00_mx", AT_WA11 + 2 * KIB)
        quantize_columns(h00_mx, h00_first[:], HALVES[0])
        quantize_columns(h00_mx, h00_second[:], HALVES[1])
        w2_mx = (quantize(w20_bf, "w20_mx", parts=WHOLE), mx_tiles("w21_mx"))
        h01_first = half_tile("h01_first", AT_H01_FIRST)
        interleave_columns(h01_first[:], hs01, nc.vector, HALVES[0])
        z0 = [open_gate(0, u, h00_mx) for u in range(PACK)]
        h10_bf = place([P, PACK * WIDTH], BF16, "h10_bf")
        for columns in HALVES:
            interleave_columns(values(h10_bf, columns), hs10, nc.vector, columns)
        h10_mx = quantize(h10_bf, "h10_mx")
        quantize_columns(w2_mx[1], values(w21_bf, HALVES[0]), HALVES[0])
        h01_second = half_tile("h01_second", AT_HS10)
        interleave_columns(h01_second[:], hs01, nc.vector, HALVES[1])
        quantize_columns(w2_mx[1], values(w21_bf, HALVES[1]), HALVES[1])
        h01_mx = mx_tiles("h01_mx", AT_HS10 + 2 * KIB)
        quantize_columns(h01_mx, h01_first[:], HALVES[0])
        quantize_columns(h01_mx, h01_second[:], HALVES[1])

        sigs = [close_gate(0, 0, z0[0], h10_mx)]
        relu(sums11[2:], 1, hs11)
        sigs.append(close_gate(0, 1, z0[1], h10_mx))
        message(0, 0, sigs[0])
        h11_bf = place([P, PACK * WIDTH], BF16, "h11_bf")
        interleave_columns(values(h11_bf, HALVES[1]), hs11, nc.vector, HALVES[1])
        interleave_columns(values(h11_bf, HALVES[0]), hs11, nc.scalar, HALVES[0])
        sigs.append(close_gate(0, 2, z0[2], h10_mx))
        sigs.append(close_gate(0, 3, z0[3], h10_mx, AT_SIG03))
        z1 = [open_gate(1, u, h01_mx) for u in range(PACK)]
        message(0, 1, sigs[1])
        h11_mx = quantize(h11_bf, "h11_mx", parts=WHOLE)
        for u in range(2, PACK):
            message(0, u, sigs[u])
        message(1, 3, close_gate(1, 3, z1[3], h11_mx, AT_SIG13))
        message(1, 0, close_gate(1, 0, z1[0], h11_mx), AT_RES10)
        message(1, 1, close_gate(1, 1, z1[1], h11_mx), AT_RES11)
        message(1, 2, close_gate(1, 2, z1[2], h11_mx), AT_SIG13, parts=HALVES)
